import numpy as np
import ml_dtypes


def mxq(x, axis, fmt="e4m3"):
    dtype, down = {"e4m3": (ml_dtypes.float8_e4m3fn, 7), "e5m2": (ml_dtypes.float8_e5m2, 14)}[fmt]
    v = np.moveaxis(np.asarray(x, np.float32).astype(ml_dtypes.bfloat16).astype(np.float64), axis, -1)
    blocks = v.reshape(v.shape[:-1] + (-1, 32))
    amax = np.abs(blocks).max(-1, keepdims=True)
    byte = np.maximum(np.where(amax > 0, np.frexp(amax)[1] - 1 + 127, 0) - down, 1)
    scale = np.exp2(byte - 127.0)
    codes = (blocks / scale).astype(np.float32).astype(dtype).astype(np.float64)
    return np.moveaxis((codes * scale).reshape(v.shape), -1, axis)


WIDE = False


def mx_kscale(k):
    if not WIDE:
        return np.ones(k)
    levels = np.array([18, -18])
    if k % 512:
        return np.exp2(np.random.permutation(np.resize(levels, k // 32))).repeat(32)
    a = np.empty((k // 512, 16))
    for p in range(k // 512):
        a[p, :8] = np.random.permutation(np.resize(levels, 8))
        for g in range(8):
            far = levels[np.abs(levels - a[p, g]) >= 10]
            a[p, g + 8] = far[np.random.randint(len(far))]
    return np.exp2(a.ravel()).repeat(32)


def f64(x):
    return np.asarray(x).astype(np.float64)


def striped(idx):
    return np.tile(np.asarray(idx).reshape(-1, 16).T, (8, 1)).astype(np.uint16)


def unstriped(offs):
    return offs[:16].T.reshape(-1).astype(np.int64)


E2M1 = np.array([0.0, 0.5, 1.0, 1.5, 2.0, 3.0, 4.0, 6.0, -0.0, -0.5, -1.0, -1.5, -2.0, -3.0, -4.0, -6.0])


def pack_weight(w, fmt):
    k, n = w.shape
    w = f64(np.asarray(w, np.float32).astype(ml_dtypes.bfloat16)).reshape(k // 32, 32, n)
    amax = np.abs(w).max(1)
    if fmt == "e4m3":
        byte = np.frexp(amax)[1] - 1 + 127 - 7
    else:
        mant, ex = np.frexp(amax / 6.0)
        byte = np.where(mant > 0.5, ex, ex - 1) + 127
    byte = np.clip(np.where(amax > 0, byte, 1), 1, 254)
    scaled = (w * np.exp2(127.0 - byte)[:, None, :]).reshape(k, n).astype(np.float32)
    by_word = np.ascontiguousarray(scaled.reshape(k // 512, 128, 4, n).transpose(0, 1, 3, 2))
    if fmt == "e4m3":
        words = by_word.astype(ml_dtypes.float8_e4m3fn).view(np.uint8)
    else:
        c = by_word.astype(ml_dtypes.float4_e2m1fn).view(np.uint8) & 0xF
        words = (c[..., 0::2] | (c[..., 1::2] << 4)).reshape(k // 512, 128, 2 * n)
    return np.ascontiguousarray(words), np.ascontiguousarray(byte.astype(np.uint8).reshape(k // 512, 16, n))


def unpack_weight(words, scales, fmt):
    g, _, n = scales.shape
    words = np.ascontiguousarray(words).reshape(g, 128, n, -1)
    if fmt == "e4m3":
        vals = words.view(ml_dtypes.float8_e4m3fn).astype(np.float64)
    else:
        nib = np.empty((g, 128, n, 4), np.uint8)
        nib[..., 0::2] = words & 0xF
        nib[..., 1::2] = words >> 4
        vals = E2M1[nib]
    vals = vals * np.repeat(np.exp2(scales.astype(np.float64) - 127.0), 8, axis=1)[..., None]
    return vals.transpose(0, 1, 3, 2).reshape(g * 512, n)


def planes(y):
    n, m = y.shape
    v = y.astype(np.float32).astype(ml_dtypes.bfloat16).astype(np.float64).reshape(n // 32, 32, m)
    top = np.abs(v).max(1)
    byte = np.clip(np.where(top > 0, np.frexp(top)[1] - 1 + 127 - 7, 1), 1, 254)
    codes = (v * np.exp2(127.0 - byte)[:, None, :]).reshape(n, m).astype(np.float32).astype(ml_dtypes.float8_e4m3fn).view(np.uint8)
    words = codes.reshape(n // 512, 128, 4, m).transpose(0, 1, 3, 2)
    return np.ascontiguousarray(words), np.ascontiguousarray(byte.astype(np.uint8).reshape(n // 512, 16, m))


T, C, D, DV = 512, 512, 512, 512
BETA = 0.25


def setup_inputs():
    n = np.random.standard_normal
    grid = lambda v: np.clip(np.round(v * 16) / 16, -4, 4)
    v = mx_kscale(DV)[:, None]
    wp = pack_weight(n((DV, D)) / np.sqrt(DV) / v, "e2m1")
    return {
        "zT": (grid(n((DV, T))) * v).astype(np.float32),
        "cb": (grid(n((DV, C))) * v).astype(np.float32),
        "cb2": (grid(0.5 * n((DV, C))) * v).astype(np.float32),
        "w_words": wp[0],
        "w_scales": wp[1],
        "offs": striped(np.random.randint(0, C, T)),
        "offs2": striped(np.random.randint(0, C, T)),
    }


def reference(zT, cb, cb2, w_words, w_scales, offs, offs2):
    e = f64(zT) - f64(cb)[:, unstriped(offs)] - f64(cb2)[:, unstriped(offs2)]
    g = BETA * e
    out_0 = unpack_weight(w_words, w_scales, "e2m1").T @ mxq(g, 0, "e5m2")
    return (out_0,) + planes(out_0)

@@ -1,0 +1,204 @@
+from contextlib import ExitStack
+
+import concourse.mybir as mybir
+from concourse.masks import make_identity
+
+T, C, D, N = 512, 512, 512, 512
+FLOPS = 2 * N * D * T
+BETA = 0.25
+
+F32 = mybir.dt.float32
+BF16 = mybir.dt.bfloat16
+I32 = mybir.dt.int32
+U32 = mybir.dt.uint32
+U16 = mybir.dt.uint16
+U8 = mybir.dt.uint8
+E4M3X4 = mybir.dt.float8_e4m3fn_x4
+E5M2X4 = mybir.dt.float8_e5m2_x4
+E2M1X4 = mybir.dt.float4_e2m1fn_x4
+ALU = mybir.AluOpType
+COPY = mybir.ActivationFunctionType.Copy
+
+P = 128
+LANES = 4
+TILE = 128
+HALF = 256
+
+
+def tile_attend_gvq_pl_r_x_kernel(tc, zT, cb, cb2, w_words, w_scales, offs, offs2, out_0, out_1, out_2):
+    nc = tc.nc
+    with ExitStack() as ctx:
+        keep = ctx.enter_context(tc.tile_pool(name="keep", bufs=1))
+        psum = ctx.enter_context(tc.psum_pool(name="psum", bufs=1))
+
+        code = keep.tile([P, T // 16], U16, name="code")
+        code2 = keep.tile([P, T // 16], U16, name="code2")
+        book = [keep.tile([P, C], F32, name=f"book{j}") for j in range(LANES)]
+        book2 = [keep.tile([P, C], F32, name=f"book2_{j}") for j in range(LANES)]
+        z = {(h, j): keep.tile([P, HALF], F32, name=f"z{h}_{j}") for h in range(2) for j in range(LANES)}
+        w_codes = keep.tile([P, 2 * D], U8, name="w_codes", align_bytes=64)
+        w_plane = keep.tile([P, D], U8, name="w_plane", align_bytes=64)
+        ident_raw = keep.tile([P, P], F32, name="ident_raw")
+        ident = keep.tile([P, P], F32, name="ident")
+
+        z_rows = zT.rearrange("(p j) t -> p j t", j=LANES)
+        cb_rows = cb.rearrange("(p j) c -> p j c", j=LANES)
+        cb2_rows = cb2.rearrange("(p j) c -> p j c", j=LANES)
+        out_rows = out_0.rearrange("(p j) t -> p j t", j=LANES)
+        out_words = out_1[0].rearrange("p t l -> p (t l)").bitcast(I32)
+        out_scales = out_2[0].bitcast(I32)
+
+        make_identity(nc, ident_raw[:])
+        nc.scalar.copy(ident[:], ident_raw[:])
+        nc.vector.memset(w_plane[:].bitcast(I32), 0)
+
+        def load_z(h, j):
+            nc.sync.dma_start(z[h, j][:], z_rows[:, j, h * HALF : (h + 1) * HALF])
+
+        nc.sync.dma_start(book[0][:], cb_rows[:, 0, :])
+        nc.sync.dma_start(code[:], offs)
+        load_z(0, 0)
+        nc.sync.dma_start(book2[0][:], cb2_rows[:, 0, :])
+        nc.sync.dma_start(code2[:], offs2)
+        load_z(1, 0)
+        for j in range(1, LANES):
+            nc.sync.dma_start(book[j][:], cb_rows[:, j, :])
+            load_z(0, j)
+            nc.sync.dma_start(book2[j][:], cb2_rows[:, j, :])
+            if j == 1:
+                for q in range(4):
+                    nc.sync.dma_start(
+                        w_plane[32 * q : 32 * q + 4, :].bitcast(I32), w_scales[0, 4 * q : 4 * q + 4, :].bitcast(I32)
+                    )
+        for j in range(1, LANES):
+            load_z(1, j)
+            if j == 1:
+                nc.sync.dma_start(w_codes[:].bitcast(I32), w_words[0].bitcast(I32))
+
+        part = [keep.tile([P, LANES, HALF], F32, name=f"part{h}") for h in range(2)]
+        neg_e = [keep.tile([P, LANES, HALF], F32, name=f"neg_e{h}") for h in range(2)]
+
+        def gather1(j, t0, n):
+            h, c0 = divmod(t0, HALF)
+            nc.vector.tensor_tensor(
+                part[h][:, j, c0 : c0 + n],
+                book[j][:].indirect(code[:, t0 // 16 : (t0 + n) // 16]),
+                z[h, j][:, c0 : c0 + n],
+                ALU.subtract,
+            )
+
+        def gather2(j, t0, n):
+            h, c0 = divmod(t0, HALF)
+            nc.vector.tensor_tensor(
+                neg_e[h][:, j, c0 : c0 + n],
+                book2[j][:].indirect(code2[:, t0 // 16 : (t0 + n) // 16]),
+                part[h][:, j, c0 : c0 + n],
+                ALU.add,
+            )
+
+        g_bf = [keep.tile([P, TILE, LANES], BF16, name=f"g_bf{i}", align_bytes=64) for i in range(4)]
+        g_codes = [keep.tile([P, TILE], U32, name=f"g_codes{i}", align_bytes=64) for i in range(4)]
+        g_plane = [keep.tile([P, TILE], U8, name=f"g_plane{i}", align_bytes=64) for i in range(4)]
+        y_tok = [keep.tile([P, LANES, P], F32, name=f"y_tok{i}") for i in range(4)]
+        y = [keep.tile([P, LANES, TILE], F32, name=f"y{i}") for i in range(4)]
+        y_bf = [keep.tile([P, TILE, LANES], BF16, name=f"y_bf{i}", align_bytes=64) for i in range(4)]
+        y_codes = [keep.tile([P, TILE], U32, name=f"y_codes{i}", align_bytes=64) for i in range(4)]
+        y_plane = keep.tile([P, T], U8, name="y_plane", align_bytes=64)
+
+        def weave_views(dst, src):
+            return (
+                dst.rearrange("p (c i) j -> p c j i", i=4),
+                src.rearrange("p j (c i) -> p c j i", i=4),
+            )
+
+        def round_g(i, on_vector):
+            h, c0 = divmod(i * TILE, HALF)
+            dst, src = weave_views(g_bf[i][:], neg_e[h][:, :, c0 : c0 + TILE])
+            if on_vector:
+                nc.vector.tensor_scalar(dst, src, -BETA, None, ALU.mult)
+            else:
+                nc.scalar.activation(dst, src, COPY, scale=-BETA)
+
+        def quantise_g(i):
+            nc.vector.quantize_mx(
+                out=g_codes[i][:].bitcast(E5M2X4), scales=g_plane[i][:], in_=g_bf[i][:].rearrange("p t j -> p (t j)")
+            )
+
+        def product(i):
+            acc = psum.tile([P, D], F32, name=f"acc{i % 2}")
+            nc.tensor.matmul_mx(
+                out=acc[:],
+                lhsT=g_codes[i][:].bitcast(E5M2X4),
+                lhsT_scale=g_plane[i][:],
+                rhs=w_codes[:].bitcast(E2M1X4),
+                rhs_scale=w_plane[:],
+                start=True,
+                stop=True,
+            )
+            nc.scalar.copy(y_tok[i][:], acc[:].rearrange("t (p j) -> t j p", j=LANES))
+
+        def turn(i, name):
+            bank = psum.tile([P, LANES, TILE], F32, name=name)
+            for j in range(LANES):
+                nc.tensor.transpose(bank[:, j, :], y_tok[i][:, j, :], ident[:])
+            return bank
+
+        def store_y(i, bank):
+            nc.scalar.copy(y[i][:], bank[:])
+            nc.sync.dma_start(out_rows[:, :, i * TILE : (i + 1) * TILE], y[i][:])
+
+        def quantise_y(i):
+            nc.vector.quantize_mx(
+                out=y_codes[i][:].bitcast(E4M3X4),
+                scales=y_plane[:, i * TILE : (i + 1) * TILE],
+                in_=y_bf[i][:].rearrange("p t j -> p (t j)"),
+            )
+            nc.sync.dma_start(out_words[:, i * TILE : (i + 1) * TILE], y_codes[i][:].bitcast(I32))
+
+        gather1(0, 0, HALF)
+        gather1(0, HALF, HALF)
+        gather2(0, 0, HALF)
+        gather2(0, HALF, HALF)
+        gather1(1, 0, HALF)
+        gather1(2, 0, HALF)
+        gather2(1, 0, HALF)
+        gather1(3, 0, HALF)
+        gather2(2, 0, HALF)
+        gather2(3, 0, TILE)
+        gather2(3, TILE, TILE)
+        round_g(0, False)
+        round_g(1, False)
+        for j in range(1, LANES):
+            gather1(j, 2 * TILE, TILE)
+        quantise_g(0)
+        product(0)
+        for j in range(1, LANES):
+            gather2(j, 2 * TILE, TILE)
+        quantise_g(1)
+        product(1)
+        round_g(2, False)
+        for j in range(1, LANES):
+            gather1(j, 3 * TILE, TILE)
+        quantise_g(2)
+        for i in range(2):
+            store_y(i, turn(i, f"turn{i}"))
+        product(2)
+        for j in range(1, LANES):
+            gather2(j, 3 * TILE, TILE)
+        round_g(3, True)
+        quantise_g(3)
+        store_y(2, turn(2, "turn2"))
+        product(3)
+        for i in range(3):
+            dst, src = weave_views(y_bf[i][:], y[i][:])
+            nc.vector.tensor_copy(dst, src)
+        for i in range(3):
+            quantise_y(i)
+        bank_b = turn(3, "turn3b")
+        bank_f = turn(3, "turn3f")
+        nc.vector.tensor_copy(y_bf[3][:], bank_b[:].rearrange("p j t -> p t j"))
+        store_y(3, bank_f)
+        quantise_y(3)
+        for q in range(4):
+            queue = nc.scalar if q % 2 else nc.sync
+            queue.dma_start(out_scales[4 * q : 4 * q + 4, :], y_plane[32 * q : 32 * q + 4, :].bitcast(I32))

@@ -1,7 +1,6 @@
 from contextlib import ExitStack
 
 import concourse.mybir as mybir
-from concourse.masks import make_identity
 
 T, C, D, N = 512, 512, 512, 512
 FLOPS = 2 * N * D * T
@@ -31,15 +30,19 @@ def tile_attend_gvq_pl_r_x_kernel(tc, zT, cb, cb2, w_words, w_scales, offs, offs
         keep = ctx.enter_context(tc.tile_pool(name="keep", bufs=1))
         psum = ctx.enter_context(tc.psum_pool(name="psum", bufs=1))
 
+        def sbuf(name, shape, dtype, tag=None):
+            return keep.tile(shape, dtype, name=name, tag=tag or name, align_bytes=64)
+
         code = keep.tile([P, T // 16], U16, name="code")
         code2 = keep.tile([P, T // 16], U16, name="code2")
-        book = [keep.tile([P, C], F32, name=f"book{j}") for j in range(LANES)]
-        book2 = [keep.tile([P, C], F32, name=f"book2_{j}") for j in range(LANES)]
-        z = {(h, j): keep.tile([P, HALF], F32, name=f"z{h}_{j}") for h in range(2) for j in range(LANES)}
-        w_codes = keep.tile([P, 2 * D], U8, name="w_codes", align_bytes=64)
-        w_plane = keep.tile([P, D], U8, name="w_plane", align_bytes=64)
-        ident_raw = keep.tile([P, P], F32, name="ident_raw")
-        ident = keep.tile([P, P], F32, name="ident")
+        book = [sbuf(f"book{j}", [P, C], F32) for j in range(LANES)]
+        book2 = [sbuf(f"book2_{j}", [P, C], F32) for j in range(LANES)]
+        z0 = [sbuf(f"z0_{h}", [P, HALF], F32) for h in range(2)]
+        z1 = sbuf("z1", [P, T], F32)
+        z_half = [sbuf(f"z_half{j}", [P, HALF], F32) for j in (2, 3)]
+        z_late = [sbuf(f"z_late{i}", [P, 2, TILE], F32) for i in (2, 3)]
+        w_raw = sbuf("w_raw", [P, 2 * D], U8)
+        w_plane_raw = sbuf("w_plane_raw", [P, D], U8)
 
         z_rows = zT.rearrange("(p j) t -> p j t", j=LANES)
         cb_rows = cb.rearrange("(p j) c -> p j c", j=LANES)
@@ -48,62 +51,49 @@ def tile_attend_gvq_pl_r_x_kernel(tc, zT, cb, cb2, w_words, w_scales, offs, offs
         out_words = out_1[0].rearrange("p t l -> p (t l)").bitcast(I32)
         out_scales = out_2[0].bitcast(I32)
 
-        make_identity(nc, ident_raw[:])
-        nc.scalar.copy(ident[:], ident_raw[:])
-        nc.vector.memset(w_plane[:].bitcast(I32), 0)
-
-        def load_z(h, j):
-            nc.sync.dma_start(z[h, j][:], z_rows[:, j, h * HALF : (h + 1) * HALF])
+        nc.vector.memset(w_plane_raw[:].bitcast(I32), 0)
+        for q in range(4):
+            nc.gpsimd.dma_start(
+                w_plane_raw[32 * q : 32 * q + 4, :].bitcast(I32), w_scales[0, 4 * q : 4 * q + 4, :].bitcast(I32)
+            )
 
         nc.sync.dma_start(book[0][:], cb_rows[:, 0, :])
         nc.sync.dma_start(code[:], offs)
-        load_z(0, 0)
+        for h in range(2):
+            nc.sync.dma_start(z0[h][:], z_rows[:, 0, h * HALF : (h + 1) * HALF])
         nc.sync.dma_start(book2[0][:], cb2_rows[:, 0, :])
         nc.sync.dma_start(code2[:], offs2)
-        load_z(1, 0)
-        for j in range(1, LANES):
+        nc.sync.dma_start(book[1][:], cb_rows[:, 1, :])
+        nc.sync.dma_start(z1[:], z_rows[:, 1, :])
+        nc.sync.dma_start(book2[1][:], cb2_rows[:, 1, :])
+        for j in (2, 3):
             nc.sync.dma_start(book[j][:], cb_rows[:, j, :])
-            load_z(0, j)
+            nc.sync.dma_start(z_half[j - 2][:], z_rows[:, j, 0:HALF])
+        for j in (2, 3):
             nc.sync.dma_start(book2[j][:], cb2_rows[:, j, :])
-            if j == 1:
-                for q in range(4):
-                    nc.sync.dma_start(
-                        w_plane[32 * q : 32 * q + 4, :].bitcast(I32), w_scales[0, 4 * q : 4 * q + 4, :].bitcast(I32)
-                    )
-        for j in range(1, LANES):
-            load_z(1, j)
-            if j == 1:
-                nc.sync.dma_start(w_codes[:].bitcast(I32), w_words[0].bitcast(I32))
+        for i in (2, 3):
+            nc.sync.dma_start(z_late[i - 2][:], z_rows[:, 2:LANES, i * TILE : (i + 1) * TILE])
+        nc.sync.dma_start(w_raw[:].bitcast(I32), w_words[0].bitcast(I32))
 
-        part = [keep.tile([P, LANES, HALF], F32, name=f"part{h}") for h in range(2)]
-        neg_e = [keep.tile([P, LANES, HALF], F32, name=f"neg_e{h}") for h in range(2)]
+        part = sbuf("part", [P, LANES, T], F32)
+        neg_e = sbuf("neg_e", [P, LANES, T], F32)
 
-        def gather1(j, t0, n):
-            h, c0 = divmod(t0, HALF)
+        def gather1(j, t0, z_cols):
+            n = z_cols.shape[1]
             nc.vector.tensor_tensor(
-                part[h][:, j, c0 : c0 + n],
+                part[:, j, t0 : t0 + n],
                 book[j][:].indirect(code[:, t0 // 16 : (t0 + n) // 16]),
-                z[h, j][:, c0 : c0 + n],
+                z_cols,
                 ALU.subtract,
             )
 
         def gather2(j, t0, n):
-            h, c0 = divmod(t0, HALF)
             nc.vector.tensor_tensor(
-                neg_e[h][:, j, c0 : c0 + n],
+                neg_e[:, j, t0 : t0 + n],
                 book2[j][:].indirect(code2[:, t0 // 16 : (t0 + n) // 16]),
-                part[h][:, j, c0 : c0 + n],
+                part[:, j, t0 : t0 + n],
                 ALU.add,
             )
-
-        g_bf = [keep.tile([P, TILE, LANES], BF16, name=f"g_bf{i}", align_bytes=64) for i in range(4)]
-        g_codes = [keep.tile([P, TILE], U32, name=f"g_codes{i}", align_bytes=64) for i in range(4)]
-        g_plane = [keep.tile([P, TILE], U8, name=f"g_plane{i}", align_bytes=64) for i in range(4)]
-        y_tok = [keep.tile([P, LANES, P], F32, name=f"y_tok{i}") for i in range(4)]
-        y = [keep.tile([P, LANES, TILE], F32, name=f"y{i}") for i in range(4)]
-        y_bf = [keep.tile([P, TILE, LANES], BF16, name=f"y_bf{i}", align_bytes=64) for i in range(4)]
-        y_codes = [keep.tile([P, TILE], U32, name=f"y_codes{i}", align_bytes=64) for i in range(4)]
-        y_plane = keep.tile([P, T], U8, name="y_plane", align_bytes=64)
 
         def weave_views(dst, src):
             return (
@@ -111,94 +101,96 @@ def tile_attend_gvq_pl_r_x_kernel(tc, zT, cb, cb2, w_words, w_scales, offs, offs
                 src.rearrange("p j (c i) -> p c j i", i=4),
             )
 
-        def round_g(i, on_vector):
-            h, c0 = divmod(i * TILE, HALF)
-            dst, src = weave_views(g_bf[i][:], neg_e[h][:, :, c0 : c0 + TILE])
+        g_codes = sbuf("g_codes", [P, T], U32)
+        g_plane = sbuf("g_plane", [P, T], U8)
+
+        def round_g(t0, g_bf, on_vector=False):
+            dst, src = weave_views(g_bf, neg_e[:, :, t0 : t0 + TILE])
             if on_vector:
                 nc.vector.tensor_scalar(dst, src, -BETA, None, ALU.mult)
             else:
                 nc.scalar.activation(dst, src, COPY, scale=-BETA)
 
-        def quantise_g(i):
+        def quantise_g(t0, g_bf):
+            n = g_bf.shape[1]
             nc.vector.quantize_mx(
-                out=g_codes[i][:].bitcast(E5M2X4), scales=g_plane[i][:], in_=g_bf[i][:].rearrange("p t j -> p (t j)")
+                out=g_codes[:, t0 : t0 + n].bitcast(E5M2X4),
+                scales=g_plane[:, t0 : t0 + n],
+                in_=g_bf[:].rearrange("p t j -> p (t j)"),
             )
 
-        def product(i):
-            acc = psum.tile([P, D], F32, name=f"acc{i % 2}")
+        for h in range(2):
+            gather1(0, h * HALF, z0[h][:])
+        for h in range(2):
+            gather2(0, h * HALF, HALF)
+        for h in range(2):
+            gather1(1, h * HALF, z1[:, h * HALF : (h + 1) * HALF])
+        for h in range(2):
+            gather2(1, h * HALF, HALF)
+        for j in (2, 3):
+            gather1(j, 0, z_half[j - 2][:])
+        for j in (2, 3):
+            gather2(j, 0, HALF)
+        g_bf01 = sbuf("g_bf01", [P, HALF, LANES], BF16)
+        for i in range(2):
+            round_g(i * TILE, g_bf01[:, i * TILE : (i + 1) * TILE, :])
+        for j in (2, 3):
+            gather1(j, 2 * TILE, z_late[0][:, j - 2, :])
+        for j in (2, 3):
+            gather2(j, 2 * TILE, TILE)
+        g_bf2 = sbuf("g_bf2", [P, TILE, LANES], BF16)
+        round_g(2 * TILE, g_bf2[:])
+        quantise_g(0, g_bf01)
+        w_dealt = w_raw[:].bitcast(U16).rearrange("p (m j) -> p j m", j=LANES)
+        w_first = sbuf("w_first", [P, P], U16)
+        nc.vector.tensor_copy(w_first[:], w_dealt[:, 0, :])
+        for j in (2, 3):
+            gather1(j, 3 * TILE, z_late[1][:, j - 2, :])
+        for j in (2, 3):
+            gather2(j, 3 * TILE, TILE)
+        g_bf3 = sbuf("g_bf3", [P, TILE, LANES], BF16)
+        round_g(3 * TILE, g_bf3[:], True)
+        w_plane = sbuf("w_plane", [P, LANES, P], U8, "neg_e")
+        nc.vector.tensor_copy(w_plane[:], w_plane_raw[:].rearrange("p (m j) -> p j m", j=LANES))
+        quantise_g(2 * TILE, g_bf2)
+        quantise_g(3 * TILE, g_bf3)
+        w_rest = sbuf("w_rest", [P, LANES - 1, P], U16, "g_bf3")
+        nc.vector.tensor_copy(w_rest[:], w_dealt[:, 1:LANES, :])
+
+        y = sbuf("y", [P, LANES, T], F32)
+        for j in range(LANES):
+            acc = psum.tile([P, T], F32, name=f"acc{j}")
+            w_cols = w_first[:] if j == 0 else w_rest[:, j - 1, :]
             nc.tensor.matmul_mx(
                 out=acc[:],
-                lhsT=g_codes[i][:].bitcast(E5M2X4),
-                lhsT_scale=g_plane[i][:],
-                rhs=w_codes[:].bitcast(E2M1X4),
-                rhs_scale=w_plane[:],
+                lhsT=w_cols.bitcast(U8).bitcast(E2M1X4),
+                lhsT_scale=w_plane[:, j, :],
+                rhs=g_codes[:].bitcast(E5M2X4),
+                rhs_scale=g_plane[:],
                 start=True,
                 stop=True,
             )
-            nc.scalar.copy(y_tok[i][:], acc[:].rearrange("t (p j) -> t j p", j=LANES))
+            if j == 1:
+                nc.vector.tensor_copy(y[:, j, :], acc[:])
+            elif j < LANES - 1:
+                nc.scalar.copy(y[:, j, :], acc[:])
+            else:
+                for h in range(2):
+                    nc.scalar.copy(y[:, j, h * HALF : (h + 1) * HALF], acc[:, h * HALF : (h + 1) * HALF])
+            nc.sync.dma_start(out_rows[:, j, :], y[:, j, :])
 
-        def turn(i, name):
-            bank = psum.tile([P, LANES, TILE], F32, name=name)
-            for j in range(LANES):
-                nc.tensor.transpose(bank[:, j, :], y_tok[i][:, j, :], ident[:])
-            return bank
-
-        def store_y(i, bank):
-            nc.scalar.copy(y[i][:], bank[:])
-            nc.sync.dma_start(out_rows[:, :, i * TILE : (i + 1) * TILE], y[i][:])
-
-        def quantise_y(i):
+        y_plane = sbuf("y_plane", [P, T], U8)
+        y_bf = [sbuf(f"y_bf{h}", [P, HALF, LANES], BF16) for h in range(2)]
+        nc.vector.tensor_copy(*weave_views(y_bf[0][:], y[:, :, 0:HALF]))
+        nc.scalar.copy(*weave_views(y_bf[1][:, 0:TILE, :], y[:, :, HALF : 3 * TILE]))
+        nc.vector.tensor_copy(*weave_views(y_bf[1][:, TILE:HALF, :], y[:, :, 3 * TILE : T]))
+        for h in range(2):
+            cols = slice(h * HALF, (h + 1) * HALF)
+            y_codes = sbuf(f"y_codes{h}", [P, HALF], U32)
             nc.vector.quantize_mx(
-                out=y_codes[i][:].bitcast(E4M3X4),
-                scales=y_plane[:, i * TILE : (i + 1) * TILE],
-                in_=y_bf[i][:].rearrange("p t j -> p (t j)"),
+                out=y_codes[:].bitcast(E4M3X4), scales=y_plane[:, cols], in_=y_bf[h][:].rearrange("p t j -> p (t j)")
             )
-            nc.sync.dma_start(out_words[:, i * TILE : (i + 1) * TILE], y_codes[i][:].bitcast(I32))
-
-        gather1(0, 0, HALF)
-        gather1(0, HALF, HALF)
-        gather2(0, 0, HALF)
-        gather2(0, HALF, HALF)
-        gather1(1, 0, HALF)
-        gather1(2, 0, HALF)
-        gather2(1, 0, HALF)
-        gather1(3, 0, HALF)
-        gather2(2, 0, HALF)
-        gather2(3, 0, TILE)
-        gather2(3, TILE, TILE)
-        round_g(0, False)
-        round_g(1, False)
-        for j in range(1, LANES):
-            gather1(j, 2 * TILE, TILE)
-        quantise_g(0)
-        product(0)
-        for j in range(1, LANES):
-            gather2(j, 2 * TILE, TILE)
-        quantise_g(1)
-        product(1)
-        round_g(2, False)
-        for j in range(1, LANES):
-            gather1(j, 3 * TILE, TILE)
-        quantise_g(2)
-        for i in range(2):
-            store_y(i, turn(i, f"turn{i}"))
-        product(2)
-        for j in range(1, LANES):
-            gather2(j, 3 * TILE, TILE)
-        round_g(3, True)
-        quantise_g(3)
-        store_y(2, turn(2, "turn2"))
-        product(3)
-        for i in range(3):
-            dst, src = weave_views(y_bf[i][:], y[i][:])
-            nc.vector.tensor_copy(dst, src)
-        for i in range(3):
-            quantise_y(i)
-        bank_b = turn(3, "turn3b")
-        bank_f = turn(3, "turn3f")
-        nc.vector.tensor_copy(y_bf[3][:], bank_b[:].rearrange("p j t -> p t j"))
-        store_y(3, bank_f)
-        quantise_y(3)
+            nc.sync.dma_start(out_words[:, cols], y_codes[:].bitcast(I32))
         for q in range(4):
             queue = nc.scalar if q % 2 else nc.sync
             queue.dma_start(out_scales[4 * q : 4 * q + 4, :], y_plane[32 * q : 32 * q + 4, :].bitcast(I32))

@@ -20,11 +20,17 @@ COPY = mybir.ActivationFunctionType.Copy
 
 P = 128
 LANES = 4
-TILE = 128
-HALF = 256
+QUADRANTS = 4
+PER_COLUMN = 16
+HALF = T // 2
+QUARTER = T // 4
+LATE_LANES = (2, 3)
+RUN = 4
 
 
-def tile_attend_gvq_pl_r_x_kernel(tc, zT, cb, cb2, w_words, w_scales, offs, offs2, out_0, out_1, out_2):
+def tile_attend_gvq_pl_r_x_kernel(
+    tc, zT, cb, cb2, w_words, w_scales, offs, offs2, out_0, out_1, out_2
+):
     nc = tc.nc
     with ExitStack() as ctx:
         keep = ctx.enter_context(tc.tile_pool(name="keep", bufs=1))
@@ -33,14 +39,14 @@ def tile_attend_gvq_pl_r_x_kernel(tc, zT, cb, cb2, w_words, w_scales, offs, offs
         def sbuf(name, shape, dtype, tag=None):
             return keep.tile(shape, dtype, name=name, tag=tag or name, align_bytes=64)
 
-        code = keep.tile([P, T // 16], U16, name="code")
-        code2 = keep.tile([P, T // 16], U16, name="code2")
+        code = keep.tile([P, T // PER_COLUMN], U16, name="code")
+        code2 = keep.tile([P, T // PER_COLUMN], U16, name="code2")
         book = [sbuf(f"book{j}", [P, C], F32) for j in range(LANES)]
         book2 = [sbuf(f"book2_{j}", [P, C], F32) for j in range(LANES)]
         z0 = [sbuf(f"z0_{h}", [P, HALF], F32) for h in range(2)]
         z1 = sbuf("z1", [P, T], F32)
-        z_half = [sbuf(f"z_half{j}", [P, HALF], F32) for j in (2, 3)]
-        z_late = [sbuf(f"z_late{i}", [P, 2, TILE], F32) for i in (2, 3)]
+        z_half = {j: sbuf(f"z_half{j}", [P, HALF], F32) for j in LATE_LANES}
+        z_late = {i: sbuf(f"z_late{i}", [P, 2, QUARTER], F32) for i in (2, 3)}
         w_raw = sbuf("w_raw", [P, 2 * D], U8)
         w_plane_raw = sbuf("w_plane_raw", [P, D], U8)
 
@@ -52,7 +58,7 @@ def tile_attend_gvq_pl_r_x_kernel(tc, zT, cb, cb2, w_words, w_scales, offs, offs
         out_scales = out_2[0].bitcast(I32)
 
         nc.vector.memset(w_plane_raw[:].bitcast(I32), 0)
-        for q in range(4):
+        for q in range(QUADRANTS):
             nc.gpsimd.dma_start(
                 w_plane_raw[32 * q : 32 * q + 4, :].bitcast(I32), w_scales[0, 4 * q : 4 * q + 4, :].bitcast(I32)
             )
@@ -66,13 +72,13 @@ def tile_attend_gvq_pl_r_x_kernel(tc, zT, cb, cb2, w_words, w_scales, offs, offs
         nc.sync.dma_start(book[1][:], cb_rows[:, 1, :])
         nc.sync.dma_start(z1[:], z_rows[:, 1, :])
         nc.sync.dma_start(book2[1][:], cb2_rows[:, 1, :])
-        for j in (2, 3):
+        for j in LATE_LANES:
             nc.sync.dma_start(book[j][:], cb_rows[:, j, :])
-            nc.sync.dma_start(z_half[j - 2][:], z_rows[:, j, 0:HALF])
-        for j in (2, 3):
+            nc.sync.dma_start(z_half[j][:], z_rows[:, j, 0:HALF])
+        for j in LATE_LANES:
             nc.sync.dma_start(book2[j][:], cb2_rows[:, j, :])
         for i in (2, 3):
-            nc.sync.dma_start(z_late[i - 2][:], z_rows[:, 2:LANES, i * TILE : (i + 1) * TILE])
+            nc.sync.dma_start(z_late[i][:], z_rows[:, 2:LANES, i * QUARTER : (i + 1) * QUARTER])
         nc.sync.dma_start(w_raw[:].bitcast(I32), w_words[0].bitcast(I32))
 
         part = sbuf("part", [P, LANES, T], F32)
@@ -82,7 +88,7 @@ def tile_attend_gvq_pl_r_x_kernel(tc, zT, cb, cb2, w_words, w_scales, offs, offs
             n = z_cols.shape[1]
             nc.vector.tensor_tensor(
                 part[:, j, t0 : t0 + n],
-                book[j][:].indirect(code[:, t0 // 16 : (t0 + n) // 16]),
+                book[j][:].indirect(code[:, t0 // PER_COLUMN : (t0 + n) // PER_COLUMN]),
                 z_cols,
                 ALU.subtract,
             )
@@ -90,26 +96,22 @@ def tile_attend_gvq_pl_r_x_kernel(tc, zT, cb, cb2, w_words, w_scales, offs, offs
         def gather2(j, t0, n):
             nc.vector.tensor_tensor(
                 neg_e[:, j, t0 : t0 + n],
-                book2[j][:].indirect(code2[:, t0 // 16 : (t0 + n) // 16]),
+                book2[j][:].indirect(code2[:, t0 // PER_COLUMN : (t0 + n) // PER_COLUMN]),
                 part[:, j, t0 : t0 + n],
                 ALU.add,
             )
 
         def weave_views(dst, src):
             return (
-                dst.rearrange("p (c i) j -> p c j i", i=4),
-                src.rearrange("p j (c i) -> p c j i", i=4),
+                dst.rearrange("p (c i) j -> p c j i", i=RUN),
+                src.rearrange("p j (c i) -> p c j i", i=RUN),
             )
+
+        def weave_g_on_scalar(t0, g_bf):
+            nc.scalar.activation(*weave_views(g_bf, neg_e[:, :, t0 : t0 + QUARTER]), COPY, scale=-BETA)
 
         g_codes = sbuf("g_codes", [P, T], U32)
         g_plane = sbuf("g_plane", [P, T], U8)
-
-        def round_g(t0, g_bf, on_vector=False):
-            dst, src = weave_views(g_bf, neg_e[:, :, t0 : t0 + TILE])
-            if on_vector:
-                nc.vector.tensor_scalar(dst, src, -BETA, None, ALU.mult)
-            else:
-                nc.scalar.activation(dst, src, COPY, scale=-BETA)
 
         def quantise_g(t0, g_bf):
             n = g_bf.shape[1]
@@ -127,44 +129,51 @@ def tile_attend_gvq_pl_r_x_kernel(tc, zT, cb, cb2, w_words, w_scales, offs, offs
             gather1(1, h * HALF, z1[:, h * HALF : (h + 1) * HALF])
         for h in range(2):
             gather2(1, h * HALF, HALF)
-        for j in (2, 3):
-            gather1(j, 0, z_half[j - 2][:])
-        for j in (2, 3):
+
+        for j in LATE_LANES:
+            gather1(j, 0, z_half[j][:])
+        for j in LATE_LANES:
             gather2(j, 0, HALF)
         g_bf01 = sbuf("g_bf01", [P, HALF, LANES], BF16)
         for i in range(2):
-            round_g(i * TILE, g_bf01[:, i * TILE : (i + 1) * TILE, :])
-        for j in (2, 3):
-            gather1(j, 2 * TILE, z_late[0][:, j - 2, :])
-        for j in (2, 3):
-            gather2(j, 2 * TILE, TILE)
-        g_bf2 = sbuf("g_bf2", [P, TILE, LANES], BF16)
-        round_g(2 * TILE, g_bf2[:])
+            weave_g_on_scalar(i * QUARTER, g_bf01[:, i * QUARTER : (i + 1) * QUARTER, :])
+
+        for k, j in enumerate(LATE_LANES):
+            gather1(j, 2 * QUARTER, z_late[2][:, k, :])
+        for j in LATE_LANES:
+            gather2(j, 2 * QUARTER, QUARTER)
+        g_bf2 = sbuf("g_bf2", [P, QUARTER, LANES], BF16)
+        weave_g_on_scalar(2 * QUARTER, g_bf2[:])
         quantise_g(0, g_bf01)
+
+        for k, j in enumerate(LATE_LANES):
+            gather1(j, 3 * QUARTER, z_late[3][:, k, :])
+        for j in LATE_LANES:
+            gather2(j, 3 * QUARTER, QUARTER)
+
         w_dealt = w_raw[:].bitcast(U16).rearrange("p (m j) -> p j m", j=LANES)
-        w_first = sbuf("w_first", [P, P], U16)
-        nc.vector.tensor_copy(w_first[:], w_dealt[:, 0, :])
-        for j in (2, 3):
-            gather1(j, 3 * TILE, z_late[1][:, j - 2, :])
-        for j in (2, 3):
-            gather2(j, 3 * TILE, TILE)
-        g_bf3 = sbuf("g_bf3", [P, TILE, LANES], BF16)
-        round_g(3 * TILE, g_bf3[:], True)
-        w_plane = sbuf("w_plane", [P, LANES, P], U8, "neg_e")
-        nc.vector.tensor_copy(w_plane[:], w_plane_raw[:].rearrange("p (m j) -> p j m", j=LANES))
-        quantise_g(2 * TILE, g_bf2)
-        quantise_g(3 * TILE, g_bf3)
-        w_rest = sbuf("w_rest", [P, LANES - 1, P], U16, "g_bf3")
-        nc.vector.tensor_copy(w_rest[:], w_dealt[:, 1:LANES, :])
+        plane_dealt = w_plane_raw[:].rearrange("p (m j) -> p j m", j=LANES)
+        w_first = sbuf("w_first", [P, 2, P], U16, "book2_2")
+        nc.vector.tensor_copy(w_first[:], w_dealt[:, 0:2, :])
+        g_bf3 = sbuf("g_bf3", [P, QUARTER, LANES], BF16)
+        nc.vector.tensor_scalar(*weave_views(g_bf3[:], neg_e[:, :, 3 * QUARTER : T]), -BETA, None, ALU.mult)
+        plane_first = sbuf("plane_first", [P, P], U8, "neg_e")
+        nc.vector.tensor_copy(plane_first[:], plane_dealt[:, 0, :])
+        quantise_g(2 * QUARTER, g_bf2)
+        quantise_g(3 * QUARTER, g_bf3)
+        w_rest = sbuf("w_rest", [P, 2, P], U16, "g_bf3")
+        nc.vector.tensor_copy(w_rest[:], w_dealt[:, 2:LANES, :])
+        plane_rest = sbuf("plane_rest", [P, LANES - 1, P], U8, "g_bf2")
+        nc.vector.tensor_copy(plane_rest[:], plane_dealt[:, 1:LANES, :])
 
         y = sbuf("y", [P, LANES, T], F32)
         for j in range(LANES):
             acc = psum.tile([P, T], F32, name=f"acc{j}")
-            w_cols = w_first[:] if j == 0 else w_rest[:, j - 1, :]
+            w_cols = w_first[:, j, :] if j < 2 else w_rest[:, j - 2, :]
             nc.tensor.matmul_mx(
                 out=acc[:],
                 lhsT=w_cols.bitcast(U8).bitcast(E2M1X4),
-                lhsT_scale=w_plane[:, j, :],
+                lhsT_scale=plane_first[:] if j == 0 else plane_rest[:, j - 1, :],
                 rhs=g_codes[:].bitcast(E5M2X4),
                 rhs_scale=g_plane[:],
                 start=True,
@@ -175,15 +184,17 @@ def tile_attend_gvq_pl_r_x_kernel(tc, zT, cb, cb2, w_words, w_scales, offs, offs
             elif j < LANES - 1:
                 nc.scalar.copy(y[:, j, :], acc[:])
             else:
-                for h in range(2):
-                    nc.scalar.copy(y[:, j, h * HALF : (h + 1) * HALF], acc[:, h * HALF : (h + 1) * HALF])
+                for t0, t1 in ((0, QUARTER), (QUARTER, HALF), (HALF, T)):
+                    nc.scalar.copy(y[:, j, t0:t1], acc[:, t0:t1])
             nc.sync.dma_start(out_rows[:, j, :], y[:, j, :])
 
         y_plane = sbuf("y_plane", [P, T], U8)
         y_bf = [sbuf(f"y_bf{h}", [P, HALF, LANES], BF16) for h in range(2)]
-        nc.vector.tensor_copy(*weave_views(y_bf[0][:], y[:, :, 0:HALF]))
-        nc.scalar.copy(*weave_views(y_bf[1][:, 0:TILE, :], y[:, :, HALF : 3 * TILE]))
-        nc.vector.tensor_copy(*weave_views(y_bf[1][:, TILE:HALF, :], y[:, :, 3 * TILE : T]))
+        for i in range(2):
+            cols = slice(i * QUARTER, (i + 1) * QUARTER)
+            nc.vector.tensor_copy(*weave_views(y_bf[0][:, cols, :], y[:, :, cols]))
+        nc.scalar.copy(*weave_views(y_bf[1][:, 0:QUARTER, :], y[:, :, HALF : 3 * QUARTER]))
+        nc.vector.tensor_copy(*weave_views(y_bf[1][:, QUARTER:HALF, :], y[:, :, 3 * QUARTER : T]))
         for h in range(2):
             cols = slice(h * HALF, (h + 1) * HALF)
             y_codes = sbuf(f"y_codes{h}", [P, HALF], U32)
@@ -191,6 +202,6 @@ def tile_attend_gvq_pl_r_x_kernel(tc, zT, cb, cb2, w_words, w_scales, offs, offs
                 out=y_codes[:].bitcast(E4M3X4), scales=y_plane[:, cols], in_=y_bf[h][:].rearrange("p t j -> p (t j)")
             )
             nc.sync.dma_start(out_words[:, cols], y_codes[:].bitcast(I32))
-        for q in range(4):
+        for q in range(QUADRANTS):
             queue = nc.scalar if q % 2 else nc.sync
             queue.dma_start(out_scales[4 * q : 4 * q + 4, :], y_plane[32 * q : 32 * q + 4, :].bitcast(I32))

@@ -1,6 +1,7 @@
 from contextlib import ExitStack
 
 import concourse.mybir as mybir
+from concourse.masks import make_identity
 
 T, C, D, N = 512, 512, 512, 512
 FLOPS = 2 * N * D * T
@@ -22,9 +23,8 @@ P = 128
 LANES = 4
 QUADRANTS = 4
 PER_COLUMN = 16
-HALF = T // 2
-QUARTER = T // 4
-LATE_LANES = (2, 3)
+Q = 128
+TA = 3 * Q
 RUN = 4
 
 
@@ -41,14 +41,17 @@ def tile_attend_gvq_pl_r_x_kernel(
 
         code = keep.tile([P, T // PER_COLUMN], U16, name="code")
         code2 = keep.tile([P, T // PER_COLUMN], U16, name="code2")
-        book = [sbuf(f"book{j}", [P, C], F32) for j in range(LANES)]
+        book = [sbuf(f"book{j}", [P, C if j == 0 else 2 * TA], F32) for j in range(LANES)]
         book2 = [sbuf(f"book2_{j}", [P, C], F32) for j in range(LANES)]
-        z0 = [sbuf(f"z0_{h}", [P, HALF], F32) for h in range(2)]
-        z1 = sbuf("z1", [P, T], F32)
-        z_half = {j: sbuf(f"z_half{j}", [P, HALF], F32) for j in LATE_LANES}
-        z_late = {i: sbuf(f"z_late{i}", [P, 2, QUARTER], F32) for i in (2, 3)}
+        z0a = sbuf("z0a", [P, Q], F32)
+        z0b = sbuf("z0b", [P, TA - Q], F32)
+        za = {j: sbuf(f"za{j}", [P, TA], F32) for j in (1, 2, 3)}
+        zb = sbuf("zb", [P, LANES, Q], F32)
         w_raw = sbuf("w_raw", [P, 2 * D], U8)
         w_plane_raw = sbuf("w_plane_raw", [P, D], U8)
+        ident = sbuf("ident", [P, P], F32)
+        ga_codes = sbuf("ga_codes", [P, T], U32)
+        ga_plane = sbuf("ga_plane", [P, T], U8)
 
         z_rows = zT.rearrange("(p j) t -> p j t", j=LANES)
         cb_rows = cb.rearrange("(p j) c -> p j c", j=LANES)
@@ -58,47 +61,41 @@ def tile_attend_gvq_pl_r_x_kernel(
         out_scales = out_2[0].bitcast(I32)
 
         nc.vector.memset(w_plane_raw[:].bitcast(I32), 0)
+        nc.vector.memset(ga_codes[:, TA:T], 0)
+        nc.vector.memset(ga_plane[:, TA:T].bitcast(I32), 0)
+        for j in (1, 2, 3):
+            nc.vector.memset(book[j][:, C:], 0.0)
         for q in range(QUADRANTS):
             nc.gpsimd.dma_start(
                 w_plane_raw[32 * q : 32 * q + 4, :].bitcast(I32), w_scales[0, 4 * q : 4 * q + 4, :].bitcast(I32)
             )
+        make_identity(nc, ident[:])
 
         nc.sync.dma_start(book[0][:], cb_rows[:, 0, :])
         nc.sync.dma_start(code[:], offs)
-        for h in range(2):
-            nc.sync.dma_start(z0[h][:], z_rows[:, 0, h * HALF : (h + 1) * HALF])
+        nc.sync.dma_start(z0a[:], z_rows[:, 0, 0:Q])
+        nc.sync.dma_start(z0b[:], z_rows[:, 0, Q:TA])
         nc.sync.dma_start(book2[0][:], cb2_rows[:, 0, :])
         nc.sync.dma_start(code2[:], offs2)
-        nc.sync.dma_start(book[1][:], cb_rows[:, 1, :])
-        nc.sync.dma_start(z1[:], z_rows[:, 1, :])
-        nc.sync.dma_start(book2[1][:], cb2_rows[:, 1, :])
-        for j in LATE_LANES:
-            nc.sync.dma_start(book[j][:], cb_rows[:, j, :])
-            nc.sync.dma_start(z_half[j][:], z_rows[:, j, 0:HALF])
-        for j in LATE_LANES:
-            nc.sync.dma_start(book2[j][:], cb2_rows[:, j, :])
-        for i in (2, 3):
-            nc.sync.dma_start(z_late[i][:], z_rows[:, 2:LANES, i * QUARTER : (i + 1) * QUARTER])
+        for j in (1, 2, 3):
+            nc.sync.dma_start(book[j][:, 0:C], cb_rows[:, j, :])
+            nc.sync.dma_start(za[j][:], z_rows[:, j, 0:TA])
+            if j > 1:
+                nc.sync.dma_start(book2[j - 1][:], cb2_rows[:, j - 1, :])
+        nc.sync.dma_start(book2[3][:], cb2_rows[:, 3, :])
+        nc.sync.dma_start(zb[:], z_rows[:, :, TA:T])
         nc.sync.dma_start(w_raw[:].bitcast(I32), w_words[0].bitcast(I32))
 
-        part = sbuf("part", [P, LANES, T], F32)
-        neg_e = sbuf("neg_e", [P, LANES, T], F32)
-
-        def gather1(j, t0, z_cols):
+        def gather1(dst, j, t0, z_cols):
             n = z_cols.shape[1]
             nc.vector.tensor_tensor(
-                part[:, j, t0 : t0 + n],
-                book[j][:].indirect(code[:, t0 // PER_COLUMN : (t0 + n) // PER_COLUMN]),
-                z_cols,
-                ALU.subtract,
+                dst, book[j][:].indirect(code[:, t0 // PER_COLUMN : (t0 + n) // PER_COLUMN]), z_cols, ALU.subtract
             )
 
-        def gather2(j, t0, n):
+        def gather2(dst, j, t0, part_cols):
+            n = part_cols.shape[1]
             nc.vector.tensor_tensor(
-                neg_e[:, j, t0 : t0 + n],
-                book2[j][:].indirect(code2[:, t0 // PER_COLUMN : (t0 + n) // PER_COLUMN]),
-                part[:, j, t0 : t0 + n],
-                ALU.add,
+                dst, book2[j][:].indirect(code2[:, t0 // PER_COLUMN : (t0 + n) // PER_COLUMN]), part_cols, ALU.add
             )
 
         def weave_views(dst, src):
@@ -107,101 +104,121 @@ def tile_attend_gvq_pl_r_x_kernel(
                 src.rearrange("p j (c i) -> p c j i", i=RUN),
             )
 
-        def weave_g_on_scalar(t0, g_bf):
-            nc.scalar.activation(*weave_views(g_bf, neg_e[:, :, t0 : t0 + QUARTER]), COPY, scale=-BETA)
+        def quantise(codes, plane, src, fmt):
+            nc.vector.quantize_mx(out=codes.bitcast(fmt), scales=plane, in_=src.rearrange("p t j -> p (t j)"))
 
-        g_codes = sbuf("g_codes", [P, T], U32)
-        g_plane = sbuf("g_plane", [P, T], U8)
+        part = sbuf("part", [P, LANES, TA], F32)
+        neg_a = sbuf("neg_a", [P, LANES, TA], F32)
 
-        def quantise_g(t0, g_bf):
-            n = g_bf.shape[1]
-            nc.vector.quantize_mx(
-                out=g_codes[:, t0 : t0 + n].bitcast(E5M2X4),
-                scales=g_plane[:, t0 : t0 + n],
-                in_=g_bf[:].rearrange("p t j -> p (t j)"),
-            )
+        gather1(part[:, 0, 0:Q], 0, 0, z0a[:])
+        gather1(part[:, 0, Q:TA], 0, Q, z0b[:])
+        gather2(neg_a[:, 0, 0:Q], 0, 0, part[:, 0, 0:Q])
+        gather2(neg_a[:, 0, Q:TA], 0, Q, part[:, 0, Q:TA])
+        for j in (1, 2, 3):
+            gather1(part[:, j, :], j, 0, za[j][:])
+            if j > 1:
+                gather2(neg_a[:, j - 1, :], j - 1, 0, part[:, j - 1, :])
 
-        for h in range(2):
-            gather1(0, h * HALF, z0[h][:])
-        for h in range(2):
-            gather2(0, h * HALF, HALF)
-        for h in range(2):
-            gather1(1, h * HALF, z1[:, h * HALF : (h + 1) * HALF])
-        for h in range(2):
-            gather2(1, h * HALF, HALF)
+        ga_bf01 = sbuf("ga_bf01", [P, 2 * Q, LANES], BF16)
+        ga_bf2 = sbuf("ga_bf2", [P, Q, LANES], BF16)
 
-        for j in LATE_LANES:
-            gather1(j, 0, z_half[j][:])
-        for j in LATE_LANES:
-            gather2(j, 0, HALF)
-        g_bf01 = sbuf("g_bf01", [P, HALF, LANES], BF16)
-        for i in range(2):
-            weave_g_on_scalar(i * QUARTER, g_bf01[:, i * QUARTER : (i + 1) * QUARTER, :])
+        def lane3_second(i):
+            gather2(neg_a[:, 3, i * Q : (i + 1) * Q], 3, i * Q, part[:, 3, i * Q : (i + 1) * Q])
+            dst = ga_bf01[:, i * Q : (i + 1) * Q, :] if i < 2 else ga_bf2[:]
+            nc.scalar.activation(*weave_views(dst, neg_a[:, :, i * Q : (i + 1) * Q]), COPY, scale=-BETA)
 
-        for k, j in enumerate(LATE_LANES):
-            gather1(j, 2 * QUARTER, z_late[2][:, k, :])
-        for j in LATE_LANES:
-            gather2(j, 2 * QUARTER, QUARTER)
-        g_bf2 = sbuf("g_bf2", [P, QUARTER, LANES], BF16)
-        weave_g_on_scalar(2 * QUARTER, g_bf2[:])
-        quantise_g(0, g_bf01)
-
-        for k, j in enumerate(LATE_LANES):
-            gather1(j, 3 * QUARTER, z_late[3][:, k, :])
-        for j in LATE_LANES:
-            gather2(j, 3 * QUARTER, QUARTER)
+        for i in range(3):
+            lane3_second(i)
 
         w_dealt = w_raw[:].bitcast(U16).rearrange("p (m j) -> p j m", j=LANES)
         plane_dealt = w_plane_raw[:].rearrange("p (m j) -> p j m", j=LANES)
-        w_first = sbuf("w_first", [P, 2, P], U16, "book2_2")
+        part_b01 = sbuf("part_b01", [P, 2, Q], F32)
+        for j in (0, 1):
+            gather1(part_b01[:, j, :], j, TA, zb[:, j, :])
+        w_first = sbuf("w_first", [P, 2, P], U16)
         nc.vector.tensor_copy(w_first[:], w_dealt[:, 0:2, :])
-        g_bf3 = sbuf("g_bf3", [P, QUARTER, LANES], BF16)
-        nc.vector.tensor_scalar(*weave_views(g_bf3[:], neg_e[:, :, 3 * QUARTER : T]), -BETA, None, ALU.mult)
-        plane_first = sbuf("plane_first", [P, P], U8, "neg_e")
-        nc.vector.tensor_copy(plane_first[:], plane_dealt[:, 0, :])
-        quantise_g(2 * QUARTER, g_bf2)
-        quantise_g(3 * QUARTER, g_bf3)
-        w_rest = sbuf("w_rest", [P, 2, P], U16, "g_bf3")
-        nc.vector.tensor_copy(w_rest[:], w_dealt[:, 2:LANES, :])
-        plane_rest = sbuf("plane_rest", [P, LANES - 1, P], U8, "g_bf2")
-        nc.vector.tensor_copy(plane_rest[:], plane_dealt[:, 1:LANES, :])
+        plane_first = sbuf("plane_first", [P, 2, P], U8, "part")
+        nc.vector.tensor_copy(plane_first[:], plane_dealt[:, 0:2, :])
+        quantise(ga_codes[:, 0 : 2 * Q], ga_plane[:, 0 : 2 * Q], ga_bf01[:], E5M2X4)
+        part_b23 = sbuf("part_b23", [P, 2, Q], F32, "ga_bf01")
+        gather1(part_b23[:, 0, :], 2, TA, zb[:, 2, :])
+        quantise(ga_codes[:, 2 * Q : TA], ga_plane[:, 2 * Q : TA], ga_bf2[:], E5M2X4)
+        gather1(part_b23[:, 1, :], 3, TA, zb[:, 3, :])
+        neg_b = sbuf("neg_b", [P, LANES, Q], F32, "ga_bf2")
+        w_rest = sbuf("w_rest", [P, 2, P], U16, "book0")
+        plane_rest = sbuf("plane_rest", [P, 2, P], U8, "book3")
+        gather2(neg_b[:, 0, :], 0, TA, part_b01[:, 0, :])
+        nc.vector.tensor_copy(w_rest[:], w_dealt[:, 2:4, :])
+        nc.vector.tensor_copy(plane_rest[:], plane_dealt[:, 2:4, :])
+        gather2(neg_b[:, 1, :], 1, TA, part_b01[:, 1, :])
+        gather2(neg_b[:, 2, :], 2, TA, part_b23[:, 0, :])
+        gather2(neg_b[:, 3, :], 3, TA, part_b23[:, 1, :])
+        gb_bf = sbuf("gb_bf", [P, Q, LANES], BF16)
+        nc.vector.tensor_scalar(*weave_views(gb_bf[:], neg_b[:]), -BETA, None, ALU.mult)
+        gb_codes = sbuf("gb_codes", [P, Q], U32)
+        gb_plane = sbuf("gb_plane", [P, Q], U8)
+        quantise(gb_codes[:], gb_plane[:], gb_bf[:], E5M2X4)
 
-        y = sbuf("y", [P, LANES, T], F32)
+        ya = sbuf("ya", [P, LANES, TA], F32)
         for j in range(LANES):
             acc = psum.tile([P, T], F32, name=f"acc{j}")
-            w_cols = w_first[:, j, :] if j < 2 else w_rest[:, j - 2, :]
             nc.tensor.matmul_mx(
                 out=acc[:],
-                lhsT=w_cols.bitcast(U8).bitcast(E2M1X4),
-                lhsT_scale=plane_first[:] if j == 0 else plane_rest[:, j - 1, :],
-                rhs=g_codes[:].bitcast(E5M2X4),
-                rhs_scale=g_plane[:],
+                lhsT=(w_first if j < 2 else w_rest)[:, j % 2, :].bitcast(U8).bitcast(E2M1X4),
+                lhsT_scale=(plane_first if j < 2 else plane_rest)[:, j % 2, :],
+                rhs=ga_codes[:].bitcast(E5M2X4),
+                rhs_scale=ga_plane[:],
                 start=True,
                 stop=True,
             )
-            if j == 1:
-                nc.vector.tensor_copy(y[:, j, :], acc[:])
-            elif j < LANES - 1:
-                nc.scalar.copy(y[:, j, :], acc[:])
+            if j < LANES - 1:
+                nc.scalar.copy(ya[:, j, :], acc[:, 0:TA])
             else:
-                for t0, t1 in ((0, QUARTER), (QUARTER, HALF), (HALF, T)):
-                    nc.scalar.copy(y[:, j, t0:t1], acc[:, t0:t1])
-            nc.sync.dma_start(out_rows[:, j, :], y[:, j, :])
+                for i in range(3):
+                    nc.scalar.copy(ya[:, j, i * Q : (i + 1) * Q], acc[:, i * Q : (i + 1) * Q])
+            nc.sync.dma_start(out_rows[:, j, 0:TA], ya[:, j, :])
+
+        acc_b = psum.tile([P, D], F32, name="acc_b")
+        nc.tensor.matmul_mx(
+            out=acc_b[:],
+            lhsT=gb_codes[:].bitcast(E5M2X4),
+            lhsT_scale=gb_plane[:],
+            rhs=w_raw[:].bitcast(E2M1X4),
+            rhs_scale=w_plane_raw[:],
+            start=True,
+            stop=True,
+        )
+        acc_dealt = acc_b[:].rearrange("t (m j) -> t j m", j=LANES)
+        turned = psum.tile([P, LANES, Q], F32, name="turned")
+        turned_pair = [psum.tile([P, 2, Q], F32, name=f"turned_pair{u}") for u in range(2)]
+        for u in range(2):
+            yb_t = sbuf(f"yb_t{u}", [P, 2, P], F32)
+            nc.scalar.copy(yb_t[:], acc_dealt[:, 2 * u : 2 * u + 2, :])
+            for e in range(2):
+                nc.tensor.transpose(turned[:, 2 * u + e, :], yb_t[:, e, :], ident[:])
+            for e in range(2):
+                nc.tensor.transpose(turned_pair[u][:, e, :], yb_t[:, e, :], ident[:])
+        for u in range(2):
+            yb = sbuf(f"yb{u}", [P, 2, Q], F32)
+            nc.scalar.copy(yb[:], turned_pair[u][:])
+            nc.sync.dma_start(out_rows[:, 2 * u : 2 * u + 2, TA:T], yb[:])
 
         y_plane = sbuf("y_plane", [P, T], U8)
-        y_bf = [sbuf(f"y_bf{h}", [P, HALF, LANES], BF16) for h in range(2)]
+        ya_bf01 = sbuf("ya_bf01", [P, 2 * Q, LANES], BF16)
+        ya_bf2 = sbuf("ya_bf2", [P, Q, LANES], BF16)
         for i in range(2):
-            cols = slice(i * QUARTER, (i + 1) * QUARTER)
-            nc.vector.tensor_copy(*weave_views(y_bf[0][:, cols, :], y[:, :, cols]))
-        nc.scalar.copy(*weave_views(y_bf[1][:, 0:QUARTER, :], y[:, :, HALF : 3 * QUARTER]))
-        nc.vector.tensor_copy(*weave_views(y_bf[1][:, QUARTER:HALF, :], y[:, :, 3 * QUARTER : T]))
-        for h in range(2):
-            cols = slice(h * HALF, (h + 1) * HALF)
-            y_codes = sbuf(f"y_codes{h}", [P, HALF], U32)
-            nc.vector.quantize_mx(
-                out=y_codes[:].bitcast(E4M3X4), scales=y_plane[:, cols], in_=y_bf[h][:].rearrange("p t j -> p (t j)")
-            )
-            nc.sync.dma_start(out_words[:, cols], y_codes[:].bitcast(I32))
+            nc.vector.tensor_copy(*weave_views(ya_bf01[:, i * Q : (i + 1) * Q, :], ya[:, :, i * Q : (i + 1) * Q]))
+        nc.vector.tensor_copy(*weave_views(ya_bf2[:], ya[:, :, 2 * Q : TA]))
+        ya_codes = sbuf("ya_codes", [P, TA], U32)
+        quantise(ya_codes[:, 0 : 2 * Q], y_plane[:, 0 : 2 * Q], ya_bf01[:], E4M3X4)
+        quantise(ya_codes[:, 2 * Q : TA], y_plane[:, 2 * Q : TA], ya_bf2[:], E4M3X4)
+        nc.sync.dma_start(out_words[:, 0:TA], ya_codes[:].bitcast(I32))
+
+        yb_bf = sbuf("yb_bf", [P, Q, LANES], BF16)
+        nc.vector.tensor_copy(*weave_views(yb_bf[:], turned[:]))
+        yb_codes = sbuf("yb_codes", [P, Q], U32)
+        quantise(yb_codes[:], y_plane[:, TA:T], yb_bf[:], E4M3X4)
+        nc.sync.dma_start(out_words[:, TA:T], yb_codes[:].bitcast(I32))
         for q in range(QUADRANTS):
-            queue = nc.scalar if q % 2 else nc.sync
+            queue = nc.scalar if q % 2 == 0 else nc.sync
             queue.dma_start(out_scales[4 * q : 4 * q + 4, :], y_plane[32 * q : 32 * q + 4, :].bitcast(I32))

@@ -41,12 +41,13 @@ def tile_attend_gvq_pl_r_x_kernel(
 
         code = keep.tile([P, T // PER_COLUMN], U16, name="code")
         code2 = keep.tile([P, T // PER_COLUMN], U16, name="code2")
-        book = [sbuf(f"book{j}", [P, C if j == 0 else 2 * TA], F32) for j in range(LANES)]
+        book = [sbuf(f"book{j}", [P, C], F32) for j in range(LANES)]
         book2 = [sbuf(f"book2_{j}", [P, C], F32) for j in range(LANES)]
         z0a = sbuf("z0a", [P, Q], F32)
-        z0b = sbuf("z0b", [P, TA - Q], F32)
-        za = {j: sbuf(f"za{j}", [P, TA], F32) for j in (1, 2, 3)}
-        zb = sbuf("zb", [P, LANES, Q], F32)
+        z0b = sbuf("z0b", [P, T - Q], F32)
+        z1 = sbuf("z1", [P, T], F32)
+        z_half = {j: sbuf(f"z_half{j}", [P, 2 * Q], F32) for j in (2, 3)}
+        z_late = {i: sbuf(f"z_late{i}", [P, 2, Q], F32) for i in (2, 3)}
         w_raw = sbuf("w_raw", [P, 2 * D], U8)
         w_plane_raw = sbuf("w_plane_raw", [P, D], U8)
         ident = sbuf("ident", [P, P], F32)
@@ -63,28 +64,32 @@ def tile_attend_gvq_pl_r_x_kernel(
         nc.vector.memset(w_plane_raw[:].bitcast(I32), 0)
         nc.vector.memset(ga_codes[:, TA:T], 0)
         nc.vector.memset(ga_plane[:, TA:T].bitcast(I32), 0)
-        for j in (1, 2, 3):
-            nc.vector.memset(book[j][:, C:], 0.0)
-        for q in range(QUADRANTS):
-            nc.gpsimd.dma_start(
+        make_identity(nc, ident[:])
+
+        def load_scale_rows(q):
+            nc.sync.dma_start(
                 w_plane_raw[32 * q : 32 * q + 4, :].bitcast(I32), w_scales[0, 4 * q : 4 * q + 4, :].bitcast(I32)
             )
-        make_identity(nc, ident[:])
 
         nc.sync.dma_start(book[0][:], cb_rows[:, 0, :])
         nc.sync.dma_start(code[:], offs)
         nc.sync.dma_start(z0a[:], z_rows[:, 0, 0:Q])
-        nc.sync.dma_start(z0b[:], z_rows[:, 0, Q:TA])
+        nc.sync.dma_start(z0b[:], z_rows[:, 0, Q:T])
         nc.sync.dma_start(book2[0][:], cb2_rows[:, 0, :])
         nc.sync.dma_start(code2[:], offs2)
-        for j in (1, 2, 3):
-            nc.sync.dma_start(book[j][:, 0:C], cb_rows[:, j, :])
-            nc.sync.dma_start(za[j][:], z_rows[:, j, 0:TA])
-            if j > 1:
-                nc.sync.dma_start(book2[j - 1][:], cb2_rows[:, j - 1, :])
-        nc.sync.dma_start(book2[3][:], cb2_rows[:, 3, :])
-        nc.sync.dma_start(zb[:], z_rows[:, :, TA:T])
+        nc.sync.dma_start(book[1][:], cb_rows[:, 1, :])
+        nc.sync.dma_start(z1[:], z_rows[:, 1, :])
+        nc.sync.dma_start(book2[1][:], cb2_rows[:, 1, :])
+        for j in (2, 3):
+            nc.sync.dma_start(book[j][:], cb_rows[:, j, :])
+            nc.sync.dma_start(z_half[j][:], z_rows[:, j, 0 : 2 * Q])
+        for j in (2, 3):
+            nc.sync.dma_start(book2[j][:], cb2_rows[:, j, :])
+        nc.sync.dma_start(z_late[2][:], z_rows[:, 2:LANES, 2 * Q : TA])
+        for q in range(QUADRANTS):
+            load_scale_rows(q)
         nc.sync.dma_start(w_raw[:].bitcast(I32), w_words[0].bitcast(I32))
+        nc.sync.dma_start(z_late[3][:], z_rows[:, 2:LANES, TA:T])
 
         def gather1(dst, j, t0, z_cols):
             n = z_cols.shape[1]
@@ -107,54 +112,58 @@ def tile_attend_gvq_pl_r_x_kernel(
         def quantise(codes, plane, src, fmt):
             nc.vector.quantize_mx(out=codes.bitcast(fmt), scales=plane, in_=src.rearrange("p t j -> p (t j)"))
 
-        part = sbuf("part", [P, LANES, TA], F32)
-        neg_a = sbuf("neg_a", [P, LANES, TA], F32)
+        part = {j: sbuf(f"part{j}", [P, T if j < 2 else TA], F32) for j in range(LANES)}
+        neg_e = sbuf("neg_e", [P, LANES, T], F32)
+        H = 2 * Q
 
-        gather1(part[:, 0, 0:Q], 0, 0, z0a[:])
-        gather1(part[:, 0, Q:TA], 0, Q, z0b[:])
-        gather2(neg_a[:, 0, 0:Q], 0, 0, part[:, 0, 0:Q])
-        gather2(neg_a[:, 0, Q:TA], 0, Q, part[:, 0, Q:TA])
-        for j in (1, 2, 3):
-            gather1(part[:, j, :], j, 0, za[j][:])
-            if j > 1:
-                gather2(neg_a[:, j - 1, :], j - 1, 0, part[:, j - 1, :])
+        gather1(part[0][:, 0:Q], 0, 0, z0a[:])
+        gather1(part[0][:, Q:TA], 0, Q, z0b[:, 0:H])
+        gather1(part[0][:, TA:T], 0, TA, z0b[:, H:TA])
+        for t0 in (0, H):
+            gather2(neg_e[:, 0, t0 : t0 + H], 0, t0, part[0][:, t0 : t0 + H])
+        for t0 in (0, H):
+            gather1(part[1][:, t0 : t0 + H], 1, t0, z1[:, t0 : t0 + H])
+        def deal_views(dst, src, j0, n):
+            return (
+                dst.rearrange("p j (h m) -> p h j m", h=2),
+                src.rearrange("p (h m j) -> p h j m", h=2, j=LANES)[:, :, j0 : j0 + n, :],
+            )
 
-        ga_bf01 = sbuf("ga_bf01", [P, 2 * Q, LANES], BF16)
+        for t0 in (0, H):
+            gather2(neg_e[:, 1, t0 : t0 + H], 1, t0, part[1][:, t0 : t0 + H])
+
+        ga_bf01 = sbuf("ga_bf01", [P, H, LANES], BF16)
         ga_bf2 = sbuf("ga_bf2", [P, Q, LANES], BF16)
+        for j in (2, 3):
+            gather1(part[j][:, 0:H], j, 0, z_half[j][:])
+        for j in (2, 3):
+            gather2(neg_e[:, j, 0:H], j, 0, part[j][:, 0:H])
+        for i in range(2):
+            cols = slice(i * Q, (i + 1) * Q)
+            nc.scalar.activation(*weave_views(ga_bf01[:, cols, :], neg_e[:, :, cols]), COPY, scale=-BETA)
+        for j in (2, 3):
+            gather1(part[j][:, H:TA], j, H, z_late[2][:, j - 2, :])
+        for j in (2, 3):
+            gather2(neg_e[:, j, H:TA], j, H, part[j][:, H:TA])
+        nc.scalar.activation(*weave_views(ga_bf2[:], neg_e[:, :, H:TA]), COPY, scale=-BETA)
 
-        def lane3_second(i):
-            gather2(neg_a[:, 3, i * Q : (i + 1) * Q], 3, i * Q, part[:, 3, i * Q : (i + 1) * Q])
-            dst = ga_bf01[:, i * Q : (i + 1) * Q, :] if i < 2 else ga_bf2[:]
-            nc.scalar.activation(*weave_views(dst, neg_a[:, :, i * Q : (i + 1) * Q]), COPY, scale=-BETA)
-
-        for i in range(3):
-            lane3_second(i)
-
-        w_dealt = w_raw[:].bitcast(U16).rearrange("p (m j) -> p j m", j=LANES)
-        plane_dealt = w_plane_raw[:].rearrange("p (m j) -> p j m", j=LANES)
-        part_b01 = sbuf("part_b01", [P, 2, Q], F32)
-        for j in (0, 1):
-            gather1(part_b01[:, j, :], j, TA, zb[:, j, :])
-        w_first = sbuf("w_first", [P, 2, P], U16)
-        nc.vector.tensor_copy(w_first[:], w_dealt[:, 0:2, :])
-        plane_first = sbuf("plane_first", [P, 2, P], U8, "part")
-        nc.vector.tensor_copy(plane_first[:], plane_dealt[:, 0:2, :])
-        quantise(ga_codes[:, 0 : 2 * Q], ga_plane[:, 0 : 2 * Q], ga_bf01[:], E5M2X4)
-        part_b23 = sbuf("part_b23", [P, 2, Q], F32, "ga_bf01")
-        gather1(part_b23[:, 0, :], 2, TA, zb[:, 2, :])
-        quantise(ga_codes[:, 2 * Q : TA], ga_plane[:, 2 * Q : TA], ga_bf2[:], E5M2X4)
-        gather1(part_b23[:, 1, :], 3, TA, zb[:, 3, :])
-        neg_b = sbuf("neg_b", [P, LANES, Q], F32, "ga_bf2")
-        w_rest = sbuf("w_rest", [P, 2, P], U16, "book0")
-        plane_rest = sbuf("plane_rest", [P, 2, P], U8, "book3")
-        gather2(neg_b[:, 0, :], 0, TA, part_b01[:, 0, :])
-        nc.vector.tensor_copy(w_rest[:], w_dealt[:, 2:4, :])
-        nc.vector.tensor_copy(plane_rest[:], plane_dealt[:, 2:4, :])
-        gather2(neg_b[:, 1, :], 1, TA, part_b01[:, 1, :])
-        gather2(neg_b[:, 2, :], 2, TA, part_b23[:, 0, :])
-        gather2(neg_b[:, 3, :], 3, TA, part_b23[:, 1, :])
+        quantise(ga_codes[:, 0:H], ga_plane[:, 0:H], ga_bf01[:], E5M2X4)
+        plane_first = sbuf("plane_first", [P, 3, P], U8)
+        nc.vector.tensor_copy(*deal_views(plane_first[:], w_plane_raw[:], 0, 3))
+        w_first = sbuf("w_first", [P, 3, P], U16)
+        nc.vector.tensor_copy(*deal_views(w_first[:], w_raw[:].bitcast(U16), 0, 3))
+        quantise(ga_codes[:, H:TA], ga_plane[:, H:TA], ga_bf2[:], E5M2X4)
+        part_b = {j: sbuf(f"part_b{j}", [P, Q], F32) for j in (2, 3)}
+        for j in (2, 3):
+            gather1(part_b[j][:], j, TA, z_late[3][:, j - 2, :])
+        for j in (2, 3):
+            gather2(neg_e[:, j, TA:T], j, TA, part_b[j][:])
+        w_rest = sbuf("w_rest", [P, 1, P], U16, "book2_2")
+        nc.vector.tensor_copy(*deal_views(w_rest[:], w_raw[:].bitcast(U16), 3, 1))
+        plane_rest = sbuf("plane_rest", [P, 1, P], U8, "part_b2")
+        nc.vector.tensor_copy(*deal_views(plane_rest[:], w_plane_raw[:], 3, 1))
         gb_bf = sbuf("gb_bf", [P, Q, LANES], BF16)
-        nc.vector.tensor_scalar(*weave_views(gb_bf[:], neg_b[:]), -BETA, None, ALU.mult)
+        nc.vector.tensor_scalar(*weave_views(gb_bf[:], neg_e[:, :, TA:T]), -BETA, None, ALU.mult)
         gb_codes = sbuf("gb_codes", [P, Q], U32)
         gb_plane = sbuf("gb_plane", [P, Q], U8)
         quantise(gb_codes[:], gb_plane[:], gb_bf[:], E5M2X4)
@@ -164,8 +173,8 @@ def tile_attend_gvq_pl_r_x_kernel(
             acc = psum.tile([P, T], F32, name=f"acc{j}")
             nc.tensor.matmul_mx(
                 out=acc[:],
-                lhsT=(w_first if j < 2 else w_rest)[:, j % 2, :].bitcast(U8).bitcast(E2M1X4),
-                lhsT_scale=(plane_first if j < 2 else plane_rest)[:, j % 2, :],
+                lhsT=(w_first if j < 3 else w_rest)[:, j % 3, :].bitcast(U8).bitcast(E2M1X4),
+                lhsT_scale=(plane_first if j < 3 else plane_rest)[:, j % 3, :],
                 rhs=ga_codes[:].bitcast(E5M2X4),
                 rhs_scale=ga_plane[:],
                 start=True,

@@ -45,9 +45,9 @@ def tile_attend_gvq_pl_r_x_kernel(
         book2 = [sbuf(f"book2_{j}", [P, C], F32) for j in range(LANES)]
         z0a = sbuf("z0a", [P, Q], F32)
         z0b = sbuf("z0b", [P, T - Q], F32)
-        z1 = sbuf("z1", [P, T], F32)
+        z1 = sbuf("z1", [P, TA], F32)
         z_half = {j: sbuf(f"z_half{j}", [P, 2 * Q], F32) for j in (2, 3)}
-        z_late = {i: sbuf(f"z_late{i}", [P, 2, Q], F32) for i in (2, 3)}
+        z_late = {i: sbuf(f"z_late{i}", [P, i, Q], F32) for i in (2, 3)}
         w_raw = sbuf("w_raw", [P, 2 * D], U8)
         w_plane_raw = sbuf("w_plane_raw", [P, D], U8)
         ident = sbuf("ident", [P, P], F32)
@@ -78,7 +78,7 @@ def tile_attend_gvq_pl_r_x_kernel(
         nc.sync.dma_start(book2[0][:], cb2_rows[:, 0, :])
         nc.sync.dma_start(code2[:], offs2)
         nc.sync.dma_start(book[1][:], cb_rows[:, 1, :])
-        nc.sync.dma_start(z1[:], z_rows[:, 1, :])
+        nc.sync.dma_start(z1[:], z_rows[:, 1, 0:TA])
         nc.sync.dma_start(book2[1][:], cb2_rows[:, 1, :])
         for j in (2, 3):
             nc.sync.dma_start(book[j][:], cb_rows[:, j, :])
@@ -89,7 +89,7 @@ def tile_attend_gvq_pl_r_x_kernel(
         for q in range(QUADRANTS):
             load_scale_rows(q)
         nc.sync.dma_start(w_raw[:].bitcast(I32), w_words[0].bitcast(I32))
-        nc.sync.dma_start(z_late[3][:], z_rows[:, 2:LANES, TA:T])
+        nc.sync.dma_start(z_late[3][:], z_rows[:, 1:LANES, TA:T])
 
         def gather1(dst, j, t0, z_cols):
             n = z_cols.shape[1]
@@ -112,7 +112,7 @@ def tile_attend_gvq_pl_r_x_kernel(
         def quantise(codes, plane, src, fmt):
             nc.vector.quantize_mx(out=codes.bitcast(fmt), scales=plane, in_=src.rearrange("p t j -> p (t j)"))
 
-        part = {j: sbuf(f"part{j}", [P, T if j < 2 else TA], F32) for j in range(LANES)}
+        part = {j: sbuf(f"part{j}", [P, T if j == 0 else TA], F32) for j in range(LANES)}
         neg_e = sbuf("neg_e", [P, LANES, T], F32)
         H = 2 * Q
 
@@ -121,16 +121,17 @@ def tile_attend_gvq_pl_r_x_kernel(
         gather1(part[0][:, TA:T], 0, TA, z0b[:, H:TA])
         for t0 in (0, H):
             gather2(neg_e[:, 0, t0 : t0 + H], 0, t0, part[0][:, t0 : t0 + H])
-        for t0 in (0, H):
-            gather1(part[1][:, t0 : t0 + H], 1, t0, z1[:, t0 : t0 + H])
+        HA = TA // 2
+        for t0 in (0, HA):
+            gather1(part[1][:, t0 : t0 + HA], 1, t0, z1[:, t0 : t0 + HA])
         def deal_views(dst, src, j0, n):
             return (
                 dst.rearrange("p j (h m) -> p h j m", h=2),
                 src.rearrange("p (h m j) -> p h j m", h=2, j=LANES)[:, :, j0 : j0 + n, :],
             )
 
-        for t0 in (0, H):
-            gather2(neg_e[:, 1, t0 : t0 + H], 1, t0, part[1][:, t0 : t0 + H])
+        for t0 in (0, HA):
+            gather2(neg_e[:, 1, t0 : t0 + HA], 1, t0, part[1][:, t0 : t0 + HA])
 
         ga_bf01 = sbuf("ga_bf01", [P, H, LANES], BF16)
         ga_bf2 = sbuf("ga_bf2", [P, Q, LANES], BF16)
@@ -153,10 +154,10 @@ def tile_attend_gvq_pl_r_x_kernel(
         w_first = sbuf("w_first", [P, 3, P], U16)
         nc.vector.tensor_copy(*deal_views(w_first[:], w_raw[:].bitcast(U16), 0, 3))
         quantise(ga_codes[:, H:TA], ga_plane[:, H:TA], ga_bf2[:], E5M2X4)
-        part_b = {j: sbuf(f"part_b{j}", [P, Q], F32) for j in (2, 3)}
-        for j in (2, 3):
-            gather1(part_b[j][:], j, TA, z_late[3][:, j - 2, :])
-        for j in (2, 3):
+        part_b = {j: sbuf(f"part_b{j}", [P, Q], F32) for j in (1, 2, 3)}
+        for j in (1, 2, 3):
+            gather1(part_b[j][:], j, TA, z_late[3][:, j - 1, :])
+        for j in (1, 2, 3):
             gather2(neg_e[:, j, TA:T], j, TA, part_b[j][:])
         w_rest = sbuf("w_rest", [P, 1, P], U16, "book2_2")
         nc.vector.tensor_copy(*deal_views(w_rest[:], w_raw[:].bitcast(U16), 3, 1))
@@ -200,13 +201,13 @@ def tile_attend_gvq_pl_r_x_kernel(
         acc_dealt = acc_b[:].rearrange("t (m j) -> t j m", j=LANES)
         turned = psum.tile([P, LANES, Q], F32, name="turned")
         turned_pair = [psum.tile([P, 2, Q], F32, name=f"turned_pair{u}") for u in range(2)]
-        for u in range(2):
-            yb_t = sbuf(f"yb_t{u}", [P, 2, P], F32)
-            nc.scalar.copy(yb_t[:], acc_dealt[:, 2 * u : 2 * u + 2, :])
-            for e in range(2):
-                nc.tensor.transpose(turned[:, 2 * u + e, :], yb_t[:, e, :], ident[:])
-            for e in range(2):
-                nc.tensor.transpose(turned_pair[u][:, e, :], yb_t[:, e, :], ident[:])
+        for j0, j1 in ((0, 1), (1, 2), (2, 3), (3, 4)):
+            yb_t = sbuf(f"yb_t{j0}", [P, j1 - j0, P], F32)
+            nc.scalar.copy(yb_t[:], acc_dealt[:, j0:j1, :])
+            for j in range(j0, j1):
+                nc.tensor.transpose(turned[:, j, :], yb_t[:, j - j0, :], ident[:])
+            for j in range(j0, j1):
+                nc.tensor.transpose(turned_pair[j // 2][:, j % 2, :], yb_t[:, j - j0, :], ident[:])
         for u in range(2):
             yb = sbuf(f"yb{u}", [P, 2, Q], F32)
             nc.scalar.copy(yb[:], turned_pair[u][:])
@@ -217,17 +218,16 @@ def tile_attend_gvq_pl_r_x_kernel(
         ya_bf2 = sbuf("ya_bf2", [P, Q, LANES], BF16)
         for i in range(2):
             nc.vector.tensor_copy(*weave_views(ya_bf01[:, i * Q : (i + 1) * Q, :], ya[:, :, i * Q : (i + 1) * Q]))
-        nc.vector.tensor_copy(*weave_views(ya_bf2[:], ya[:, :, 2 * Q : TA]))
-        ya_codes = sbuf("ya_codes", [P, TA], U32)
-        quantise(ya_codes[:, 0 : 2 * Q], y_plane[:, 0 : 2 * Q], ya_bf01[:], E4M3X4)
-        quantise(ya_codes[:, 2 * Q : TA], y_plane[:, 2 * Q : TA], ya_bf2[:], E4M3X4)
-        nc.sync.dma_start(out_words[:, 0:TA], ya_codes[:].bitcast(I32))
+        y_codes = [sbuf(f"y_codes{h}", [P, H], U32) for h in range(2)]
+        quantise(y_codes[0][:], y_plane[:, 0:H], ya_bf01[:], E4M3X4)
+        nc.sync.dma_start(out_words[:, 0:H], y_codes[0][:].bitcast(I32))
+        nc.vector.tensor_copy(*weave_views(ya_bf2[:], ya[:, :, H:TA]))
+        quantise(y_codes[1][:, 0:Q], y_plane[:, H:TA], ya_bf2[:], E4M3X4)
 
         yb_bf = sbuf("yb_bf", [P, Q, LANES], BF16)
         nc.vector.tensor_copy(*weave_views(yb_bf[:], turned[:]))
-        yb_codes = sbuf("yb_codes", [P, Q], U32)
-        quantise(yb_codes[:], y_plane[:, TA:T], yb_bf[:], E4M3X4)
-        nc.sync.dma_start(out_words[:, TA:T], yb_codes[:].bitcast(I32))
+        quantise(y_codes[1][:, Q:H], y_plane[:, TA:T], yb_bf[:], E4M3X4)
+        nc.sync.dma_start(out_words[:, H:T], y_codes[1][:].bitcast(I32))
         for q in range(QUADRANTS):
             queue = nc.scalar if q % 2 == 0 else nc.sync
             queue.dma_start(out_scales[4 * q : 4 * q + 4, :], y_plane[32 * q : 32 * q + 4, :].bitcast(I32))

@@ -26,6 +26,7 @@ PER_COLUMN = 16
 Q = 128
 TA = 3 * Q
 RUN = 4
+Z0 = 192
 
 
 def tile_attend_gvq_pl_r_x_kernel(
@@ -43,8 +44,8 @@ def tile_attend_gvq_pl_r_x_kernel(
         code2 = keep.tile([P, T // PER_COLUMN], U16, name="code2")
         book = [sbuf(f"book{j}", [P, C], F32) for j in range(LANES)]
         book2 = [sbuf(f"book2_{j}", [P, C], F32) for j in range(LANES)]
-        z0a = sbuf("z0a", [P, Q], F32)
-        z0b = sbuf("z0b", [P, T - Q], F32)
+        z0a = sbuf("z0a", [P, Z0], F32)
+        z0b = sbuf("z0b", [P, T - Z0], F32)
         z1 = sbuf("z1", [P, TA], F32)
         z_half = {j: sbuf(f"z_half{j}", [P, 2 * Q], F32) for j in (2, 3)}
         z_late = {i: sbuf(f"z_late{i}", [P, i, Q], F32) for i in (2, 3)}
@@ -73,8 +74,8 @@ def tile_attend_gvq_pl_r_x_kernel(
 
         nc.sync.dma_start(book[0][:], cb_rows[:, 0, :])
         nc.sync.dma_start(code[:], offs)
-        nc.sync.dma_start(z0a[:], z_rows[:, 0, 0:Q])
-        nc.sync.dma_start(z0b[:], z_rows[:, 0, Q:T])
+        nc.sync.dma_start(z0a[:], z_rows[:, 0, 0:Z0])
+        nc.sync.dma_start(z0b[:], z_rows[:, 0, Z0:T])
         nc.sync.dma_start(book2[0][:], cb2_rows[:, 0, :])
         nc.sync.dma_start(code2[:], offs2)
         nc.sync.dma_start(book[1][:], cb_rows[:, 1, :])
@@ -88,8 +89,8 @@ def tile_attend_gvq_pl_r_x_kernel(
         nc.sync.dma_start(z_late[2][:], z_rows[:, 2:LANES, 2 * Q : TA])
         for q in range(QUADRANTS):
             load_scale_rows(q)
-        nc.sync.dma_start(w_raw[:].bitcast(I32), w_words[0].bitcast(I32))
         nc.sync.dma_start(z_late[3][:], z_rows[:, 1:LANES, TA:T])
+        nc.sync.dma_start(w_raw[:].bitcast(I32), w_words[0].bitcast(I32))
 
         def gather1(dst, j, t0, z_cols):
             n = z_cols.shape[1]
@@ -116,9 +117,10 @@ def tile_attend_gvq_pl_r_x_kernel(
         neg_e = sbuf("neg_e", [P, LANES, T], F32)
         H = 2 * Q
 
-        gather1(part[0][:, 0:Q], 0, 0, z0a[:])
-        gather1(part[0][:, Q:TA], 0, Q, z0b[:, 0:H])
-        gather1(part[0][:, TA:T], 0, TA, z0b[:, H:TA])
+        gather1(part[0][:, 0:Z0], 0, 0, z0a[:])
+        mid = (Z0 + T) // 2
+        gather1(part[0][:, Z0:mid], 0, Z0, z0b[:, 0 : mid - Z0])
+        gather1(part[0][:, mid:T], 0, mid, z0b[:, mid - Z0 : T - Z0])
         for t0 in (0, H):
             gather2(neg_e[:, 0, t0 : t0 + H], 0, t0, part[0][:, t0 : t0 + H])
         HA = TA // 2
@@ -149,22 +151,25 @@ def tile_attend_gvq_pl_r_x_kernel(
         nc.scalar.activation(*weave_views(ga_bf2[:], neg_e[:, :, H:TA]), COPY, scale=-BETA)
 
         quantise(ga_codes[:, 0:H], ga_plane[:, 0:H], ga_bf01[:], E5M2X4)
-        plane_first = sbuf("plane_first", [P, 3, P], U8)
-        nc.vector.tensor_copy(*deal_views(plane_first[:], w_plane_raw[:], 0, 3))
-        w_first = sbuf("w_first", [P, 3, P], U16)
-        nc.vector.tensor_copy(*deal_views(w_first[:], w_raw[:].bitcast(U16), 0, 3))
+        plane_dealt = sbuf("plane_dealt", [P, LANES, P], U8)
+        nc.vector.tensor_copy(*deal_views(plane_dealt[:], w_plane_raw[:], 0, LANES))
+        w_first = sbuf("w_first", [P, 1, P], U16)
+        nc.scalar.copy(*deal_views(w_first[:], w_raw[:].bitcast(U16), 0, 1))
+        w_rest = sbuf("w_rest", [P, 3, P], U16)
+        nc.scalar.copy(*deal_views(w_rest[:], w_raw[:].bitcast(U16), 1, 3))
         quantise(ga_codes[:, H:TA], ga_plane[:, H:TA], ga_bf2[:], E5M2X4)
-        part_b = {j: sbuf(f"part_b{j}", [P, Q], F32) for j in (1, 2, 3)}
-        for j in (1, 2, 3):
-            gather1(part_b[j][:], j, TA, z_late[3][:, j - 1, :])
-        for j in (1, 2, 3):
-            gather2(neg_e[:, j, TA:T], j, TA, part_b[j][:])
-        w_rest = sbuf("w_rest", [P, 1, P], U16, "book2_2")
-        nc.vector.tensor_copy(*deal_views(w_rest[:], w_raw[:].bitcast(U16), 3, 1))
-        plane_rest = sbuf("plane_rest", [P, 1, P], U8, "part_b2")
-        nc.vector.tensor_copy(*deal_views(plane_rest[:], w_plane_raw[:], 3, 1))
-        gb_bf = sbuf("gb_bf", [P, Q, LANES], BF16)
-        nc.vector.tensor_scalar(*weave_views(gb_bf[:], neg_e[:, :, TA:T]), -BETA, None, ALU.mult)
+        part_b1 = sbuf("part_b1", [P, Q], F32)
+        part_b23 = sbuf("part_b23", [P, 2, Q], F32, "ga_bf2")
+        gather1(part_b1[:], 1, TA, z_late[3][:, 0, :])
+        gather2(neg_e[:, 1, TA:T], 1, TA, part_b1[:])
+        for j in (2, 3):
+            gather1(part_b23[:, j - 2, :], j, TA, z_late[3][:, j - 1, :])
+        for j in (2, 3):
+            gather2(neg_e[:, j, TA:T], j, TA, part_b23[:, j - 2, :])
+        gb_bf = sbuf("gb_bf", [P, Q, LANES], BF16, "book2_2")
+        for u in range(2):
+            pair = slice(2 * u, 2 * u + 2)
+            nc.vector.tensor_scalar(*weave_views(gb_bf[:, :, pair], neg_e[:, pair, TA:T]), -BETA, None, ALU.mult)
         gb_codes = sbuf("gb_codes", [P, Q], U32)
         gb_plane = sbuf("gb_plane", [P, Q], U8)
         quantise(gb_codes[:], gb_plane[:], gb_bf[:], E5M2X4)
@@ -174,8 +179,8 @@ def tile_attend_gvq_pl_r_x_kernel(
             acc = psum.tile([P, T], F32, name=f"acc{j}")
             nc.tensor.matmul_mx(
                 out=acc[:],
-                lhsT=(w_first if j < 3 else w_rest)[:, j % 3, :].bitcast(U8).bitcast(E2M1X4),
-                lhsT_scale=(plane_first if j < 3 else plane_rest)[:, j % 3, :],
+                lhsT=(w_first[:, 0, :] if j == 0 else w_rest[:, j - 1, :]).bitcast(U8).bitcast(E2M1X4),
+                lhsT_scale=plane_dealt[:, j, :],
                 rhs=ga_codes[:].bitcast(E5M2X4),
                 rhs_scale=ga_plane[:],
                 start=True,
@@ -184,8 +189,8 @@ def tile_attend_gvq_pl_r_x_kernel(
             if j < LANES - 1:
                 nc.scalar.copy(ya[:, j, :], acc[:, 0:TA])
             else:
-                for i in range(3):
-                    nc.scalar.copy(ya[:, j, i * Q : (i + 1) * Q], acc[:, i * Q : (i + 1) * Q])
+                for t0, t1 in ((0, Q), (Q, TA)):
+                    nc.scalar.copy(ya[:, j, t0:t1], acc[:, t0:t1])
             nc.sync.dma_start(out_rows[:, j, 0:TA], ya[:, j, :])
 
         acc_b = psum.tile([P, D], F32, name="acc_b")

@@ -189,7 +189,7 @@ def tile_attend_gvq_pl_r_x_kernel(
             if j < LANES - 1:
                 nc.scalar.copy(ya[:, j, :], acc[:, 0:TA])
             else:
-                for t0, t1 in ((0, Q), (Q, TA)):
+                for t0, t1 in ((0, Q), (Q, H), (H, TA)):
                     nc.scalar.copy(ya[:, j, t0:t1], acc[:, t0:t1])
             nc.sync.dma_start(out_rows[:, j, 0:TA], ya[:, j, :])
 
@@ -219,15 +219,15 @@ def tile_attend_gvq_pl_r_x_kernel(
             nc.sync.dma_start(out_rows[:, 2 * u : 2 * u + 2, TA:T], yb[:])
 
         y_plane = sbuf("y_plane", [P, T], U8)
-        ya_bf01 = sbuf("ya_bf01", [P, 2 * Q, LANES], BF16)
-        ya_bf2 = sbuf("ya_bf2", [P, Q, LANES], BF16)
-        for i in range(2):
-            nc.vector.tensor_copy(*weave_views(ya_bf01[:, i * Q : (i + 1) * Q, :], ya[:, :, i * Q : (i + 1) * Q]))
+        ya_bf = sbuf("ya_bf", [P, TA, LANES], BF16, "neg_e")
+        nc.vector.tensor_copy(*weave_views(ya_bf[:, :, 0:2], ya[:, 0:2, :]))
+        for i in range(3):
+            cols = slice(i * Q, (i + 1) * Q)
+            nc.vector.tensor_copy(*weave_views(ya_bf[:, cols, 2:4], ya[:, 2:4, cols]))
         y_codes = [sbuf(f"y_codes{h}", [P, H], U32) for h in range(2)]
-        quantise(y_codes[0][:], y_plane[:, 0:H], ya_bf01[:], E4M3X4)
+        quantise(y_codes[0][:], y_plane[:, 0:H], ya_bf[:, 0:H, :], E4M3X4)
         nc.sync.dma_start(out_words[:, 0:H], y_codes[0][:].bitcast(I32))
-        nc.vector.tensor_copy(*weave_views(ya_bf2[:], ya[:, :, H:TA]))
-        quantise(y_codes[1][:, 0:Q], y_plane[:, H:TA], ya_bf2[:], E4M3X4)
+        quantise(y_codes[1][:, 0:Q], y_plane[:, H:TA], ya_bf[:, H:TA, :], E4M3X4)
 
         yb_bf = sbuf("yb_bf", [P, Q, LANES], BF16)
         nc.vector.tensor_copy(*weave_views(yb_bf[:], turned[:]))

@@ -79,16 +79,19 @@ def tile_attend_gvq_pl_r_x_kernel(
         nc.sync.dma_start(book2[0][:], cb2_rows[:, 0, :])
         nc.sync.dma_start(code2[:], offs2)
         nc.sync.dma_start(book[1][:], cb_rows[:, 1, :])
+        load_scale_rows(0)
         nc.sync.dma_start(z1[:], z_rows[:, 1, 0:TA])
+        load_scale_rows(1)
         nc.sync.dma_start(book2[1][:], cb2_rows[:, 1, :])
+        load_scale_rows(2)
         for j in (2, 3):
             nc.sync.dma_start(book[j][:], cb_rows[:, j, :])
+            if j == 2:
+                load_scale_rows(3)
             nc.sync.dma_start(z_half[j][:], z_rows[:, j, 0 : 2 * Q])
         for j in (2, 3):
             nc.sync.dma_start(book2[j][:], cb2_rows[:, j, :])
         nc.sync.dma_start(z_late[2][:], z_rows[:, 2:LANES, 2 * Q : TA])
-        for q in range(QUADRANTS):
-            load_scale_rows(q)
         nc.sync.dma_start(z_late[3][:], z_rows[:, 1:LANES, TA:T])
         nc.sync.dma_start(w_raw[:].bitcast(I32), w_words[0].bitcast(I32))
 
@@ -114,62 +117,64 @@ def tile_attend_gvq_pl_r_x_kernel(
             nc.vector.quantize_mx(out=codes.bitcast(fmt), scales=plane, in_=src.rearrange("p t j -> p (t j)"))
 
         part = {j: sbuf(f"part{j}", [P, T if j == 0 else TA], F32) for j in range(LANES)}
-        neg_e = sbuf("neg_e", [P, LANES, T], F32)
+        neg_a = sbuf("neg_a", [P, LANES, TA], F32)
+        neg_b01 = sbuf("neg_b01", [P, 2, Q], F32)
         H = 2 * Q
 
-        gather1(part[0][:, 0:Z0], 0, 0, z0a[:])
-        mid = (Z0 + T) // 2
-        gather1(part[0][:, Z0:mid], 0, Z0, z0b[:, 0 : mid - Z0])
-        gather1(part[0][:, mid:T], 0, mid, z0b[:, mid - Z0 : T - Z0])
-        for t0 in (0, H):
-            gather2(neg_e[:, 0, t0 : t0 + H], 0, t0, part[0][:, t0 : t0 + H])
-        HA = TA // 2
-        for t0 in (0, HA):
-            gather1(part[1][:, t0 : t0 + HA], 1, t0, z1[:, t0 : t0 + HA])
         def deal_views(dst, src, j0, n):
             return (
                 dst.rearrange("p j (h m) -> p h j m", h=2),
                 src.rearrange("p (h m j) -> p h j m", h=2, j=LANES)[:, :, j0 : j0 + n, :],
             )
 
+        gather1(part[0][:, 0:Z0], 0, 0, z0a[:])
+        mid = (Z0 + T) // 2
+        gather1(part[0][:, Z0:mid], 0, Z0, z0b[:, 0 : mid - Z0])
+        gather1(part[0][:, mid:T], 0, mid, z0b[:, mid - Z0 : T - Z0])
+        HA = TA // 2
         for t0 in (0, HA):
-            gather2(neg_e[:, 1, t0 : t0 + HA], 1, t0, part[1][:, t0 : t0 + HA])
+            gather2(neg_a[:, 0, t0 : t0 + HA], 0, t0, part[0][:, t0 : t0 + HA])
+        gather2(neg_b01[:, 0, :], 0, TA, part[0][:, TA:T])
+        for t0 in (0, HA):
+            gather1(part[1][:, t0 : t0 + HA], 1, t0, z1[:, t0 : t0 + HA])
+        for t0 in (0, HA):
+            gather2(neg_a[:, 1, t0 : t0 + HA], 1, t0, part[1][:, t0 : t0 + HA])
 
+        plane_dealt = sbuf("plane_dealt", [P, LANES, P], U8)
+        nc.vector.tensor_copy(*deal_views(plane_dealt[:], w_plane_raw[:], 0, LANES))
         ga_bf01 = sbuf("ga_bf01", [P, H, LANES], BF16)
         ga_bf2 = sbuf("ga_bf2", [P, Q, LANES], BF16)
         for j in (2, 3):
             gather1(part[j][:, 0:H], j, 0, z_half[j][:])
         for j in (2, 3):
-            gather2(neg_e[:, j, 0:H], j, 0, part[j][:, 0:H])
+            gather2(neg_a[:, j, 0:H], j, 0, part[j][:, 0:H])
         for i in range(2):
             cols = slice(i * Q, (i + 1) * Q)
-            nc.scalar.activation(*weave_views(ga_bf01[:, cols, :], neg_e[:, :, cols]), COPY, scale=-BETA)
+            nc.scalar.activation(*weave_views(ga_bf01[:, cols, :], neg_a[:, :, cols]), COPY, scale=-BETA)
         for j in (2, 3):
             gather1(part[j][:, H:TA], j, H, z_late[2][:, j - 2, :])
         for j in (2, 3):
-            gather2(neg_e[:, j, H:TA], j, H, part[j][:, H:TA])
-        nc.scalar.activation(*weave_views(ga_bf2[:], neg_e[:, :, H:TA]), COPY, scale=-BETA)
+            gather2(neg_a[:, j, H:TA], j, H, part[j][:, H:TA])
+        nc.scalar.activation(*weave_views(ga_bf2[:], neg_a[:, :, H:TA]), COPY, scale=-BETA)
 
         quantise(ga_codes[:, 0:H], ga_plane[:, 0:H], ga_bf01[:], E5M2X4)
-        plane_dealt = sbuf("plane_dealt", [P, LANES, P], U8)
-        nc.vector.tensor_copy(*deal_views(plane_dealt[:], w_plane_raw[:], 0, LANES))
         w_first = sbuf("w_first", [P, 1, P], U16)
         nc.scalar.copy(*deal_views(w_first[:], w_raw[:].bitcast(U16), 0, 1))
         w_rest = sbuf("w_rest", [P, 3, P], U16)
         nc.scalar.copy(*deal_views(w_rest[:], w_raw[:].bitcast(U16), 1, 3))
         quantise(ga_codes[:, H:TA], ga_plane[:, H:TA], ga_bf2[:], E5M2X4)
-        part_b1 = sbuf("part_b1", [P, Q], F32)
-        part_b23 = sbuf("part_b23", [P, 2, Q], F32, "ga_bf2")
-        gather1(part_b1[:], 1, TA, z_late[3][:, 0, :])
-        gather2(neg_e[:, 1, TA:T], 1, TA, part_b1[:])
+        part_b23 = sbuf("part_b23", [P, 2, Q], F32)
         for j in (2, 3):
             gather1(part_b23[:, j - 2, :], j, TA, z_late[3][:, j - 1, :])
+        part_b1 = sbuf("part_b1", [P, Q], F32, "neg_a")
+        neg_b23 = sbuf("neg_b23", [P, 2, Q], F32, "ga_bf2")
+        gather1(part_b1[:], 1, TA, z_late[3][:, 0, :])
         for j in (2, 3):
-            gather2(neg_e[:, j, TA:T], j, TA, part_b23[:, j - 2, :])
-        gb_bf = sbuf("gb_bf", [P, Q, LANES], BF16, "book2_2")
-        for u in range(2):
-            pair = slice(2 * u, 2 * u + 2)
-            nc.vector.tensor_scalar(*weave_views(gb_bf[:, :, pair], neg_e[:, pair, TA:T]), -BETA, None, ALU.mult)
+            gather2(neg_b23[:, j - 2, :], j, TA, part_b23[:, j - 2, :])
+        gather2(neg_b01[:, 1, :], 1, TA, part_b1[:])
+        gb_bf = sbuf("gb_bf", [P, Q, LANES], BF16)
+        nc.vector.tensor_scalar(*weave_views(gb_bf[:, :, 2:4], neg_b23[:]), -BETA, None, ALU.mult)
+        nc.vector.tensor_scalar(*weave_views(gb_bf[:, :, 0:2], neg_b01[:]), -BETA, None, ALU.mult)
         gb_codes = sbuf("gb_codes", [P, Q], U32)
         gb_plane = sbuf("gb_plane", [P, Q], U8)
         quantise(gb_codes[:], gb_plane[:], gb_bf[:], E5M2X4)
@@ -219,18 +224,18 @@ def tile_attend_gvq_pl_r_x_kernel(
             nc.sync.dma_start(out_rows[:, 2 * u : 2 * u + 2, TA:T], yb[:])
 
         y_plane = sbuf("y_plane", [P, T], U8)
-        ya_bf = sbuf("ya_bf", [P, TA, LANES], BF16, "neg_e")
+        ya_bf = sbuf("ya_bf", [P, TA, LANES], BF16, "neg_b01")
         nc.vector.tensor_copy(*weave_views(ya_bf[:, :, 0:2], ya[:, 0:2, :]))
         for i in range(3):
             cols = slice(i * Q, (i + 1) * Q)
             nc.vector.tensor_copy(*weave_views(ya_bf[:, cols, 2:4], ya[:, 2:4, cols]))
-        y_codes = [sbuf(f"y_codes{h}", [P, H], U32) for h in range(2)]
+        y_codes = [sbuf("y_codes0", [P, H], U32), sbuf("y_codes1", [P, H], U32, "yb_t3")]
         quantise(y_codes[0][:], y_plane[:, 0:H], ya_bf[:, 0:H, :], E4M3X4)
         nc.sync.dma_start(out_words[:, 0:H], y_codes[0][:].bitcast(I32))
-        quantise(y_codes[1][:, 0:Q], y_plane[:, H:TA], ya_bf[:, H:TA, :], E4M3X4)
 
         yb_bf = sbuf("yb_bf", [P, Q, LANES], BF16)
         nc.vector.tensor_copy(*weave_views(yb_bf[:], turned[:]))
+        quantise(y_codes[1][:, 0:Q], y_plane[:, H:TA], ya_bf[:, H:TA, :], E4M3X4)
         quantise(y_codes[1][:, Q:H], y_plane[:, TA:T], yb_bf[:], E4M3X4)
         nc.sync.dma_start(out_words[:, H:T], y_codes[1][:].bitcast(I32))
         for q in range(QUADRANTS):

@@ -63,9 +63,9 @@ def tile_attend_gvq_pl_r_x_kernel(
         out_scales = out_2[0].bitcast(I32)
 
         nc.vector.memset(w_plane_raw[:].bitcast(I32), 0)
-        nc.vector.memset(ga_codes[:, TA:T], 0)
-        nc.vector.memset(ga_plane[:, TA:T].bitcast(I32), 0)
         make_identity(nc, ident[:])
+        nc.gpsimd.memset(ga_codes[:, TA:T], 0)
+        nc.gpsimd.memset(ga_plane[:, TA:T].bitcast(I32), 0)
 
         def load_scale_rows(q):
             nc.sync.dma_start(
@@ -79,21 +79,18 @@ def tile_attend_gvq_pl_r_x_kernel(
         nc.sync.dma_start(book2[0][:], cb2_rows[:, 0, :])
         nc.sync.dma_start(code2[:], offs2)
         nc.sync.dma_start(book[1][:], cb_rows[:, 1, :])
-        load_scale_rows(0)
         nc.sync.dma_start(z1[:], z_rows[:, 1, 0:TA])
-        load_scale_rows(1)
         nc.sync.dma_start(book2[1][:], cb2_rows[:, 1, :])
-        load_scale_rows(2)
         for j in (2, 3):
             nc.sync.dma_start(book[j][:], cb_rows[:, j, :])
-            if j == 2:
-                load_scale_rows(3)
             nc.sync.dma_start(z_half[j][:], z_rows[:, j, 0 : 2 * Q])
         for j in (2, 3):
             nc.sync.dma_start(book2[j][:], cb2_rows[:, j, :])
         nc.sync.dma_start(z_late[2][:], z_rows[:, 2:LANES, 2 * Q : TA])
-        nc.sync.dma_start(z_late[3][:], z_rows[:, 1:LANES, TA:T])
+        for q in range(QUADRANTS):
+            load_scale_rows(q)
         nc.sync.dma_start(w_raw[:].bitcast(I32), w_words[0].bitcast(I32))
+        nc.sync.dma_start(z_late[3][:], z_rows[:, 1:LANES, TA:T])
 
         def gather1(dst, j, t0, z_cols):
             n = z_cols.shape[1]
@@ -117,8 +114,8 @@ def tile_attend_gvq_pl_r_x_kernel(
             nc.vector.quantize_mx(out=codes.bitcast(fmt), scales=plane, in_=src.rearrange("p t j -> p (t j)"))
 
         part = {j: sbuf(f"part{j}", [P, T if j == 0 else TA], F32) for j in range(LANES)}
-        neg_a = sbuf("neg_a", [P, LANES, TA], F32)
-        neg_b01 = sbuf("neg_b01", [P, 2, Q], F32)
+        neg_a = sbuf("neg_a", [P, LANES, 2 * Q], F32)
+        neg_q = sbuf("neg_q", [P, LANES, Q], F32)
         H = 2 * Q
 
         def deal_views(dst, src, j0, n):
@@ -131,53 +128,54 @@ def tile_attend_gvq_pl_r_x_kernel(
         mid = (Z0 + T) // 2
         gather1(part[0][:, Z0:mid], 0, Z0, z0b[:, 0 : mid - Z0])
         gather1(part[0][:, mid:T], 0, mid, z0b[:, mid - Z0 : T - Z0])
-        HA = TA // 2
-        for t0 in (0, HA):
-            gather2(neg_a[:, 0, t0 : t0 + HA], 0, t0, part[0][:, t0 : t0 + HA])
-        gather2(neg_b01[:, 0, :], 0, TA, part[0][:, TA:T])
-        for t0 in (0, HA):
-            gather1(part[1][:, t0 : t0 + HA], 1, t0, z1[:, t0 : t0 + HA])
-        for t0 in (0, HA):
-            gather2(neg_a[:, 1, t0 : t0 + HA], 1, t0, part[1][:, t0 : t0 + HA])
+        gather2(neg_a[:, 0, :], 0, 0, part[0][:, 0:H])
+        gather2(neg_q[:, 0, :], 0, H, part[0][:, H:TA])
+        gather1(part[1][:, 0:H], 1, 0, z1[:, 0:H])
+        gather1(part[1][:, H:TA], 1, H, z1[:, H:TA])
+        gather2(neg_a[:, 1, :], 1, 0, part[1][:, 0:H])
+        gather2(neg_q[:, 1, :], 1, H, part[1][:, H:TA])
 
-        plane_dealt = sbuf("plane_dealt", [P, LANES, P], U8)
-        nc.vector.tensor_copy(*deal_views(plane_dealt[:], w_plane_raw[:], 0, LANES))
         ga_bf01 = sbuf("ga_bf01", [P, H, LANES], BF16)
         ga_bf2 = sbuf("ga_bf2", [P, Q, LANES], BF16)
         for j in (2, 3):
             gather1(part[j][:, 0:H], j, 0, z_half[j][:])
         for j in (2, 3):
-            gather2(neg_a[:, j, 0:H], j, 0, part[j][:, 0:H])
+            gather2(neg_a[:, j, :], j, 0, part[j][:, 0:H])
         for i in range(2):
             cols = slice(i * Q, (i + 1) * Q)
             nc.scalar.activation(*weave_views(ga_bf01[:, cols, :], neg_a[:, :, cols]), COPY, scale=-BETA)
         for j in (2, 3):
             gather1(part[j][:, H:TA], j, H, z_late[2][:, j - 2, :])
         for j in (2, 3):
-            gather2(neg_a[:, j, H:TA], j, H, part[j][:, H:TA])
-        nc.scalar.activation(*weave_views(ga_bf2[:], neg_a[:, :, H:TA]), COPY, scale=-BETA)
+            gather2(neg_q[:, j, :], j, H, part[j][:, H:TA])
+        nc.scalar.activation(*weave_views(ga_bf2[:], neg_q[:]), COPY, scale=-BETA)
 
+        neg_b = sbuf("neg_b", [P, LANES, Q], F32, "part2")
+        gather2(neg_b[:, 0, :], 0, TA, part[0][:, TA:T])
         quantise(ga_codes[:, 0:H], ga_plane[:, 0:H], ga_bf01[:], E5M2X4)
+        plane_dealt = sbuf("plane_dealt", [P, LANES, P], U8, "neg_a")
+        nc.vector.tensor_copy(*deal_views(plane_dealt[:], w_plane_raw[:], 0, LANES))
         w_first = sbuf("w_first", [P, 1, P], U16)
         nc.scalar.copy(*deal_views(w_first[:], w_raw[:].bitcast(U16), 0, 1))
         w_rest = sbuf("w_rest", [P, 3, P], U16)
         nc.scalar.copy(*deal_views(w_rest[:], w_raw[:].bitcast(U16), 1, 3))
         quantise(ga_codes[:, H:TA], ga_plane[:, H:TA], ga_bf2[:], E5M2X4)
-        part_b23 = sbuf("part_b23", [P, 2, Q], F32)
-        for j in (2, 3):
-            gather1(part_b23[:, j - 2, :], j, TA, z_late[3][:, j - 1, :])
-        part_b1 = sbuf("part_b1", [P, Q], F32, "neg_a")
-        neg_b23 = sbuf("neg_b23", [P, 2, Q], F32, "ga_bf2")
-        gather1(part_b1[:], 1, TA, z_late[3][:, 0, :])
-        for j in (2, 3):
-            gather2(neg_b23[:, j - 2, :], j, TA, part_b23[:, j - 2, :])
-        gather2(neg_b01[:, 1, :], 1, TA, part_b1[:])
+        part_b = sbuf("part_b", [P, 3, Q], F32, "neg_q")
+        for j in (1, 2, 3):
+            gather1(part_b[:, j - 1, :], j, TA, z_late[3][:, j - 1, :])
+        for j in (1, 2):
+            gather2(neg_b[:, j, :], j, TA, part_b[:, j - 1, :])
+        E = Q // 2
+        halves = (slice(0, E), slice(E, Q))
+        for cols in halves:
+            gather2(neg_b[:, 3, cols], 3, TA + cols.start, part_b[:, 2, cols])
         gb_bf = sbuf("gb_bf", [P, Q, LANES], BF16)
-        nc.vector.tensor_scalar(*weave_views(gb_bf[:, :, 2:4], neg_b23[:]), -BETA, None, ALU.mult)
-        nc.vector.tensor_scalar(*weave_views(gb_bf[:, :, 0:2], neg_b01[:]), -BETA, None, ALU.mult)
         gb_codes = sbuf("gb_codes", [P, Q], U32)
         gb_plane = sbuf("gb_plane", [P, Q], U8)
-        quantise(gb_codes[:], gb_plane[:], gb_bf[:], E5M2X4)
+        for cols in halves:
+            nc.vector.tensor_scalar(*weave_views(gb_bf[:, cols, :], neg_b[:, :, cols]), -BETA, None, ALU.mult)
+        for cols in halves:
+            quantise(gb_codes[:, cols], gb_plane[:, cols], gb_bf[:, cols, :], E5M2X4)
 
         ya = sbuf("ya", [P, LANES, TA], F32)
         for j in range(LANES):
@@ -194,7 +192,7 @@ def tile_attend_gvq_pl_r_x_kernel(
             if j < LANES - 1:
                 nc.scalar.copy(ya[:, j, :], acc[:, 0:TA])
             else:
-                for t0, t1 in ((0, Q), (Q, H), (H, TA)):
+                for t0, t1 in ((0, H), (H, TA)):
                     nc.scalar.copy(ya[:, j, t0:t1], acc[:, t0:t1])
             nc.sync.dma_start(out_rows[:, j, 0:TA], ya[:, j, :])
 
@@ -211,24 +209,23 @@ def tile_attend_gvq_pl_r_x_kernel(
         acc_dealt = acc_b[:].rearrange("t (m j) -> t j m", j=LANES)
         turned = psum.tile([P, LANES, Q], F32, name="turned")
         turned_pair = [psum.tile([P, 2, Q], F32, name=f"turned_pair{u}") for u in range(2)]
-        for j0, j1 in ((0, 1), (1, 2), (2, 3), (3, 4)):
-            yb_t = sbuf(f"yb_t{j0}", [P, j1 - j0, P], F32)
-            nc.scalar.copy(yb_t[:], acc_dealt[:, j0:j1, :])
-            for j in range(j0, j1):
-                nc.tensor.transpose(turned[:, j, :], yb_t[:, j - j0, :], ident[:])
-            for j in range(j0, j1):
-                nc.tensor.transpose(turned_pair[j // 2][:, j % 2, :], yb_t[:, j - j0, :], ident[:])
+        yb_t = [sbuf(f"yb_t{j}", [P, P], F32) for j in range(LANES)]
+        for j in range(LANES):
+            nc.scalar.copy(yb_t[j][:], acc_dealt[:, j, :])
+            nc.tensor.transpose(turned[:, j, :], yb_t[j][:], ident[:])
+            if j < 2:
+                nc.tensor.transpose(turned_pair[0][:, j, :], yb_t[j][:], ident[:])
+        for j in (2, 3):
+            nc.tensor.transpose(turned_pair[1][:, j - 2, :], yb_t[j][:], ident[:])
         for u in range(2):
             yb = sbuf(f"yb{u}", [P, 2, Q], F32)
             nc.scalar.copy(yb[:], turned_pair[u][:])
             nc.sync.dma_start(out_rows[:, 2 * u : 2 * u + 2, TA:T], yb[:])
 
         y_plane = sbuf("y_plane", [P, T], U8)
-        ya_bf = sbuf("ya_bf", [P, TA, LANES], BF16, "neg_b01")
-        nc.vector.tensor_copy(*weave_views(ya_bf[:, :, 0:2], ya[:, 0:2, :]))
-        for i in range(3):
-            cols = slice(i * Q, (i + 1) * Q)
-            nc.vector.tensor_copy(*weave_views(ya_bf[:, cols, 2:4], ya[:, 2:4, cols]))
+        ya_bf = sbuf("ya_bf", [P, TA, LANES], BF16, "part2")
+        for cols in (slice(0, H), slice(H, TA)):
+            nc.vector.tensor_copy(*weave_views(ya_bf[:, cols, :], ya[:, :, cols]))
         y_codes = [sbuf("y_codes0", [P, H], U32), sbuf("y_codes1", [P, H], U32, "yb_t3")]
         quantise(y_codes[0][:], y_plane[:, 0:H], ya_bf[:, 0:H, :], E4M3X4)
         nc.sync.dma_start(out_words[:, 0:H], y_codes[0][:].bitcast(I32))

@@ -26,7 +26,7 @@ PER_COLUMN = 16
 Q = 128
 TA = 3 * Q
 RUN = 4
-Z0 = 192
+Z0 = 256
 
 
 def tile_attend_gvq_pl_r_x_kernel(
@@ -46,9 +46,9 @@ def tile_attend_gvq_pl_r_x_kernel(
         book2 = [sbuf(f"book2_{j}", [P, C], F32) for j in range(LANES)]
         z0a = sbuf("z0a", [P, Z0], F32)
         z0b = sbuf("z0b", [P, T - Z0], F32)
-        z1 = sbuf("z1", [P, TA], F32)
+        z1 = sbuf("z1", [P, T], F32)
         z_half = {j: sbuf(f"z_half{j}", [P, 2 * Q], F32) for j in (2, 3)}
-        z_late = {i: sbuf(f"z_late{i}", [P, i, Q], F32) for i in (2, 3)}
+        z_late = {i: sbuf(f"z_late{i}", [P, 2, Q], F32) for i in (2, 3)}
         w_raw = sbuf("w_raw", [P, 2 * D], U8)
         w_plane_raw = sbuf("w_plane_raw", [P, D], U8)
         ident = sbuf("ident", [P, P], F32)
@@ -79,18 +79,21 @@ def tile_attend_gvq_pl_r_x_kernel(
         nc.sync.dma_start(book2[0][:], cb2_rows[:, 0, :])
         nc.sync.dma_start(code2[:], offs2)
         nc.sync.dma_start(book[1][:], cb_rows[:, 1, :])
-        nc.sync.dma_start(z1[:], z_rows[:, 1, 0:TA])
+        load_scale_rows(0)
+        nc.sync.dma_start(z1[:], z_rows[:, 1, :])
+        load_scale_rows(1)
         nc.sync.dma_start(book2[1][:], cb2_rows[:, 1, :])
+        load_scale_rows(2)
         for j in (2, 3):
             nc.sync.dma_start(book[j][:], cb_rows[:, j, :])
+            if j == 2:
+                load_scale_rows(3)
             nc.sync.dma_start(z_half[j][:], z_rows[:, j, 0 : 2 * Q])
         for j in (2, 3):
             nc.sync.dma_start(book2[j][:], cb2_rows[:, j, :])
         nc.sync.dma_start(z_late[2][:], z_rows[:, 2:LANES, 2 * Q : TA])
-        for q in range(QUADRANTS):
-            load_scale_rows(q)
+        nc.sync.dma_start(z_late[3][:], z_rows[:, 2:LANES, TA:T])
         nc.sync.dma_start(w_raw[:].bitcast(I32), w_words[0].bitcast(I32))
-        nc.sync.dma_start(z_late[3][:], z_rows[:, 1:LANES, TA:T])
 
         def gather1(dst, j, t0, z_cols):
             n = z_cols.shape[1]
@@ -113,7 +116,7 @@ def tile_attend_gvq_pl_r_x_kernel(
         def quantise(codes, plane, src, fmt):
             nc.vector.quantize_mx(out=codes.bitcast(fmt), scales=plane, in_=src.rearrange("p t j -> p (t j)"))
 
-        part = {j: sbuf(f"part{j}", [P, T if j == 0 else TA], F32) for j in range(LANES)}
+        part = {j: sbuf(f"part{j}", [P, T if j < 2 else TA], F32) for j in range(LANES)}
         neg_a = sbuf("neg_a", [P, LANES, 2 * Q], F32)
         neg_q = sbuf("neg_q", [P, LANES, Q], F32)
         H = 2 * Q
@@ -125,16 +128,16 @@ def tile_attend_gvq_pl_r_x_kernel(
             )
 
         gather1(part[0][:, 0:Z0], 0, 0, z0a[:])
-        mid = (Z0 + T) // 2
-        gather1(part[0][:, Z0:mid], 0, Z0, z0b[:, 0 : mid - Z0])
-        gather1(part[0][:, mid:T], 0, mid, z0b[:, mid - Z0 : T - Z0])
+        gather1(part[0][:, Z0:T], 0, Z0, z0b[:])
         gather2(neg_a[:, 0, :], 0, 0, part[0][:, 0:H])
         gather2(neg_q[:, 0, :], 0, H, part[0][:, H:TA])
         gather1(part[1][:, 0:H], 1, 0, z1[:, 0:H])
-        gather1(part[1][:, H:TA], 1, H, z1[:, H:TA])
+        gather1(part[1][:, H:T], 1, H, z1[:, H:T])
         gather2(neg_a[:, 1, :], 1, 0, part[1][:, 0:H])
         gather2(neg_q[:, 1, :], 1, H, part[1][:, H:TA])
 
+        plane_dealt = sbuf("plane_dealt", [P, LANES, P], U8)
+        nc.vector.tensor_copy(*deal_views(plane_dealt[:], w_plane_raw[:], 0, LANES))
         ga_bf01 = sbuf("ga_bf01", [P, H, LANES], BF16)
         ga_bf2 = sbuf("ga_bf2", [P, Q, LANES], BF16)
         for j in (2, 3):
@@ -153,22 +156,20 @@ def tile_attend_gvq_pl_r_x_kernel(
         neg_b = sbuf("neg_b", [P, LANES, Q], F32, "part2")
         gather2(neg_b[:, 0, :], 0, TA, part[0][:, TA:T])
         quantise(ga_codes[:, 0:H], ga_plane[:, 0:H], ga_bf01[:], E5M2X4)
-        plane_dealt = sbuf("plane_dealt", [P, LANES, P], U8, "neg_a")
-        nc.vector.tensor_copy(*deal_views(plane_dealt[:], w_plane_raw[:], 0, LANES))
+        gather2(neg_b[:, 1, :], 1, TA, part[1][:, TA:T])
         w_first = sbuf("w_first", [P, 1, P], U16)
         nc.scalar.copy(*deal_views(w_first[:], w_raw[:].bitcast(U16), 0, 1))
         w_rest = sbuf("w_rest", [P, 3, P], U16)
         nc.scalar.copy(*deal_views(w_rest[:], w_raw[:].bitcast(U16), 1, 3))
         quantise(ga_codes[:, H:TA], ga_plane[:, H:TA], ga_bf2[:], E5M2X4)
-        part_b = sbuf("part_b", [P, 3, Q], F32, "neg_q")
-        for j in (1, 2, 3):
-            gather1(part_b[:, j - 1, :], j, TA, z_late[3][:, j - 1, :])
-        for j in (1, 2):
-            gather2(neg_b[:, j, :], j, TA, part_b[:, j - 1, :])
+        part_b = sbuf("part_b", [P, 2, Q], F32, "neg_q")
+        for j in (2, 3):
+            gather1(part_b[:, j - 2, :], j, TA, z_late[3][:, j - 2, :])
+        gather2(neg_b[:, 2, :], 2, TA, part_b[:, 0, :])
         E = Q // 2
         halves = (slice(0, E), slice(E, Q))
         for cols in halves:
-            gather2(neg_b[:, 3, cols], 3, TA + cols.start, part_b[:, 2, cols])
+            gather2(neg_b[:, 3, cols], 3, TA + cols.start, part_b[:, 1, cols])
         gb_bf = sbuf("gb_bf", [P, Q, LANES], BF16)
         gb_codes = sbuf("gb_codes", [P, Q], U32)
         gb_plane = sbuf("gb_plane", [P, Q], U8)

@@ -193,7 +193,7 @@ def tile_attend_gvq_pl_r_x_kernel(
             if j < LANES - 1:
                 nc.scalar.copy(ya[:, j, :], acc[:, 0:TA])
             else:
-                for t0, t1 in ((0, H), (H, TA)):
+                for t0, t1 in ((0, Q), (Q, H), (H, TA)):
                     nc.scalar.copy(ya[:, j, t0:t1], acc[:, t0:t1])
             nc.sync.dma_start(out_rows[:, j, 0:TA], ya[:, j, :])
 
@@ -225,8 +225,10 @@ def tile_attend_gvq_pl_r_x_kernel(
 
         y_plane = sbuf("y_plane", [P, T], U8)
         ya_bf = sbuf("ya_bf", [P, TA, LANES], BF16, "part2")
-        for cols in (slice(0, H), slice(H, TA)):
-            nc.vector.tensor_copy(*weave_views(ya_bf[:, cols, :], ya[:, :, cols]))
+        nc.vector.tensor_copy(*weave_views(ya_bf[:, :, 0:2], ya[:, 0:2, :]))
+        for i in range(3):
+            cols = slice(i * Q, (i + 1) * Q)
+            nc.vector.tensor_copy(*weave_views(ya_bf[:, cols, 2:4], ya[:, 2:4, cols]))
         y_codes = [sbuf("y_codes0", [P, H], U32), sbuf("y_codes1", [P, H], U32, "yb_t3")]
         quantise(y_codes[0][:], y_plane[:, 0:H], ya_bf[:, 0:H, :], E4M3X4)
         nc.sync.dma_start(out_words[:, 0:H], y_codes[0][:].bitcast(I32))

@@ -214,10 +214,7 @@ def tile_attend_gvq_pl_r_x_kernel(
         for j in range(LANES):
             nc.scalar.copy(yb_t[j][:], acc_dealt[:, j, :])
             nc.tensor.transpose(turned[:, j, :], yb_t[j][:], ident[:])
-            if j < 2:
-                nc.tensor.transpose(turned_pair[0][:, j, :], yb_t[j][:], ident[:])
-        for j in (2, 3):
-            nc.tensor.transpose(turned_pair[1][:, j - 2, :], yb_t[j][:], ident[:])
+            nc.tensor.transpose(turned_pair[j // 2][:, j % 2, :], yb_t[j][:], ident[:])
         for u in range(2):
             yb = sbuf(f"yb{u}", [P, 2, Q], F32)
             nc.scalar.copy(yb[:], turned_pair[u][:])

@@ -1,7 +1,6 @@
 from contextlib import ExitStack
 
 import concourse.mybir as mybir
-from concourse.masks import make_identity
 
 T, C, D, N = 512, 512, 512, 512
 FLOPS = 2 * N * D * T
@@ -24,9 +23,9 @@ LANES = 4
 QUADRANTS = 4
 PER_COLUMN = 16
 Q = 128
-TA = 3 * Q
+H = 2 * Q
+TILES = T // Q
 RUN = 4
-Z0 = 256
 
 
 def tile_attend_gvq_pl_r_x_kernel(
@@ -44,16 +43,9 @@ def tile_attend_gvq_pl_r_x_kernel(
         code2 = keep.tile([P, T // PER_COLUMN], U16, name="code2")
         book = [sbuf(f"book{j}", [P, C], F32) for j in range(LANES)]
         book2 = [sbuf(f"book2_{j}", [P, C], F32) for j in range(LANES)]
-        z0a = sbuf("z0a", [P, Z0], F32)
-        z0b = sbuf("z0b", [P, T - Z0], F32)
-        z1 = sbuf("z1", [P, T], F32)
-        z_half = {j: sbuf(f"z_half{j}", [P, 2 * Q], F32) for j in (2, 3)}
-        z_late = {i: sbuf(f"z_late{i}", [P, 2, Q], F32) for i in (2, 3)}
+        z = [sbuf(f"z{i}", [P, LANES, Q], F32) for i in range(TILES)]
         w_raw = sbuf("w_raw", [P, 2 * D], U8)
         w_plane_raw = sbuf("w_plane_raw", [P, D], U8)
-        ident = sbuf("ident", [P, P], F32)
-        ga_codes = sbuf("ga_codes", [P, T], U32)
-        ga_plane = sbuf("ga_plane", [P, T], U8)
 
         z_rows = zT.rearrange("(p j) t -> p j t", j=LANES)
         cb_rows = cb.rearrange("(p j) c -> p j c", j=LANES)
@@ -63,48 +55,41 @@ def tile_attend_gvq_pl_r_x_kernel(
         out_scales = out_2[0].bitcast(I32)
 
         nc.vector.memset(w_plane_raw[:].bitcast(I32), 0)
-        make_identity(nc, ident[:])
-        nc.gpsimd.memset(ga_codes[:, TA:T], 0)
-        nc.gpsimd.memset(ga_plane[:, TA:T].bitcast(I32), 0)
 
         def load_scale_rows(q):
             nc.sync.dma_start(
                 w_plane_raw[32 * q : 32 * q + 4, :].bitcast(I32), w_scales[0, 4 * q : 4 * q + 4, :].bitcast(I32)
             )
 
+        nc.sync.dma_start(w_raw[:].bitcast(I32), w_words[0].bitcast(I32))
         nc.sync.dma_start(book[0][:], cb_rows[:, 0, :])
         nc.sync.dma_start(code[:], offs)
-        nc.sync.dma_start(z0a[:], z_rows[:, 0, 0:Z0])
-        nc.sync.dma_start(z0b[:], z_rows[:, 0, Z0:T])
         nc.sync.dma_start(book2[0][:], cb2_rows[:, 0, :])
         nc.sync.dma_start(code2[:], offs2)
-        nc.sync.dma_start(book[1][:], cb_rows[:, 1, :])
-        load_scale_rows(0)
-        nc.sync.dma_start(z1[:], z_rows[:, 1, :])
-        load_scale_rows(1)
-        nc.sync.dma_start(book2[1][:], cb2_rows[:, 1, :])
-        load_scale_rows(2)
-        for j in (2, 3):
+        for j in range(1, LANES):
             nc.sync.dma_start(book[j][:], cb_rows[:, j, :])
-            if j == 2:
-                load_scale_rows(3)
-            nc.sync.dma_start(z_half[j][:], z_rows[:, j, 0 : 2 * Q])
-        for j in (2, 3):
+            if j > 1:
+                load_scale_rows(2 * j - 3)
+            if j == LANES - 1:
+                nc.sync.dma_start(z[0][:], z_rows[:, :, 0:Q])
             nc.sync.dma_start(book2[j][:], cb2_rows[:, j, :])
-        nc.sync.dma_start(z_late[2][:], z_rows[:, 2:LANES, 2 * Q : TA])
-        nc.sync.dma_start(z_late[3][:], z_rows[:, 2:LANES, TA:T])
-        nc.sync.dma_start(w_raw[:].bitcast(I32), w_words[0].bitcast(I32))
+            if j < 3:
+                load_scale_rows(2 * j - 2)
+        for i in range(1, TILES):
+            nc.sync.dma_start(z[i][:], z_rows[:, :, i * Q : (i + 1) * Q])
 
-        def gather1(dst, j, t0, z_cols):
-            n = z_cols.shape[1]
-            nc.vector.tensor_tensor(
-                dst, book[j][:].indirect(code[:, t0 // PER_COLUMN : (t0 + n) // PER_COLUMN]), z_cols, ALU.subtract
-            )
+        first = sbuf("first", [P, LANES, T], F32)
+        both = sbuf("both", [P, LANES, T], F32)
 
-        def gather2(dst, j, t0, part_cols):
-            n = part_cols.shape[1]
+        def entries(lst, t0, t1):
+            return lst[:, t0 // PER_COLUMN : t1 // PER_COLUMN]
+
+        def gather1(j, t0, t1):
+            nc.scalar.activation(first[:, j, t0:t1], book[j][:].indirect(entries(code, t0, t1)), COPY)
+
+        def gather2(j, t0, t1):
             nc.vector.tensor_tensor(
-                dst, book2[j][:].indirect(code2[:, t0 // PER_COLUMN : (t0 + n) // PER_COLUMN]), part_cols, ALU.add
+                both[:, j, t0:t1], book2[j][:].indirect(entries(code2, t0, t1)), first[:, j, t0:t1], ALU.add
             )
 
         def weave_views(dst, src):
@@ -116,125 +101,80 @@ def tile_attend_gvq_pl_r_x_kernel(
         def quantise(codes, plane, src, fmt):
             nc.vector.quantize_mx(out=codes.bitcast(fmt), scales=plane, in_=src.rearrange("p t j -> p (t j)"))
 
-        part = {j: sbuf(f"part{j}", [P, T if j < 2 else TA], F32) for j in range(LANES)}
-        neg_a = sbuf("neg_a", [P, LANES, 2 * Q], F32)
-        neg_q = sbuf("neg_q", [P, LANES, Q], F32)
-        H = 2 * Q
-
-        def deal_views(dst, src, j0, n):
+        def deal_views(dst, src):
             return (
                 dst.rearrange("p j (h m) -> p h j m", h=2),
-                src.rearrange("p (h m j) -> p h j m", h=2, j=LANES)[:, :, j0 : j0 + n, :],
+                src.rearrange("p (h m j) -> p h j m", h=2, j=LANES),
             )
 
-        gather1(part[0][:, 0:Z0], 0, 0, z0a[:])
-        gather1(part[0][:, Z0:T], 0, Z0, z0b[:])
-        gather2(neg_a[:, 0, :], 0, 0, part[0][:, 0:H])
-        gather2(neg_q[:, 0, :], 0, H, part[0][:, H:TA])
-        gather1(part[1][:, 0:H], 1, 0, z1[:, 0:H])
-        gather1(part[1][:, H:T], 1, H, z1[:, H:T])
-        gather2(neg_a[:, 1, :], 1, 0, part[1][:, 0:H])
-        gather2(neg_q[:, 1, :], 1, H, part[1][:, H:TA])
+        w_dealt = sbuf("w_dealt", [P, LANES, P], U16)
+        nc.scalar.copy(*deal_views(w_dealt[:], w_raw[:].bitcast(U16)))
+        for j in range(LANES):
+            for t0 in (0, H):
+                if j == 0 and t0 == H:
+                    nc.vector.tensor_copy(first[:, 0, H:T], book[0][:].indirect(entries(code, H, T)))
+                else:
+                    gather1(j, t0, t0 + H)
+            if j < LANES - 1:
+                for t0 in (0, H):
+                    gather2(j, t0, t0 + H)
 
         plane_dealt = sbuf("plane_dealt", [P, LANES, P], U8)
-        nc.vector.tensor_copy(*deal_views(plane_dealt[:], w_plane_raw[:], 0, LANES))
-        ga_bf01 = sbuf("ga_bf01", [P, H, LANES], BF16)
-        ga_bf2 = sbuf("ga_bf2", [P, Q, LANES], BF16)
-        for j in (2, 3):
-            gather1(part[j][:, 0:H], j, 0, z_half[j][:])
-        for j in (2, 3):
-            gather2(neg_a[:, j, :], j, 0, part[j][:, 0:H])
-        for i in range(2):
-            cols = slice(i * Q, (i + 1) * Q)
-            nc.scalar.activation(*weave_views(ga_bf01[:, cols, :], neg_a[:, :, cols]), COPY, scale=-BETA)
-        for j in (2, 3):
-            gather1(part[j][:, H:TA], j, H, z_late[2][:, j - 2, :])
-        for j in (2, 3):
-            gather2(neg_q[:, j, :], j, H, part[j][:, H:TA])
-        nc.scalar.activation(*weave_views(ga_bf2[:], neg_q[:]), COPY, scale=-BETA)
-
-        neg_b = sbuf("neg_b", [P, LANES, Q], F32, "part2")
-        gather2(neg_b[:, 0, :], 0, TA, part[0][:, TA:T])
-        quantise(ga_codes[:, 0:H], ga_plane[:, 0:H], ga_bf01[:], E5M2X4)
-        gather2(neg_b[:, 1, :], 1, TA, part[1][:, TA:T])
-        w_first = sbuf("w_first", [P, 1, P], U16)
-        nc.scalar.copy(*deal_views(w_first[:], w_raw[:].bitcast(U16), 0, 1))
-        w_rest = sbuf("w_rest", [P, 3, P], U16)
-        nc.scalar.copy(*deal_views(w_rest[:], w_raw[:].bitcast(U16), 1, 3))
-        quantise(ga_codes[:, H:TA], ga_plane[:, H:TA], ga_bf2[:], E5M2X4)
-        part_b = sbuf("part_b", [P, 2, Q], F32, "neg_q")
-        for j in (2, 3):
-            gather1(part_b[:, j - 2, :], j, TA, z_late[3][:, j - 2, :])
-        gather2(neg_b[:, 2, :], 2, TA, part_b[:, 0, :])
-        E = Q // 2
-        halves = (slice(0, E), slice(E, Q))
-        for cols in halves:
-            gather2(neg_b[:, 3, cols], 3, TA + cols.start, part_b[:, 1, cols])
-        gb_bf = sbuf("gb_bf", [P, Q, LANES], BF16)
-        gb_codes = sbuf("gb_codes", [P, Q], U32)
-        gb_plane = sbuf("gb_plane", [P, Q], U8)
-        for cols in halves:
-            nc.vector.tensor_scalar(*weave_views(gb_bf[:, cols, :], neg_b[:, :, cols]), -BETA, None, ALU.mult)
-        for cols in halves:
-            quantise(gb_codes[:, cols], gb_plane[:, cols], gb_bf[:, cols, :], E5M2X4)
-
-        ya = sbuf("ya", [P, LANES, TA], F32)
-        for j in range(LANES):
-            acc = psum.tile([P, T], F32, name=f"acc{j}")
-            nc.tensor.matmul_mx(
-                out=acc[:],
-                lhsT=(w_first[:, 0, :] if j == 0 else w_rest[:, j - 1, :]).bitcast(U8).bitcast(E2M1X4),
-                lhsT_scale=plane_dealt[:, j, :],
-                rhs=ga_codes[:].bitcast(E5M2X4),
-                rhs_scale=ga_plane[:],
-                start=True,
-                stop=True,
-            )
-            if j < LANES - 1:
-                nc.scalar.copy(ya[:, j, :], acc[:, 0:TA])
-            else:
-                for t0, t1 in ((0, Q), (Q, H), (H, TA)):
-                    nc.scalar.copy(ya[:, j, t0:t1], acc[:, t0:t1])
-            nc.sync.dma_start(out_rows[:, j, 0:TA], ya[:, j, :])
-
-        acc_b = psum.tile([P, D], F32, name="acc_b")
-        nc.tensor.matmul_mx(
-            out=acc_b[:],
-            lhsT=gb_codes[:].bitcast(E5M2X4),
-            lhsT_scale=gb_plane[:],
-            rhs=w_raw[:].bitcast(E2M1X4),
-            rhs_scale=w_plane_raw[:],
-            start=True,
-            stop=True,
-        )
-        acc_dealt = acc_b[:].rearrange("t (m j) -> t j m", j=LANES)
-        turned = psum.tile([P, LANES, Q], F32, name="turned")
-        turned_pair = [psum.tile([P, 2, Q], F32, name=f"turned_pair{u}") for u in range(2)]
-        yb_t = [sbuf(f"yb_t{j}", [P, P], F32) for j in range(LANES)]
-        for j in range(LANES):
-            nc.scalar.copy(yb_t[j][:], acc_dealt[:, j, :])
-            nc.tensor.transpose(turned[:, j, :], yb_t[j][:], ident[:])
-            nc.tensor.transpose(turned_pair[j // 2][:, j % 2, :], yb_t[j][:], ident[:])
-        for u in range(2):
-            yb = sbuf(f"yb{u}", [P, 2, Q], F32)
-            nc.scalar.copy(yb[:], turned_pair[u][:])
-            nc.sync.dma_start(out_rows[:, 2 * u : 2 * u + 2, TA:T], yb[:])
+        nc.vector.tensor_copy(*deal_views(plane_dealt[:], w_plane_raw[:]))
+        last = LANES - 1
+        gather2(last, 0, Q)
+        gather2(last, Q, H)
+        second = sbuf("second", [P, H], F32)
+        nc.scalar.activation(second[:], book2[last][:].indirect(entries(code2, H, T)), COPY)
 
         y_plane = sbuf("y_plane", [P, T], U8)
-        ya_bf = sbuf("ya_bf", [P, TA, LANES], BF16, "part2")
-        nc.vector.tensor_copy(*weave_views(ya_bf[:, :, 0:2], ya[:, 0:2, :]))
-        for i in range(3):
-            cols = slice(i * Q, (i + 1) * Q)
-            nc.vector.tensor_copy(*weave_views(ya_bf[:, cols, 2:4], ya[:, 2:4, cols]))
-        y_codes = [sbuf("y_codes0", [P, H], U32), sbuf("y_codes1", [P, H], U32, "yb_t3")]
-        quantise(y_codes[0][:], y_plane[:, 0:H], ya_bf[:, 0:H, :], E4M3X4)
-        nc.sync.dma_start(out_words[:, 0:H], y_codes[0][:].bitcast(I32))
+        y_codes = [sbuf(f"y_codes{h}", [P, H], U32) for h in range(2)]
+        g_bf, acc, y, y_bf = {}, {}, {}, {}
 
-        yb_bf = sbuf("yb_bf", [P, Q, LANES], BF16)
-        nc.vector.tensor_copy(*weave_views(yb_bf[:], turned[:]))
-        quantise(y_codes[1][:, 0:Q], y_plane[:, H:TA], ya_bf[:, H:TA, :], E4M3X4)
-        quantise(y_codes[1][:, Q:H], y_plane[:, TA:T], yb_bf[:], E4M3X4)
-        nc.sync.dma_start(out_words[:, H:T], y_codes[1][:].bitcast(I32))
+        def subtract_and_weave(i):
+            if i == 1:
+                nc.vector.tensor_tensor(both[:, last, H:T], first[:, last, H:T], second[:], ALU.add)
+            e = sbuf(f"e{i}", [P, LANES, Q], F32)
+            nc.vector.tensor_tensor(e[:], z[i][:], both[:, :, i * Q : (i + 1) * Q], ALU.subtract)
+            g_bf[i] = sbuf(f"g_bf{i}", [P, Q, LANES], BF16)
+            nc.scalar.activation(*weave_views(g_bf[i][:], e[:]), COPY, scale=BETA)
+
+        def multiply(i):
+            g_codes = sbuf(f"g_codes{i}", [P, Q], U32)
+            g_plane = sbuf(f"g_plane{i}", [P, Q], U8)
+            quantise(g_codes[:], g_plane[:], g_bf[i][:], E5M2X4)
+            acc[i] = psum.tile([P, LANES, Q], F32, name=f"acc{i}")
+            for j in range(LANES):
+                nc.tensor.matmul_mx(
+                    out=acc[i][:, j, :],
+                    lhsT=w_dealt[:, j, :].bitcast(U8).bitcast(E2M1X4),
+                    lhsT_scale=plane_dealt[:, j, :],
+                    rhs=g_codes[:].bitcast(E5M2X4),
+                    rhs_scale=g_plane[:],
+                    start=True,
+                    stop=True,
+                )
+
+        def copy_out(i):
+            y[i] = sbuf(f"y{i}", [P, LANES, Q], F32)
+            nc.scalar.copy(y[i][:], acc[i][:])
+            nc.sync.dma_start(out_rows[:, :, i * Q : (i + 1) * Q], y[i][:])
+
+        def weave_result(i):
+            y_bf[i] = sbuf(f"y_bf{i}", [P, Q, LANES], BF16)
+            nc.vector.tensor_copy(*weave_views(y_bf[i][:], y[i][:]))
+
+        def quantise_result(i):
+            h, half = divmod(i, 2)
+            quantise(y_codes[h][:, half * Q : (half + 1) * Q], y_plane[:, i * Q : (i + 1) * Q], y_bf[i][:], E4M3X4)
+            if half == 1:
+                nc.sync.dma_start(out_words[:, h * H : (h + 1) * H], y_codes[h][:].bitcast(I32))
+
+        stages = ((0, subtract_and_weave), (1, multiply), (3, copy_out), (4, weave_result), (5, quantise_result))
+        for step in range(TILES + stages[-1][0]):
+            for s, stage in stages:
+                if 0 <= step - s < TILES:
+                    stage(step - s)
         for q in range(QUADRANTS):
             queue = nc.scalar if q % 2 == 0 else nc.sync
             queue.dma_start(out_scales[4 * q : 4 * q + 4, :], y_plane[32 * q : 32 * q + 4, :].bitcast(I32))

@@ -61,41 +61,34 @@ def tile_attend_gvq_pl_r_x_kernel(
                 w_plane_raw[32 * q : 32 * q + 4, :].bitcast(I32), w_scales[0, 4 * q : 4 * q + 4, :].bitcast(I32)
             )
 
-        nc.sync.dma_start(w_raw[:].bitcast(I32), w_words[0].bitcast(I32))
+        warm = sbuf("warm", [P, 2], F32)
+        nc.gpsimd.memset(warm[:, 0:1], 0.0)
+        nc.scalar.activation(warm[:, 1:2], warm[:, 0:1], COPY)
+
         nc.sync.dma_start(book[0][:], cb_rows[:, 0, :])
         nc.sync.dma_start(code[:], offs)
-        nc.sync.dma_start(book2[0][:], cb2_rows[:, 0, :])
-        nc.sync.dma_start(code2[:], offs2)
-        for j in range(1, LANES):
-            nc.sync.dma_start(book[j][:], cb_rows[:, j, :])
-            if j > 1:
-                load_scale_rows(2 * j - 3)
-            if j == LANES - 1:
-                nc.sync.dma_start(z[0][:], z_rows[:, :, 0:Q])
+        for j in range(LANES):
+            if j + 1 < LANES:
+                nc.sync.dma_start(book[j + 1][:], cb_rows[:, j + 1, :])
+            if j == 0:
+                nc.sync.dma_start(w_raw[:].bitcast(I32), w_words[0].bitcast(I32))
+            else:
+                load_scale_rows(j)
             nc.sync.dma_start(book2[j][:], cb2_rows[:, j, :])
-            if j < 3:
-                load_scale_rows(2 * j - 2)
-        for i in range(1, TILES):
+            if j == 0:
+                nc.sync.dma_start(code2[:], offs2)
+            if j == 1:
+                load_scale_rows(0)
+        for i in range(TILES):
             nc.sync.dma_start(z[i][:], z_rows[:, :, i * Q : (i + 1) * Q])
-
-        first = sbuf("first", [P, LANES, T], F32)
-        both = sbuf("both", [P, LANES, T], F32)
 
         def entries(lst, t0, t1):
             return lst[:, t0 // PER_COLUMN : t1 // PER_COLUMN]
 
-        def gather1(j, t0, t1):
-            nc.scalar.activation(first[:, j, t0:t1], book[j][:].indirect(entries(code, t0, t1)), COPY)
-
-        def gather2(j, t0, t1):
-            nc.vector.tensor_tensor(
-                both[:, j, t0:t1], book2[j][:].indirect(entries(code2, t0, t1)), first[:, j, t0:t1], ALU.add
-            )
-
-        def weave_views(dst, src):
+        def weave_views(run, dst, *srcs):
             return (
-                dst.rearrange("p (c i) j -> p c j i", i=RUN),
-                src.rearrange("p j (c i) -> p c j i", i=RUN),
+                dst.rearrange("p (c i) j -> p c j i", i=run),
+                *(src.rearrange("p j (c i) -> p c j i", i=run) for src in srcs),
             )
 
         def quantise(codes, plane, src, fmt):
@@ -107,72 +100,119 @@ def tile_attend_gvq_pl_r_x_kernel(
                 src.rearrange("p (h m j) -> p h j m", h=2, j=LANES),
             )
 
+        first = sbuf("first", [P, LANES, H], F32)
+        both = sbuf("both", [P, LANES, H], F32)
+        scaled = sbuf("scaled", [P, LANES, H], F32)
+        scaled2 = sbuf("scaled2", [P, LANES, H], F32)
         w_dealt = sbuf("w_dealt", [P, LANES, P], U16)
-        nc.scalar.copy(*deal_views(w_dealt[:], w_raw[:].bitcast(U16)))
-        for j in range(LANES):
-            for t0 in (0, H):
-                if j == 0 and t0 == H:
-                    nc.vector.tensor_copy(first[:, 0, H:T], book[0][:].indirect(entries(code, H, T)))
-                else:
-                    gather1(j, t0, t0 + H)
-            if j < LANES - 1:
-                for t0 in (0, H):
-                    gather2(j, t0, t0 + H)
 
-        plane_dealt = sbuf("plane_dealt", [P, LANES, P], U8)
-        nc.vector.tensor_copy(*deal_views(plane_dealt[:], w_plane_raw[:]))
-        last = LANES - 1
-        gather2(last, 0, Q)
-        gather2(last, Q, H)
-        second = sbuf("second", [P, H], F32)
-        nc.scalar.activation(second[:], book2[last][:].indirect(entries(code2, H, T)), COPY)
+        def gather1(j):
+            nc.vector.tensor_copy(first[:, j, :], book[j][:].indirect(entries(code, 0, H)))
+            nc.scalar.activation(scaled[:, j, :], book[j][:].indirect(entries(code, H, T)), COPY, scale=BETA)
+
+        def gather2(j):
+            width = H if j < LANES - 1 else Q
+            for t0 in range(0, H, width):
+                cols = slice(t0, t0 + width)
+                nc.vector.tensor_tensor(
+                    both[:, j, cols], book2[j][:].indirect(entries(code2, t0, t0 + width)), first[:, j, cols], ALU.add
+                )
+            nc.scalar.activation(scaled2[:, j, :], book2[j][:].indirect(entries(code2, H, T)), COPY, scale=BETA)
+
+        gather1(0)
+        for j in range(LANES):
+            if j + 1 < LANES:
+                gather1(j + 1)
+            if j == 0:
+                nc.scalar.copy(*deal_views(w_dealt[:], w_raw[:].bitcast(U16)))
+            gather2(j)
 
         y_plane = sbuf("y_plane", [P, T], U8)
         y_codes = [sbuf(f"y_codes{h}", [P, H], U32) for h in range(2)]
-        g_bf, acc, y, y_bf = {}, {}, {}, {}
+        e, g_bf, acc, y, y_bf = {}, {}, {}, {}, {}
+        E = Q // 2
+        final = TILES - 1
 
-        def subtract_and_weave(i):
+        def pieces(i):
+            return (slice(0, E), slice(E, Q)) if i == final else (slice(0, Q),)
+
+        def subtract(i):
+            e[i] = sbuf(f"e{i}", [P, LANES, Q], F32, "g_bf0" if i == final else None)
+            own = slice(i * Q % H, i * Q % H + Q)
+            if i * Q < H:
+                nc.vector.tensor_tensor(e[i][:], z[i][:], both[:, :, own], ALU.subtract)
+            else:
+                nc.vector.scalar_tensor_tensor(e[i][:], z[i][:], BETA, scaled[:, :, own], ALU.mult, ALU.subtract)
+
+        planes = []
+
+        def weave(i):
             if i == 1:
-                nc.vector.tensor_tensor(both[:, last, H:T], first[:, last, H:T], second[:], ALU.add)
-            e = sbuf(f"e{i}", [P, LANES, Q], F32)
-            nc.vector.tensor_tensor(e[:], z[i][:], both[:, :, i * Q : (i + 1) * Q], ALU.subtract)
+                planes.append(sbuf("plane_dealt", [P, LANES, P], U8, "z1"))
+                nc.vector.tensor_copy(*deal_views(planes[0][:], w_plane_raw[:]))
             g_bf[i] = sbuf(f"g_bf{i}", [P, Q, LANES], BF16)
-            nc.scalar.activation(*weave_views(g_bf[i][:], e[:]), COPY, scale=BETA)
+            if i * Q < H:
+                nc.scalar.activation(*weave_views(RUN, g_bf[i][:], e[i][:]), COPY, scale=BETA)
+                return
+            own = scaled2[:, :, i * Q - H : (i + 1) * Q - H]
+            for cols in pieces(i):
+                nc.vector.tensor_tensor(
+                    *weave_views(2, g_bf[i][:, cols, :], e[i][:, :, cols], own[:, :, cols]), ALU.subtract
+                )
+
+        def banks(i):
+            return ((0, 2), (2, LANES)) if i == final else ((0, LANES),)
 
         def multiply(i):
             g_codes = sbuf(f"g_codes{i}", [P, Q], U32)
             g_plane = sbuf(f"g_plane{i}", [P, Q], U8)
-            quantise(g_codes[:], g_plane[:], g_bf[i][:], E5M2X4)
-            acc[i] = psum.tile([P, LANES, Q], F32, name=f"acc{i}")
-            for j in range(LANES):
-                nc.tensor.matmul_mx(
-                    out=acc[i][:, j, :],
-                    lhsT=w_dealt[:, j, :].bitcast(U8).bitcast(E2M1X4),
-                    lhsT_scale=plane_dealt[:, j, :],
-                    rhs=g_codes[:].bitcast(E5M2X4),
-                    rhs_scale=g_plane[:],
-                    start=True,
-                    stop=True,
-                )
+            for cols in pieces(i):
+                quantise(g_codes[:, cols], g_plane[:, cols], g_bf[i][:, cols, :], E5M2X4)
+            for j0, j1 in banks(i):
+                acc[i, j0] = psum.tile([P, j1 - j0, Q], F32, name=f"acc{i}_{j0}")
+                for j in range(j0, j1):
+                    nc.tensor.matmul_mx(
+                        out=acc[i, j0][:, j - j0, :],
+                        lhsT=w_dealt[:, j, :].bitcast(U8).bitcast(E2M1X4),
+                        lhsT_scale=planes[0][:, j, :],
+                        rhs=g_codes[:].bitcast(E5M2X4),
+                        rhs_scale=g_plane[:],
+                        start=True,
+                        stop=True,
+                    )
 
         def copy_out(i):
             y[i] = sbuf(f"y{i}", [P, LANES, Q], F32)
-            nc.scalar.copy(y[i][:], acc[i][:])
+            for j0, j1 in banks(i):
+                nc.scalar.copy(y[i][:, j0:j1, :], acc[i, j0][:])
             nc.sync.dma_start(out_rows[:, :, i * Q : (i + 1) * Q], y[i][:])
 
+        y_bf_first = sbuf("y_bf_first", [P, H, LANES], BF16)
+
         def weave_result(i):
-            y_bf[i] = sbuf(f"y_bf{i}", [P, Q, LANES], BF16)
-            nc.vector.tensor_copy(*weave_views(y_bf[i][:], y[i][:]))
+            if i == 0:
+                nc.scalar.activation(*weave_views(RUN, y_bf_first[:, 0:Q, :], acc[0, 0][:]), COPY)
+            elif i == 1:
+                nc.vector.tensor_copy(*weave_views(RUN, y_bf_first[:, Q:H, :], y[1][:]))
+            else:
+                y_bf[i] = sbuf(f"y_bf{i}", [P, Q, LANES], BF16)
+                for cols in pieces(i):
+                    nc.vector.tensor_copy(*weave_views(RUN, y_bf[i][:, cols, :], y[i][:, :, cols]))
 
         def quantise_result(i):
             h, half = divmod(i, 2)
-            quantise(y_codes[h][:, half * Q : (half + 1) * Q], y_plane[:, i * Q : (i + 1) * Q], y_bf[i][:], E4M3X4)
+            codes, plane = y_codes[h][:, half * Q : (half + 1) * Q], y_plane[:, i * Q : (i + 1) * Q]
+            if i == 1:
+                quantise(y_codes[0][:], y_plane[:, 0:H], y_bf_first[:], E4M3X4)
+            elif i > 1:
+                for cols in pieces(i):
+                    quantise(codes[:, cols], plane[:, cols], y_bf[i][:, cols, :], E4M3X4)
             if half == 1:
                 nc.sync.dma_start(out_words[:, h * H : (h + 1) * H], y_codes[h][:].bitcast(I32))
 
-        stages = ((0, subtract_and_weave), (1, multiply), (3, copy_out), (4, weave_result), (5, quantise_result))
+        stages = ((0, subtract), (1, weave), (2, multiply), (4, copy_out), (5, weave_result), (6, quantise_result))
         for step in range(TILES + stages[-1][0]):
-            for s, stage in stages:
+            for s, stage in (stages[1], stages[2], stages[0], *stages[3:]):
                 if 0 <= step - s < TILES:
                     stage(step - s)
         for q in range(QUADRANTS):

@@ -70,10 +70,10 @@ def tile_attend_gvq_pl_r_x_kernel(
         for j in range(LANES):
             if j + 1 < LANES:
                 nc.sync.dma_start(book[j + 1][:], cb_rows[:, j + 1, :])
-            if j == 0:
-                nc.sync.dma_start(w_raw[:].bitcast(I32), w_words[0].bitcast(I32))
-            else:
+            if j > 0:
                 load_scale_rows(j)
+            if j == LANES - 1:
+                nc.sync.dma_start(w_raw[:].bitcast(I32), w_words[0].bitcast(I32))
             nc.sync.dma_start(book2[j][:], cb2_rows[:, j, :])
             if j == 0:
                 nc.sync.dma_start(code2[:], offs2)
@@ -103,11 +103,15 @@ def tile_attend_gvq_pl_r_x_kernel(
         first = sbuf("first", [P, LANES, H], F32)
         both = sbuf("both", [P, LANES, H], F32)
         scaled = sbuf("scaled", [P, LANES, H], F32)
-        scaled2 = sbuf("scaled2", [P, LANES, H], F32)
+        shared = sbuf("shared", [P, LANES + 1, H], F32)
+        scaled2 = shared[:, 0:LANES, :]
         w_dealt = sbuf("w_dealt", [P, LANES, P], U16)
 
         def gather1(j):
-            nc.vector.tensor_copy(first[:, j, :], book[j][:].indirect(entries(code, 0, H)))
+            if j < LANES - 1:
+                nc.vector.tensor_copy(first[:, j, :], book[j][:].indirect(entries(code, 0, H)))
+            else:
+                nc.scalar.activation(first[:, j, :], book[j][:].indirect(entries(code, 0, H)), COPY)
             nc.scalar.activation(scaled[:, j, :], book[j][:].indirect(entries(code, H, T)), COPY, scale=BETA)
 
         def gather2(j):
@@ -117,15 +121,18 @@ def tile_attend_gvq_pl_r_x_kernel(
                 nc.vector.tensor_tensor(
                     both[:, j, cols], book2[j][:].indirect(entries(code2, t0, t0 + width)), first[:, j, cols], ALU.add
                 )
+            if j < LANES - 1:
+                gather2_scaled(j)
+
+        def gather2_scaled(j):
             nc.scalar.activation(scaled2[:, j, :], book2[j][:].indirect(entries(code2, H, T)), COPY, scale=BETA)
 
         gather1(0)
         for j in range(LANES):
             if j + 1 < LANES:
                 gather1(j + 1)
-            if j == 0:
-                nc.scalar.copy(*deal_views(w_dealt[:], w_raw[:].bitcast(U16)))
             gather2(j)
+        nc.scalar.copy(*deal_views(w_dealt[:], w_raw[:].bitcast(U16)))
 
         y_plane = sbuf("y_plane", [P, T], U8)
         y_codes = [sbuf(f"y_codes{h}", [P, H], U32) for h in range(2)]
@@ -137,7 +144,10 @@ def tile_attend_gvq_pl_r_x_kernel(
             return (slice(0, E), slice(E, Q)) if i == final else (slice(0, Q),)
 
         def subtract(i):
-            e[i] = sbuf(f"e{i}", [P, LANES, Q], F32, "g_bf0" if i == final else None)
+            if i == 0:
+                e[i] = shared[:, LANES - 1 : LANES + 1, :].rearrange("p a (b t) -> p (a b) t", t=Q)
+            else:
+                e[i] = sbuf(f"e{i}", [P, LANES, Q], F32, "g_bf0" if i == final else None)
             own = slice(i * Q % H, i * Q % H + Q)
             if i * Q < H:
                 nc.vector.tensor_tensor(e[i][:], z[i][:], both[:, :, own], ALU.subtract)
@@ -147,12 +157,14 @@ def tile_attend_gvq_pl_r_x_kernel(
         planes = []
 
         def weave(i):
-            if i == 1:
-                planes.append(sbuf("plane_dealt", [P, LANES, P], U8, "z1"))
+            if i == 0:
+                planes.append(sbuf("plane_dealt", [P, LANES, P], U8))
                 nc.vector.tensor_copy(*deal_views(planes[0][:], w_plane_raw[:]))
             g_bf[i] = sbuf(f"g_bf{i}", [P, Q, LANES], BF16)
             if i * Q < H:
                 nc.scalar.activation(*weave_views(RUN, g_bf[i][:], e[i][:]), COPY, scale=BETA)
+                if i == 1:
+                    gather2_scaled(LANES - 1)
                 return
             own = scaled2[:, :, i * Q - H : (i + 1) * Q - H]
             for cols in pieces(i):
@@ -212,7 +224,7 @@ def tile_attend_gvq_pl_r_x_kernel(
 
         stages = ((0, subtract), (1, weave), (2, multiply), (4, copy_out), (5, weave_result), (6, quantise_result))
         for step in range(TILES + stages[-1][0]):
-            for s, stage in (stages[1], stages[2], stages[0], *stages[3:]):
+            for s, stage in (stages[2], stages[1], stages[0], *stages[3:]):
                 if 0 <= step - s < TILES:
                     stage(step - s)
         for q in range(QUADRANTS):

@@ -169,7 +169,7 @@ def tile_attend_gvq_pl_r_x_kernel(
             own = scaled2[:, :, i * Q - H : (i + 1) * Q - H]
             for cols in pieces(i):
                 nc.vector.tensor_tensor(
-                    *weave_views(2, g_bf[i][:, cols, :], e[i][:, :, cols], own[:, :, cols]), ALU.subtract
+                    *weave_views(RUN, g_bf[i][:, cols, :], e[i][:, :, cols], own[:, :, cols]), ALU.subtract
                 )
 
         def banks(i):

@@ -70,15 +70,12 @@ def tile_attend_gvq_pl_r_x_kernel(
         for j in range(LANES):
             if j + 1 < LANES:
                 nc.sync.dma_start(book[j + 1][:], cb_rows[:, j + 1, :])
-            if j > 0:
-                load_scale_rows(j)
-            if j == LANES - 1:
-                nc.sync.dma_start(w_raw[:].bitcast(I32), w_words[0].bitcast(I32))
             nc.sync.dma_start(book2[j][:], cb2_rows[:, j, :])
             if j == 0:
                 nc.sync.dma_start(code2[:], offs2)
-            if j == 1:
-                load_scale_rows(0)
+        for q in range(QUADRANTS):
+            load_scale_rows(q)
+        nc.sync.dma_start(w_raw[:].bitcast(I32), w_words[0].bitcast(I32))
         for i in range(TILES):
             nc.sync.dma_start(z[i][:], z_rows[:, :, i * Q : (i + 1) * Q])
 

@@ -43,7 +43,8 @@ def tile_attend_gvq_pl_r_x_kernel(
         code2 = keep.tile([P, T // PER_COLUMN], U16, name="code2")
         book = [sbuf(f"book{j}", [P, C], F32) for j in range(LANES)]
         book2 = [sbuf(f"book2_{j}", [P, C], F32) for j in range(LANES)]
-        z = [sbuf(f"z{i}", [P, LANES, Q], F32) for i in range(TILES)]
+        z = [sbuf(f"z{i}", [P, LANES, Q], F32) for i in range(2)]
+        z_pair = [sbuf(f"z_pair{u}", [P, 2, H], F32) for u in range(2)]
         w_raw = sbuf("w_raw", [P, 2 * D], U8)
         w_plane_raw = sbuf("w_plane_raw", [P, D], U8)
 
@@ -76,8 +77,10 @@ def tile_attend_gvq_pl_r_x_kernel(
         for q in range(QUADRANTS):
             load_scale_rows(q)
         nc.sync.dma_start(w_raw[:].bitcast(I32), w_words[0].bitcast(I32))
-        for i in range(TILES):
+        for i in range(2):
             nc.sync.dma_start(z[i][:], z_rows[:, :, i * Q : (i + 1) * Q])
+        for u in range(2):
+            nc.sync.dma_start(z_pair[u][:], z_rows[:, 2 * u : 2 * u + 2, H:T])
 
         def entries(lst, t0, t1):
             return lst[:, t0 // PER_COLUMN : t1 // PER_COLUMN]
@@ -140,16 +143,22 @@ def tile_attend_gvq_pl_r_x_kernel(
         def pieces(i):
             return (slice(0, E), slice(E, Q)) if i == final else (slice(0, Q),)
 
+        late = sbuf("late", [P, LANES, H], F32)
+
         def subtract(i):
             if i == 0:
                 e[i] = shared[:, LANES - 1 : LANES + 1, :].rearrange("p a (b t) -> p (a b) t", t=Q)
+            elif i == 1:
+                e[i] = sbuf("e1", [P, LANES, Q], F32)[:]
             else:
-                e[i] = sbuf(f"e{i}", [P, LANES, Q], F32, "g_bf0" if i == final else None)
-            own = slice(i * Q % H, i * Q % H + Q)
+                e[i] = late[:, :, i * Q - H : (i + 1) * Q - H]
             if i * Q < H:
-                nc.vector.tensor_tensor(e[i][:], z[i][:], both[:, :, own], ALU.subtract)
+                nc.vector.tensor_tensor(e[i], z[i][:], both[:, :, i * Q : (i + 1) * Q], ALU.subtract)
             else:
-                nc.vector.scalar_tensor_tensor(e[i][:], z[i][:], BETA, scaled[:, :, own], ALU.mult, ALU.subtract)
+                pair = slice(2 * (i - 2), 2 * (i - 1))
+                nc.vector.scalar_tensor_tensor(
+                    late[:, pair, :], z_pair[i - 2][:], BETA, scaled[:, pair, :], ALU.mult, ALU.subtract
+                )
 
         planes = []
 
@@ -219,11 +228,20 @@ def tile_attend_gvq_pl_r_x_kernel(
             if half == 1:
                 nc.sync.dma_start(out_words[:, h * H : (h + 1) * H], y_codes[h][:].bitcast(I32))
 
-        stages = ((0, subtract), (1, weave), (2, multiply), (4, copy_out), (5, weave_result), (6, quantise_result))
-        for step in range(TILES + stages[-1][0]):
-            for s, stage in (stages[2], stages[1], stages[0], *stages[3:]):
-                if 0 <= step - s < TILES:
-                    stage(step - s)
+        for i in range(2):
+            subtract(i)
+            weave(i)
+        multiply(0)
+        subtract(2)
+        subtract(3)
+        multiply(1)
+        for i in range(2, TILES):
+            weave(i)
+            multiply(i)
+        for i in range(TILES):
+            copy_out(i)
+            weave_result(i)
+            quantise_result(i)
         for q in range(QUADRANTS):
             queue = nc.scalar if q % 2 == 0 else nc.sync
             queue.dma_start(out_scales[4 * q : 4 * q + 4, :], y_plane[32 * q : 32 * q + 4, :].bitcast(I32))

@@ -205,26 +205,19 @@ def tile_attend_gvq_pl_r_x_kernel(
                 nc.scalar.copy(y[i][:, j0:j1, :], acc[i, j0][:])
             nc.sync.dma_start(out_rows[:, :, i * Q : (i + 1) * Q], y[i][:])
 
-        y_bf_first = sbuf("y_bf_first", [P, H, LANES], BF16)
-
         def weave_result(i):
+            y_bf[i] = sbuf(f"y_bf{i}", [P, Q, LANES], BF16, {0: "g_bf2", 1: "late"}.get(i))
             if i == 0:
-                nc.scalar.activation(*weave_views(RUN, y_bf_first[:, 0:Q, :], acc[0, 0][:]), COPY)
-            elif i == 1:
-                nc.vector.tensor_copy(*weave_views(RUN, y_bf_first[:, Q:H, :], y[1][:]))
-            else:
-                y_bf[i] = sbuf(f"y_bf{i}", [P, Q, LANES], BF16)
-                for cols in pieces(i):
-                    nc.vector.tensor_copy(*weave_views(RUN, y_bf[i][:, cols, :], y[i][:, :, cols]))
+                nc.scalar.activation(*weave_views(RUN, y_bf[i][:], acc[i, 0][:]), COPY)
+                return
+            for cols in pieces(i):
+                nc.vector.tensor_copy(*weave_views(RUN, y_bf[i][:, cols, :], y[i][:, :, cols]))
 
         def quantise_result(i):
             h, half = divmod(i, 2)
             codes, plane = y_codes[h][:, half * Q : (half + 1) * Q], y_plane[:, i * Q : (i + 1) * Q]
-            if i == 1:
-                quantise(y_codes[0][:], y_plane[:, 0:H], y_bf_first[:], E4M3X4)
-            elif i > 1:
-                for cols in pieces(i):
-                    quantise(codes[:, cols], plane[:, cols], y_bf[i][:, cols, :], E4M3X4)
+            for cols in pieces(i):
+                quantise(codes[:, cols], plane[:, cols], y_bf[i][:, cols, :], E4M3X4)
             if half == 1:
                 nc.sync.dma_start(out_words[:, h * H : (h + 1) * H], y_codes[h][:].bitcast(I32))
 

@@ -24,8 +24,11 @@ QUADRANTS = 4
 PER_COLUMN = 16
 Q = 128
 H = 2 * Q
+E = Q // 2
 TILES = T // Q
 RUN = 4
+LAST = LANES - 1
+WIDE = 4 * C
 
 
 def tile_attend_gvq_pl_r_x_kernel(
@@ -41,10 +44,9 @@ def tile_attend_gvq_pl_r_x_kernel(
 
         code = keep.tile([P, T // PER_COLUMN], U16, name="code")
         code2 = keep.tile([P, T // PER_COLUMN], U16, name="code2")
-        book = [sbuf(f"book{j}", [P, C], F32) for j in range(LANES)]
+        book = [sbuf(f"book{j}", [P, WIDE if j < LAST else C], F32) for j in range(LANES)]
         book2 = [sbuf(f"book2_{j}", [P, C], F32) for j in range(LANES)]
-        z = [sbuf(f"z{i}", [P, LANES, Q], F32) for i in range(2)]
-        z_pair = [sbuf(f"z_pair{u}", [P, 2, H], F32) for u in range(2)]
+        z = [sbuf(f"z{i}", [P, LANES, Q], F32) for i in range(TILES)]
         w_raw = sbuf("w_raw", [P, 2 * D], U8)
         w_plane_raw = sbuf("w_plane_raw", [P, D], U8)
 
@@ -57,39 +59,40 @@ def tile_attend_gvq_pl_r_x_kernel(
 
         nc.vector.memset(w_plane_raw[:].bitcast(I32), 0)
 
+        warm = sbuf("warm", [P, 2], F32)
+        nc.gpsimd.memset(warm[:, 0:1], 0.0)
+        nc.scalar.activation(warm[:, 1:2], warm[:, 0:1], COPY)
+
         def load_scale_rows(q):
             nc.sync.dma_start(
                 w_plane_raw[32 * q : 32 * q + 4, :].bitcast(I32), w_scales[0, 4 * q : 4 * q + 4, :].bitcast(I32)
             )
 
-        warm = sbuf("warm", [P, 2], F32)
-        nc.gpsimd.memset(warm[:, 0:1], 0.0)
-        nc.scalar.activation(warm[:, 1:2], warm[:, 0:1], COPY)
+        def load_z(i):
+            nc.sync.dma_start(z[i][:], z_rows[:, :, i * Q : (i + 1) * Q])
 
-        nc.sync.dma_start(book[0][:], cb_rows[:, 0, :])
-        nc.sync.dma_start(code[:], offs)
         for j in range(LANES):
-            if j + 1 < LANES:
-                nc.sync.dma_start(book[j + 1][:], cb_rows[:, j + 1, :])
             nc.sync.dma_start(book2[j][:], cb2_rows[:, j, :])
             if j == 0:
                 nc.sync.dma_start(code2[:], offs2)
-        for q in range(QUADRANTS):
-            load_scale_rows(q)
-        nc.sync.dma_start(w_raw[:].bitcast(I32), w_words[0].bitcast(I32))
-        for i in range(2):
-            nc.sync.dma_start(z[i][:], z_rows[:, :, i * Q : (i + 1) * Q])
-        for u in range(2):
-            nc.sync.dma_start(z_pair[u][:], z_rows[:, 2 * u : 2 * u + 2, H:T])
+                nc.sync.dma_start(code[:], offs)
+            if j == LAST:
+                load_scale_rows(1)
+                nc.sync.dma_start(w_raw[:].bitcast(I32), w_words[0].bitcast(I32))
+            nc.sync.dma_start(book[j][:, 0:C], cb_rows[:, j, :])
+            if j == LAST - 1:
+                load_scale_rows(0)
+        load_scale_rows(2)
+        load_z(0)
+        load_scale_rows(3)
+        for i in range(1, TILES):
+            load_z(i)
 
         def entries(lst, t0, t1):
             return lst[:, t0 // PER_COLUMN : t1 // PER_COLUMN]
 
-        def weave_views(run, dst, *srcs):
-            return (
-                dst.rearrange("p (c i) j -> p c j i", i=run),
-                *(src.rearrange("p j (c i) -> p c j i", i=run) for src in srcs),
-            )
+        def weave_views(run, dst, src):
+            return dst.rearrange("p (c i) j -> p c j i", i=run), src.rearrange("p j (c i) -> p c j i", i=run)
 
         def quantise(codes, plane, src, fmt):
             nc.vector.quantize_mx(out=codes.bitcast(fmt), scales=plane, in_=src.rearrange("p t j -> p (t j)"))
@@ -100,82 +103,52 @@ def tile_attend_gvq_pl_r_x_kernel(
                 src.rearrange("p (h m j) -> p h j m", h=2, j=LANES),
             )
 
-        first = sbuf("first", [P, LANES, H], F32)
-        both = sbuf("both", [P, LANES, H], F32)
-        scaled = sbuf("scaled", [P, LANES, H], F32)
-        shared = sbuf("shared", [P, LANES + 1, H], F32)
-        scaled2 = shared[:, 0:LANES, :]
+        first = [sbuf(f"first{j}", [P, T if j < LAST else H], F32) for j in range(LANES)]
+        second = [sbuf(f"second{j}", [P, T if j < LAST else H], F32) for j in range(LANES)]
+        both = sbuf("both", [P, TILES, LANES, Q], F32)
         w_dealt = sbuf("w_dealt", [P, LANES, P], U16)
+        plane_dealt = sbuf("plane_dealt", [P, LANES, P], U8)
 
-        def gather1(j):
-            if j < LANES - 1:
-                nc.vector.tensor_copy(first[:, j, :], book[j][:].indirect(entries(code, 0, H)))
-            else:
-                nc.scalar.activation(first[:, j, :], book[j][:].indirect(entries(code, 0, H)), COPY)
-            nc.scalar.activation(scaled[:, j, :], book[j][:].indirect(entries(code, H, T)), COPY, scale=BETA)
+        def add(engine, j, i0, i1):
+            shift = H if j == LAST and i0 >= 2 else 0
+            first_part = first[j][:, i0 * Q - shift : i1 * Q - shift].rearrange("p (i t) -> p i t", t=Q)
+            second_part = second[j][:, i0 * Q - shift : i1 * Q - shift].rearrange("p (i t) -> p i t", t=Q)
+            engine.tensor_tensor(both[:, i0:i1, j, :], first_part, second_part, ALU.add)
 
-        def gather2(j):
-            width = H if j < LANES - 1 else Q
-            for t0 in range(0, H, width):
-                cols = slice(t0, t0 + width)
-                nc.vector.tensor_tensor(
-                    both[:, j, cols], book2[j][:].indirect(entries(code2, t0, t0 + width)), first[:, j, cols], ALU.add
-                )
-            if j < LANES - 1:
-                gather2_scaled(j)
+        def gather_scaled(dst, window, lst, t0, t1):
+            nc.scalar.activation(dst, window[:].indirect(entries(lst, t0, t1)), COPY, scale=BETA)
 
-        def gather2_scaled(j):
-            nc.scalar.activation(scaled2[:, j, :], book2[j][:].indirect(entries(code2, H, T)), COPY, scale=BETA)
-
-        gather1(0)
-        for j in range(LANES):
-            if j + 1 < LANES:
-                gather1(j + 1)
-            gather2(j)
+        for j in range(LAST):
+            for t0 in (0, H):
+                gather_scaled(second[j][:, t0 : t0 + H], book2[j], code2, t0, t0 + H)
+            nc.vector.tensor_scalar(first[j][:], book[j][:].indirect(code[:]), BETA, 0.0, ALU.mult, ALU.add)
+            add(nc.gpsimd if j < LAST - 1 else nc.vector, j, 0, TILES)
+        gather_scaled(second[LAST][:], book2[LAST], code2, 0, H)
         nc.scalar.copy(*deal_views(w_dealt[:], w_raw[:].bitcast(U16)))
+        for i in range(2):
+            gather_scaled(first[LAST][:, i * Q : (i + 1) * Q], book[LAST], code, i * Q, (i + 1) * Q)
+            add(nc.vector, LAST, i, i + 1)
+        gather_scaled(second[LAST][:], book2[LAST], code2, H, T)
 
         y_plane = sbuf("y_plane", [P, T], U8)
         y_codes = [sbuf(f"y_codes{h}", [P, H], U32) for h in range(2)]
-        e, g_bf, acc, y, y_bf = {}, {}, {}, {}, {}
-        E = Q // 2
+        g_bf, acc, y, y_bf = {}, {}, {}, {}
         final = TILES - 1
 
         def pieces(i):
             return (slice(0, E), slice(E, Q)) if i == final else (slice(0, Q),)
 
-        late = sbuf("late", [P, LANES, H], F32)
-
-        def subtract(i):
-            if i == 0:
-                e[i] = shared[:, LANES - 1 : LANES + 1, :].rearrange("p a (b t) -> p (a b) t", t=Q)
-            elif i == 1:
-                e[i] = sbuf("e1", [P, LANES, Q], F32)[:]
-            else:
-                e[i] = late[:, :, i * Q - H : (i + 1) * Q - H]
-            if i * Q < H:
-                nc.vector.tensor_tensor(e[i], z[i][:], both[:, :, i * Q : (i + 1) * Q], ALU.subtract)
-            else:
-                pair = slice(2 * (i - 2), 2 * (i - 1))
-                nc.vector.scalar_tensor_tensor(
-                    late[:, pair, :], z_pair[i - 2][:], BETA, scaled[:, pair, :], ALU.mult, ALU.subtract
-                )
-
-        planes = []
-
-        def weave(i):
-            if i == 0:
-                planes.append(sbuf("plane_dealt", [P, LANES, P], U8))
-                nc.vector.tensor_copy(*deal_views(planes[0][:], w_plane_raw[:]))
+        def form(i):
             g_bf[i] = sbuf(f"g_bf{i}", [P, Q, LANES], BF16)
-            if i * Q < H:
-                nc.scalar.activation(*weave_views(RUN, g_bf[i][:], e[i][:]), COPY, scale=BETA)
-                if i == 1:
-                    gather2_scaled(LANES - 1)
-                return
-            own = scaled2[:, :, i * Q - H : (i + 1) * Q - H]
+            own = both[:, i, :, :]
             for cols in pieces(i):
-                nc.vector.tensor_tensor(
-                    *weave_views(RUN, g_bf[i][:, cols, :], e[i][:, :, cols], own[:, :, cols]), ALU.subtract
+                nc.vector.scalar_tensor_tensor(
+                    g_bf[i][:, cols, :],
+                    z[i][:, :, cols].rearrange("p j t -> p t j"),
+                    BETA,
+                    own[:, :, cols].rearrange("p j t -> p t j"),
+                    ALU.mult,
+                    ALU.subtract,
                 )
 
         def banks(i):
@@ -192,7 +165,7 @@ def tile_attend_gvq_pl_r_x_kernel(
                     nc.tensor.matmul_mx(
                         out=acc[i, j0][:, j - j0, :],
                         lhsT=w_dealt[:, j, :].bitcast(U8).bitcast(E2M1X4),
-                        lhsT_scale=planes[0][:, j, :],
+                        lhsT_scale=plane_dealt[:, j, :],
                         rhs=g_codes[:].bitcast(E5M2X4),
                         rhs_scale=g_plane[:],
                         start=True,
@@ -206,7 +179,7 @@ def tile_attend_gvq_pl_r_x_kernel(
             nc.sync.dma_start(out_rows[:, :, i * Q : (i + 1) * Q], y[i][:])
 
         def weave_result(i):
-            y_bf[i] = sbuf(f"y_bf{i}", [P, Q, LANES], BF16, {0: "g_bf2", 1: "late"}.get(i))
+            y_bf[i] = sbuf(f"y_bf{i}", [P, Q, LANES], BF16)
             if i == 0:
                 nc.scalar.activation(*weave_views(RUN, y_bf[i][:], acc[i, 0][:]), COPY)
                 return
@@ -221,15 +194,14 @@ def tile_attend_gvq_pl_r_x_kernel(
             if half == 1:
                 nc.sync.dma_start(out_words[:, h * H : (h + 1) * H], y_codes[h][:].bitcast(I32))
 
-        for i in range(2):
-            subtract(i)
-            weave(i)
-        multiply(0)
-        subtract(2)
-        subtract(3)
-        multiply(1)
-        for i in range(2, TILES):
-            weave(i)
+        for i in range(TILES):
+            form(i)
+            if i == 0:
+                nc.vector.tensor_copy(*deal_views(plane_dealt[:], w_plane_raw[:]))
+                first[LAST] = sbuf("first_late", [P, H], F32, "z0")
+                gather_scaled(first[LAST][:], book[LAST], code, H, T)
+            if i == 1:
+                add(nc.vector, LAST, 2, TILES)
             multiply(i)
         for i in range(TILES):
             copy_out(i)

@@ -45,8 +45,9 @@ def tile_attend_gvq_pl_r_x_kernel(
         code = keep.tile([P, T // PER_COLUMN], U16, name="code")
         code2 = keep.tile([P, T // PER_COLUMN], U16, name="code2")
         book = [sbuf(f"book{j}", [P, WIDE if j < LAST else C], F32) for j in range(LANES)]
-        book2 = [sbuf(f"book2_{j}", [P, C], F32) for j in range(LANES)]
-        z = [sbuf(f"z{i}", [P, LANES, Q], F32) for i in range(TILES)]
+        book2 = [sbuf(f"book2_{j}", [P, 2 * C if 0 < j < LAST else C], F32) for j in range(LANES)]
+        z_early = sbuf("z_early", [P, LANES, H], F32)
+        z = [z_early[:, :, i * Q : (i + 1) * Q] if i < 2 else sbuf(f"z{i}", [P, LANES, Q], F32) for i in range(TILES)]
         w_raw = sbuf("w_raw", [P, 2 * D], U8)
         w_plane_raw = sbuf("w_plane_raw", [P, D], U8)
 
@@ -72,20 +73,18 @@ def tile_attend_gvq_pl_r_x_kernel(
             nc.sync.dma_start(z[i][:], z_rows[:, :, i * Q : (i + 1) * Q])
 
         for j in range(LANES):
-            nc.sync.dma_start(book2[j][:], cb2_rows[:, j, :])
+            nc.sync.dma_start(book2[j][:, 0:C], cb2_rows[:, j, :])
             if j == 0:
                 nc.sync.dma_start(code2[:], offs2)
                 nc.sync.dma_start(code[:], offs)
-            if j == LAST:
-                load_scale_rows(1)
-                nc.sync.dma_start(w_raw[:].bitcast(I32), w_words[0].bitcast(I32))
+            if j > 1:
+                load_scale_rows(2 * j - 4)
             nc.sync.dma_start(book[j][:, 0:C], cb_rows[:, j, :])
-            if j == LAST - 1:
-                load_scale_rows(0)
-        load_scale_rows(2)
-        load_z(0)
-        load_scale_rows(3)
-        for i in range(1, TILES):
+            if j in (1, 2):
+                load_scale_rows(2 * j - 1)
+        nc.sync.dma_start(w_raw[:].bitcast(I32), w_words[0].bitcast(I32))
+        nc.sync.dma_start(z_early[:], z_rows[:, :, 0:H])
+        for i in range(2, TILES):
             load_z(i)
 
         def entries(lst, t0, t1):
@@ -105,30 +104,29 @@ def tile_attend_gvq_pl_r_x_kernel(
 
         first = [sbuf(f"first{j}", [P, T if j < LAST else H], F32) for j in range(LANES)]
         second = [sbuf(f"second{j}", [P, T if j < LAST else H], F32) for j in range(LANES)]
-        both = sbuf("both", [P, TILES, LANES, Q], F32)
+        both = sbuf("both", [P, LANES, T], F32)
         w_dealt = sbuf("w_dealt", [P, LANES, P], U16)
         plane_dealt = sbuf("plane_dealt", [P, LANES, P], U8)
 
-        def add(engine, j, i0, i1):
-            shift = H if j == LAST and i0 >= 2 else 0
-            first_part = first[j][:, i0 * Q - shift : i1 * Q - shift].rearrange("p (i t) -> p i t", t=Q)
-            second_part = second[j][:, i0 * Q - shift : i1 * Q - shift].rearrange("p (i t) -> p i t", t=Q)
-            engine.tensor_tensor(both[:, i0:i1, j, :], first_part, second_part, ALU.add)
+        def add(engine, j, t0, t1):
+            engine.tensor_tensor(both[:, j, t0:t1], first[j][:, t0:t1], second[j][:, t0:t1], ALU.add)
 
         def gather_scaled(dst, window, lst, t0, t1):
             nc.scalar.activation(dst, window[:].indirect(entries(lst, t0, t1)), COPY, scale=BETA)
 
+        beta = sbuf("beta", [P, Q], F32)
+        nc.gpsimd.memset(beta[:], BETA)
+        nc.vector.tensor_tensor(second[0][:, 0:Q], book2[0][:].indirect(entries(code2, 0, Q)), beta[:], ALU.mult)
         for j in range(LAST):
-            for t0 in (0, H):
-                gather_scaled(second[j][:, t0 : t0 + H], book2[j], code2, t0, t0 + H)
+            t0 = Q if j == 0 else 0
+            gather_scaled(second[j][:, t0:T], book2[j], code2, t0, T)
             nc.vector.tensor_scalar(first[j][:], book[j][:].indirect(code[:]), BETA, 0.0, ALU.mult, ALU.add)
-            add(nc.gpsimd if j < LAST - 1 else nc.vector, j, 0, TILES)
-        gather_scaled(second[LAST][:], book2[LAST], code2, 0, H)
-        nc.scalar.copy(*deal_views(w_dealt[:], w_raw[:].bitcast(U16)))
-        for i in range(2):
-            gather_scaled(first[LAST][:, i * Q : (i + 1) * Q], book[LAST], code, i * Q, (i + 1) * Q)
-            add(nc.vector, LAST, i, i + 1)
-        gather_scaled(second[LAST][:], book2[LAST], code2, H, T)
+            add(nc.gpsimd if j < 2 else nc.vector, j, 0, T)
+
+        def last_lane(t0):
+            gather_scaled(second[LAST][:], book2[LAST], code2, t0, t0 + H)
+            gather_scaled(first[LAST][:], book[LAST], code, t0, t0 + H)
+            nc.vector.tensor_tensor(both[:, LAST, t0 : t0 + H], first[LAST][:], second[LAST][:], ALU.add)
 
         y_plane = sbuf("y_plane", [P, T], U8)
         y_codes = [sbuf(f"y_codes{h}", [P, H], U32) for h in range(2)]
@@ -140,7 +138,7 @@ def tile_attend_gvq_pl_r_x_kernel(
 
         def form(i):
             g_bf[i] = sbuf(f"g_bf{i}", [P, Q, LANES], BF16)
-            own = both[:, i, :, :]
+            own = both[:, :, i * Q : (i + 1) * Q]
             for cols in pieces(i):
                 nc.vector.scalar_tensor_tensor(
                     g_bf[i][:, cols, :],
@@ -194,14 +192,16 @@ def tile_attend_gvq_pl_r_x_kernel(
             if half == 1:
                 nc.sync.dma_start(out_words[:, h * H : (h + 1) * H], y_codes[h][:].bitcast(I32))
 
-        for i in range(TILES):
+        nc.vector.tensor_copy(*deal_views(plane_dealt[:], w_plane_raw[:]))
+        last_lane(0)
+        nc.scalar.copy(*deal_views(w_dealt[:], w_raw[:].bitcast(U16)))
+        form(0)
+        form(1)
+        multiply(0)
+        last_lane(H)
+        multiply(1)
+        for i in range(2, TILES):
             form(i)
-            if i == 0:
-                nc.vector.tensor_copy(*deal_views(plane_dealt[:], w_plane_raw[:]))
-                first[LAST] = sbuf("first_late", [P, H], F32, "z0")
-                gather_scaled(first[LAST][:], book[LAST], code, H, T)
-            if i == 1:
-                add(nc.vector, LAST, 2, TILES)
             multiply(i)
         for i in range(TILES):
             copy_out(i)

@@ -80,8 +80,8 @@ def tile_attend_gvq_pl_r_x_kernel(
             if j > 1:
                 load_scale_rows(2 * j - 4)
             nc.sync.dma_start(book[j][:, 0:C], cb_rows[:, j, :])
-            if j in (1, 2):
-                load_scale_rows(2 * j - 1)
+            if j > 1:
+                load_scale_rows(2 * j - 3)
         nc.sync.dma_start(w_raw[:].bitcast(I32), w_words[0].bitcast(I32))
         nc.sync.dma_start(z_early[:], z_rows[:, :, 0:H])
         for i in range(2, TILES):
@@ -123,10 +123,10 @@ def tile_attend_gvq_pl_r_x_kernel(
             nc.vector.tensor_scalar(first[j][:], book[j][:].indirect(code[:]), BETA, 0.0, ALU.mult, ALU.add)
             add(nc.gpsimd if j < 2 else nc.vector, j, 0, T)
 
-        def last_lane(t0):
-            gather_scaled(second[LAST][:], book2[LAST], code2, t0, t0 + H)
-            gather_scaled(first[LAST][:], book[LAST], code, t0, t0 + H)
-            nc.vector.tensor_tensor(both[:, LAST, t0 : t0 + H], first[LAST][:], second[LAST][:], ALU.add)
+        def last_lane(t0, place, place2):
+            gather_scaled(place2, book2[LAST], code2, t0, t0 + H)
+            gather_scaled(place, book[LAST], code, t0, t0 + H)
+            nc.vector.tensor_tensor(both[:, LAST, t0 : t0 + H], place, place2, ALU.add)
 
         y_plane = sbuf("y_plane", [P, T], U8)
         y_codes = [sbuf(f"y_codes{h}", [P, H], U32) for h in range(2)]
@@ -192,13 +192,14 @@ def tile_attend_gvq_pl_r_x_kernel(
             if half == 1:
                 nc.sync.dma_start(out_words[:, h * H : (h + 1) * H], y_codes[h][:].bitcast(I32))
 
+        last_lane(0, first[LAST][:], second[LAST][:])
         nc.vector.tensor_copy(*deal_views(plane_dealt[:], w_plane_raw[:]))
-        last_lane(0)
         nc.scalar.copy(*deal_views(w_dealt[:], w_raw[:].bitcast(U16)))
+        late = sbuf("late", [P, 2, H], F32, "w_raw")
         form(0)
         form(1)
         multiply(0)
-        last_lane(H)
+        last_lane(H, late[:, 0, :], late[:, 1, :])
         multiply(1)
         for i in range(2, TILES):
             form(i)

@@ -173,12 +173,13 @@ def tile_attend_gvq_pl_r_x_kernel(
         def copy_out(i):
             y[i] = sbuf(f"y{i}", [P, LANES, Q], F32)
             for j0, j1 in banks(i):
-                nc.scalar.copy(y[i][:, j0:j1, :], acc[i, j0][:])
+                for cols in pieces(i) if j0 > 0 else (slice(0, Q),):
+                    nc.scalar.copy(y[i][:, j0:j1, cols], acc[i, j0][:, :, cols])
             nc.sync.dma_start(out_rows[:, :, i * Q : (i + 1) * Q], y[i][:])
 
         def weave_result(i):
-            y_bf[i] = sbuf(f"y_bf{i}", [P, Q, LANES], BF16)
-            if i == 0:
+            y_bf[i] = sbuf(f"y_bf{i}", [P, Q, LANES], BF16, "z3" if i == 0 else None)
+            if i == 1:
                 nc.scalar.activation(*weave_views(RUN, y_bf[i][:], acc[i, 0][:]), COPY)
                 return
             for cols in pieces(i):

@@ -123,14 +123,15 @@ def tile_attend_gvq_pl_r_x_kernel(
             nc.vector.tensor_scalar(first[j][:], book[j][:].indirect(code[:]), BETA, 0.0, ALU.mult, ALU.add)
             add(nc.gpsimd if j < 2 else nc.vector, j, 0, T)
 
-        def last_lane(t0, place, place2):
-            gather_scaled(place2, book2[LAST], code2, t0, t0 + H)
-            gather_scaled(place, book[LAST], code, t0, t0 + H)
-            nc.vector.tensor_tensor(both[:, LAST, t0 : t0 + H], place, place2, ALU.add)
+        def last_lane(t0, t1, place, place2):
+            gather_scaled(place2, book2[LAST], code2, t0, t1)
+            gather_scaled(place, book[LAST], code, t0, t1)
+            nc.vector.tensor_tensor(both[:, LAST, t0:t1], place, place2, ALU.add)
 
         y_plane = sbuf("y_plane", [P, T], U8)
         y_codes = [sbuf(f"y_codes{h}", [P, H], U32) for h in range(2)]
         g_bf, acc, y, y_bf = {}, {}, {}, {}
+        y_early = []
         final = TILES - 1
 
         def pieces(i):
@@ -178,10 +179,12 @@ def tile_attend_gvq_pl_r_x_kernel(
             nc.sync.dma_start(out_rows[:, :, i * Q : (i + 1) * Q], y[i][:])
 
         def weave_result(i):
-            y_bf[i] = sbuf(f"y_bf{i}", [P, Q, LANES], BF16, "z3" if i == 0 else None)
-            if i == 1:
-                nc.scalar.activation(*weave_views(RUN, y_bf[i][:], acc[i, 0][:]), COPY)
-                return
+            if i == 0:
+                y_early.append(sbuf("y_bf_early", [P, H, LANES], BF16, "z3"))
+            if i < 2:
+                y_bf[i] = y_early[0][:, i * Q : (i + 1) * Q, :]
+            else:
+                y_bf[i] = sbuf(f"y_bf{i}", [P, Q, LANES], BF16)
             for cols in pieces(i):
                 nc.vector.tensor_copy(*weave_views(RUN, y_bf[i][:, cols, :], y[i][:, :, cols]))
 
@@ -193,18 +196,20 @@ def tile_attend_gvq_pl_r_x_kernel(
             if half == 1:
                 nc.sync.dma_start(out_words[:, h * H : (h + 1) * H], y_codes[h][:].bitcast(I32))
 
-        last_lane(0, first[LAST][:], second[LAST][:])
+        last_lane(0, H, first[LAST][:], second[LAST][:])
         nc.vector.tensor_copy(*deal_views(plane_dealt[:], w_plane_raw[:]))
         nc.scalar.copy(*deal_views(w_dealt[:], w_raw[:].bitcast(U16)))
         late = sbuf("late", [P, 2, H], F32, "w_raw")
         form(0)
         form(1)
         multiply(0)
-        last_lane(H, late[:, 0, :], late[:, 1, :])
+        last_lane(H, H + Q, late[:, 0, 0:Q], late[:, 1, 0:Q])
         multiply(1)
-        for i in range(2, TILES):
-            form(i)
-            multiply(i)
+        form(2)
+        last_lane(H + Q, T, late[:, 0, Q:H], late[:, 1, Q:H])
+        multiply(2)
+        form(3)
+        multiply(3)
         for i in range(TILES):
             copy_out(i)
             weave_result(i)

from contextlib import ExitStack

import concourse.mybir as mybir

T, C, D, N = 512, 512, 512, 512
FLOPS = 2 * N * D * T
BETA = 0.25

F32 = mybir.dt.float32
BF16 = mybir.dt.bfloat16
I32 = mybir.dt.int32
U32 = mybir.dt.uint32
U16 = mybir.dt.uint16
U8 = mybir.dt.uint8
E4M3X4 = mybir.dt.float8_e4m3fn_x4
E5M2X4 = mybir.dt.float8_e5m2_x4
E2M1X4 = mybir.dt.float4_e2m1fn_x4
ALU = mybir.AluOpType
COPY = mybir.ActivationFunctionType.Copy

P = 128
LANES = 4
QUADRANTS = 4
PER_COLUMN = 16
Q = 128
H = 2 * Q
E = Q // 2
TILES = T // Q
RUN = 4
LAST = LANES - 1
WIDE = 4 * C


def tile_attend_gvq_pl_r_x_kernel(
    tc, zT, cb, cb2, w_words, w_scales, offs, offs2, out_0, out_1, out_2
):
    nc = tc.nc
    with ExitStack() as ctx:
        keep = ctx.enter_context(tc.tile_pool(name="keep", bufs=1))
        psum = ctx.enter_context(tc.psum_pool(name="psum", bufs=1))

        def sbuf(name, shape, dtype, tag=None):
            return keep.tile(shape, dtype, name=name, tag=tag or name, align_bytes=64)

        code = keep.tile([P, T // PER_COLUMN], U16, name="code")
        code2 = keep.tile([P, T // PER_COLUMN], U16, name="code2")
        book = [sbuf(f"book{j}", [P, WIDE if j < LAST else C], F32) for j in range(LANES)]
        book2 = [sbuf(f"book2_{j}", [P, 2 * C if 0 < j < LAST else C], F32) for j in range(LANES)]
        z_early = sbuf("z_early", [P, LANES, H], F32)
        z = [z_early[:, :, i * Q : (i + 1) * Q] if i < 2 else sbuf(f"z{i}", [P, LANES, Q], F32) for i in range(TILES)]
        w_raw = sbuf("w_raw", [P, 2 * D], U8)
        w_plane_raw = sbuf("w_plane_raw", [P, D], U8)

        z_rows = zT.rearrange("(p j) t -> p j t", j=LANES)
        cb_rows = cb.rearrange("(p j) c -> p j c", j=LANES)
        cb2_rows = cb2.rearrange("(p j) c -> p j c", j=LANES)
        out_rows = out_0.rearrange("(p j) t -> p j t", j=LANES)
        out_words = out_1[0].rearrange("p t l -> p (t l)").bitcast(I32)
        out_scales = out_2[0].bitcast(I32)

        nc.vector.memset(w_plane_raw[:].bitcast(I32), 0)

        warm = sbuf("warm", [P, 2], F32)
        nc.gpsimd.memset(warm[:, 0:1], 0.0)
        nc.scalar.activation(warm[:, 1:2], warm[:, 0:1], COPY)

        def load_scale_rows(q):
            nc.sync.dma_start(
                w_plane_raw[32 * q : 32 * q + 4, :].bitcast(I32), w_scales[0, 4 * q : 4 * q + 4, :].bitcast(I32)
            )

        def load_z(i):
            nc.sync.dma_start(z[i][:], z_rows[:, :, i * Q : (i + 1) * Q])

        for j in range(LANES):
            nc.sync.dma_start(book2[j][:, 0:C], cb2_rows[:, j, :])
            if j == 0:
                nc.sync.dma_start(code2[:], offs2)
                nc.sync.dma_start(code[:], offs)
            if j > 1:
                load_scale_rows(2 * j - 4)
            nc.sync.dma_start(book[j][:, 0:C], cb_rows[:, j, :])
            if j > 1:
                load_scale_rows(2 * j - 3)
        nc.sync.dma_start(w_raw[:].bitcast(I32), w_words[0].bitcast(I32))
        nc.sync.dma_start(z_early[:], z_rows[:, :, 0:H])
        for i in range(2, TILES):
            load_z(i)

        def entries(lst, t0, t1):
            return lst[:, t0 // PER_COLUMN : t1 // PER_COLUMN]

        def weave_views(run, dst, src):
            return dst.rearrange("p (c i) j -> p c j i", i=run), src.rearrange("p j (c i) -> p c j i", i=run)

        def quantise(codes, plane, src, fmt):
            nc.vector.quantize_mx(out=codes.bitcast(fmt), scales=plane, in_=src.rearrange("p t j -> p (t j)"))

        def deal_views(dst, src):
            return (
                dst.rearrange("p j (h m) -> p h j m", h=2),
                src.rearrange("p (h m j) -> p h j m", h=2, j=LANES),
            )

        first = [sbuf(f"first{j}", [P, T if j < LAST else H], F32) for j in range(LANES)]
        second = [sbuf(f"second{j}", [P, T if j < LAST else H], F32) for j in range(LANES)]
        both = sbuf("both", [P, LANES, T], F32)
        w_dealt = sbuf("w_dealt", [P, LANES, P], U16)
        plane_dealt = sbuf("plane_dealt", [P, LANES, P], U8)

        def add(engine, j, t0, t1):
            engine.tensor_tensor(both[:, j, t0:t1], first[j][:, t0:t1], second[j][:, t0:t1], ALU.add)

        def gather_scaled(dst, window, lst, t0, t1):
            nc.scalar.activation(dst, window[:].indirect(entries(lst, t0, t1)), COPY, scale=BETA)

        beta = sbuf("beta", [P, Q], F32)
        nc.gpsimd.memset(beta[:], BETA)
        nc.vector.tensor_tensor(second[0][:, 0:Q], book2[0][:].indirect(entries(code2, 0, Q)), beta[:], ALU.mult)
        for j in range(LAST):
            t0 = Q if j == 0 else 0
            gather_scaled(second[j][:, t0:T], book2[j], code2, t0, T)
            nc.vector.tensor_scalar(first[j][:], book[j][:].indirect(code[:]), BETA, 0.0, ALU.mult, ALU.add)
            add(nc.gpsimd if j < 2 else nc.vector, j, 0, T)

        def last_lane(t0, t1, place, place2):
            gather_scaled(place2, book2[LAST], code2, t0, t1)
            gather_scaled(place, book[LAST], code, t0, t1)
            nc.vector.tensor_tensor(both[:, LAST, t0:t1], place, place2, ALU.add)

        y_plane = sbuf("y_plane", [P, T], U8)
        y_codes = [sbuf(f"y_codes{h}", [P, H], U32) for h in range(2)]
        g_bf, acc, y, y_bf = {}, {}, {}, {}
        y_early = []
        final = TILES - 1

        def pieces(i):
            return (slice(0, E), slice(E, Q)) if i == final else (slice(0, Q),)

        def form(i):
            g_bf[i] = sbuf(f"g_bf{i}", [P, Q, LANES], BF16)
            own = both[:, :, i * Q : (i + 1) * Q]
            for cols in pieces(i):
                nc.vector.scalar_tensor_tensor(
                    g_bf[i][:, cols, :],
                    z[i][:, :, cols].rearrange("p j t -> p t j"),
                    BETA,
                    own[:, :, cols].rearrange("p j t -> p t j"),
                    ALU.mult,
                    ALU.subtract,
                )

        def banks(i):
            return ((0, 2), (2, LANES)) if i == final else ((0, LANES),)

        def multiply(i):
            g_codes = sbuf(f"g_codes{i}", [P, Q], U32)
            g_plane = sbuf(f"g_plane{i}", [P, Q], U8)
            for cols in pieces(i):
                quantise(g_codes[:, cols], g_plane[:, cols], g_bf[i][:, cols, :], E5M2X4)
            for j0, j1 in banks(i):
                acc[i, j0] = psum.tile([P, j1 - j0, Q], F32, name=f"acc{i}_{j0}")
                for j in range(j0, j1):
                    nc.tensor.matmul_mx(
                        out=acc[i, j0][:, j - j0, :],
                        lhsT=w_dealt[:, j, :].bitcast(U8).bitcast(E2M1X4),
                        lhsT_scale=plane_dealt[:, j, :],
                        rhs=g_codes[:].bitcast(E5M2X4),
                        rhs_scale=g_plane[:],
                        start=True,
                        stop=True,
                    )

        def copy_out(i):
            y[i] = sbuf(f"y{i}", [P, LANES, Q], F32)
            for j0, j1 in banks(i):
                for cols in pieces(i) if j0 > 0 else (slice(0, Q),):
                    nc.scalar.copy(y[i][:, j0:j1, cols], acc[i, j0][:, :, cols])
            nc.sync.dma_start(out_rows[:, :, i * Q : (i + 1) * Q], y[i][:])

        def weave_result(i):
            if i == 0:
                y_early.append(sbuf("y_bf_early", [P, H, LANES], BF16, "z3"))
            if i < 2:
                y_bf[i] = y_early[0][:, i * Q : (i + 1) * Q, :]
            else:
                y_bf[i] = sbuf(f"y_bf{i}", [P, Q, LANES], BF16)
            for cols in pieces(i):
                nc.vector.tensor_copy(*weave_views(RUN, y_bf[i][:, cols, :], y[i][:, :, cols]))

        def quantise_result(i):
            h, half = divmod(i, 2)
            codes, plane = y_codes[h][:, half * Q : (half + 1) * Q], y_plane[:, i * Q : (i + 1) * Q]
            for cols in pieces(i):
                quantise(codes[:, cols], plane[:, cols], y_bf[i][:, cols, :], E4M3X4)
            if half == 1:
                nc.sync.dma_start(out_words[:, h * H : (h + 1) * H], y_codes[h][:].bitcast(I32))

        last_lane(0, H, first[LAST][:], second[LAST][:])
        nc.vector.tensor_copy(*deal_views(plane_dealt[:], w_plane_raw[:]))
        nc.scalar.copy(*deal_views(w_dealt[:], w_raw[:].bitcast(U16)))
        late = sbuf("late", [P, 2, H], F32, "w_raw")
        form(0)
        form(1)
        multiply(0)
        last_lane(H, H + Q, late[:, 0, 0:Q], late[:, 1, 0:Q])
        multiply(1)
        form(2)
        last_lane(H + Q, T, late[:, 0, Q:H], late[:, 1, Q:H])
        multiply(2)
        form(3)
        multiply(3)
        for i in range(TILES):
            copy_out(i)
            weave_result(i)
            quantise_result(i)
        for q in range(QUADRANTS):
            queue = nc.scalar if q % 2 == 0 else nc.sync
            queue.dma_start(out_scales[4 * q : 4 * q + 4, :], y_plane[32 * q : 32 * q + 4, :].bitcast(I32))
